import numpy as np, ml_dtypes
CORES = [36,164,52,180,100,228,116,244]
N = 8
BF = ml_dtypes.bfloat16
def gentries(a):
    return np.ascontiguousarray(a.reshape(8, 16, -1).transpose(0, 2, 1)).reshape(8, -1)
def gtable(e):
    e = np.asarray(e); return np.ascontiguousarray(e.reshape(8, -1, 16).transpose(0, 2, 1)).reshape(128, -1).astype(np.int32)
P, S, F, SW = 256, 5, 3, 3
V, RO = S * P, S - F
def node(rng, shape):
    return rng.integers(0, 2, shape) * V + rng.integers(0, F * P, shape)
def parts(rng):
    r = rng.integers(-1024, 1025, (N, 8, 16, F, P)); o = rng.integers(-256, 257, (N, 8, 16, S, P)); v = 0.5 + rng.random((N, 8, 16, S, P))
    m = rng.integers(0, 3, (N, 8, 16, 2 * (S - 1))); a = node(rng, (N, 8, F * P))
    return r, o, v, m, a
def lonely(rng, a):
    for q in range(N):
        for g in range(8):
            p = rng.permutation(P)[:7]
            for s in range(F):
                a[q, g, s * P + p[0]] = s * P + p[0]; a[q, g, s * P + p[1]] = s * P + p[2]; a[q, g, s * P + p[2]] = s * P + p[1]
                a[q, g, s * P + p[3]] = s * P + (p[4] if s else p[3]); a[q, g, s * P + p[4]] = s * P + p[3]
                a[q, g, s * P + p[5]] = s * P + (p[5] if s else p[6])
            a[q, g, p[6]] = p[5]
    return a
def pack(r, o, v, m, a):
    return {"r0": np.ascontiguousarray(r.reshape(N, 128, F * P)).astype(np.int32), "oc": o.reshape(N, 128, V).astype(np.float32).astype(BF), "stake": v.reshape(N, 128, V).astype(np.float32).astype(BF),
            "mu": m.reshape(N, 128, 2 * (S - 1)).astype(np.float32).astype(BF), "opp": np.stack([gtable(b) for b in a])}
def setup_inputs(rng):
    r, o, v, m, a = parts(rng)
    return pack(r, o, v, m, lonely(rng, a))
def setup_inputs_spread(rng):
    r, o, v, m, a = parts(rng)
    r = (np.exp2(4 + 6 * rng.random((N, 8, 1, F, P))) * (2 * rng.random(r.shape) - 1)).astype(np.int64)
    o = (np.exp2(8 * rng.random((N, 8, 1, S, P))) * (2 * rng.random(o.shape) - 1)).astype(np.int64)
    v = v * np.exp2(rng.integers(-1, 2, (N, 8, 1, S, P))); m = (3 * rng.random(m.shape) ** 2).astype(np.int64)
    a = rng.integers(0, 2, a.shape) * V + np.minimum((F * P * rng.random(a.shape) ** 2).astype(np.int64), F * P - 1)
    return pack(r, o, v, m, lonely(rng, a))
def setup_inputs_ends(rng):
    r, o, v, m, a = parts(rng); lo, hi = 0, V + F * P - 1
    r = np.where(rng.random(r.shape) < 0.5, -1024, 1024); o = np.where(rng.random(o.shape) < 0.5, -256, 256)
    v = np.where(rng.random(v.shape) < 0.5, 0.25, 4.0); m = 2 * rng.integers(0, 2, m.shape)
    a = np.where(rng.random(a.shape) < 0.7, np.where(rng.random(a.shape) < 0.5, lo, hi), a)
    b = np.where(rng.random((N, 8, P)) < 0.5, -1, 1); b[:, :, 0] = 1; b[:, :, P - 1] = -1
    for g in (0, 3, 5, 7):
        r[:, g] = 1024 * b[:, g, None, None, :]; o[:, g] = -256 * b[:, g, None, None, :]
        m[:, g, ::2] = 2; m[:, g, 15] = 2
        a[:, g] = np.where(rng.random((N, F * P)) < 0.8, np.tile(np.where(b[:, g] > 0, hi, lo), (1, F)), a[:, g])
    return pack(r, o, v, m, a)
def setup_inputs_corners(rng):
    r, o, v, m, a = parts(rng); own = np.arange(F * P)
    o = np.where(rng.random((N, 8, 1, S, P)) < 0.6, 256 * rng.integers(-1, 2, (N, 8, 1, S, P)), o)
    r[:, ::2] = rng.choice(np.array([-1024, -1, 0, 1, 1024]), (N, 4, 16, F, P))
    for i in range(16): m[:, 1::2, i] = i % 3
    far = np.array([0, F * P - 1, V, V + F * P - 1])
    for q in range(N):
        for g in range(8):
            k = (g + q) & 7
            if k == 0: a[q, g] = own
            if k == 1: a[q, g] = own ^ 1
            if k == 2: a[q, g] = (own + 1) % (F * P)
            if k == 3: a[q, g] = V + own
            if k == 4: a[q, g] = rng.choice(far, F * P)
            if k == 5: a[q, g, :P] = own[:P]
            if k == 6: a[q, g, :(F - 1) * P] = own[:(F - 1) * P]
            if k == 7:
                t = rng.integers(0, 5, F * P)
                a[q, g] = np.where(t == 0, own, np.where(t == 1, own ^ 1, np.where(t == 2, V + own, np.where(t == 3, rng.choice(far, F * P), a[q, g]))))
    x = int(rng.integers(0, N)); w = (x - 1) % N; mine = own.reshape(F, P)
    b = 2 * (rng.permutation(P) & 1) - 1; climb = rng.permutation(P) < P // 2
    odd = 2 * rng.permutation(P // 2)[:4] + 1; evn = 2 * rng.permutation(P // 2)[:8]; t = np.array([1, -1])
    d1, d2, low, mid, up, led = odd[:2], odd[2:], evn[:2], evn[2:4], evn[4:6], evn[6:]
    for z in (d1, d2, up, led): b[z] = t
    for z in (low, mid): b[z] = -t
    lead = np.where(climb & (np.arange(F)[:, None] > 0), -b, b); to = np.where(climb, np.arange(P), mine)
    for z in (low, mid, up): lead[:, z] = -t
    lead[:, led] = t
    to[:, up] = led; to[:, led] = mine[:, led]; to[:, mid] = d1
    to[:, low] = d2; to[0, low] = mid; to[F - 1, low] = mine[F - 1, low]
    for z in (d1, d2): to[:, z] = z; to[F - 1, z] = mine[F - 1, low]
    inner = (np.arange(F) > 0) & (np.arange(F) < F - 1)
    run = np.where(inner, -1020, 1024)[None, :, None] - 3 * (np.arange(16) & 1)[:, None, None]
    to = to.reshape(-1)
    for q in (x, w):
        r[q] = lead * (1024 - rng.integers(0, 4, r[q].shape)); o[q] = 256 * b; m[q] = 2
        r[q][..., d1] = t * run; r[q][..., d2] = t * (run - 1)
        a[q] = to if q == x else V + to
    return pack(r, o, v, m, a)
def setup_inputs_crowd(rng):
    r, o, v, m, a = parts(rng); two = rng.permutation(P)[:2]; x, y = int(two[0]), int(two[1])
    for q in range(N):
        for g in range(7):
            w = int(rng.integers(0, F * P)); one = int(rng.integers(0, F * P))
            if g == 6: w = F * P - 1
            if g in (0, 1, 6): a[q, g] = w
            if g == 2: a[q, g] = w; a[q, g, one] = V + one
            if g == 3: a[q, g] = V + w
            if g == 4: a[q, g] = V + w; a[q, g, one] = one
        a[q, 5] = np.where(rng.random(F * P) < 0.5, x, V + y); a[q, 5, x] = x
        r[q, 5, :, F - 1] = rng.integers(-50, 51, (16, P)); r[q, 5, :, 0, x] = 900; r[q, 5, :, 0, y] = 100
        if q % 2: r[q, 5, 3, 0, y] = 1020
    return pack(r, o, v, m, a)
def setup_inputs_ties(rng):
    r, o, v, m, a = parts(rng)
    b = (rng.integers(500, 1001, 16) * (2 * rng.integers(0, 2, 16) - 1))[None, None, :, None, None]
    k = rng.choice(np.array([0, 7, 8, 9, 10, 16]), (N, 8, 1, F, P)); place = np.argsort(np.argsort(rng.random(r.shape), axis=2), axis=2)
    dist = np.where(place < k, 4, 5 + rng.integers(0, 2, (N, 8, 1, F, P)))
    r = b + dist * (2 * rng.integers(0, 2, r.shape) - 1); r[:, :, :, F - 1] = b[:, :, :, 0]
    o = rng.integers(-1, 2, o.shape); m[:, :4] = 0
    a = rng.integers(0, 2, a.shape) * V + rng.integers(0, (F - 1) * P, a.shape)
    return pack(r, o, v, m, a)
def check_ranges(d):
    bad = []
    for k, lo, hi in (("r0", -1024, 1024), ("oc", -256, 256), ("mu", 0, 2), ("opp", 0, V + F * P - 1), ("stake", 0.25, 4)):
        w = np.asarray(d[k]).astype(np.float64)
        if not (np.min(w) >= lo and np.max(w) <= hi): bad.append("range of " + k)
        if k in ("oc", "mu") and np.any(w != np.floor(w)): bad.append("whole numbers of " + k)
    w = np.asarray(d["opp"]).astype(np.int64)
    if np.any((w >= F * P) & (w < V)): bad.append("opp names an empty slot")
    return bad
def both(R):
    w = R.reshape(N, 8, 16, V)
    return np.concatenate([w, np.roll(w, -1, axis=0)], axis=3)
def met(R, a):
    return np.take_along_axis(both(R), a[:, :, None, :], 3).reshape(N, 8, 16, -1, P)
def reference(r0, oc, stake, mu, opp):
    R = np.zeros((N, 8, 16, S, P), np.int64); R[:, :, :, :F] = r0.astype(np.int64).reshape(N, 8, 16, F, P)
    o = oc.astype(np.float64).reshape(N, 8, 16, S, P); v = stake.astype(np.float64).reshape(N, 8, 16, S, P)
    m = mu.astype(np.float64).reshape(N, 8, 16, 2 * (S - 1)); al, ga = m[..., :S - 1], m[..., S - 1:]
    L = np.zeros((N, 8, V), np.int64); L[:, :, :F * P] = np.stack([gentries(b) for b in opp])
    for rnd in range(RO):
        n = F + rnd
        a = L[:, :, :n * P].copy(); home = a < V
        c = np.where(home, np.take_along_axis(L, np.where(home, a, 0), 2), a)
        oneself = ((c < V) & ((c & (P - 1)) == np.tile(np.arange(P), n))).reshape(N, 8, n, P)
        me = R[:, :, :, n - 1].copy()
        dist = np.abs(met(R, c) - me[:, :, :, None, :])
        best = np.full((N, 8, 16, P), 2 ** 17, np.int64); pick = a[:, :, :P].copy(); c = c.reshape(N, 8, n, P)
        for k in range(n):
            nearer = np.add.reduce((dist[:, :, :, k] < best).astype(np.int64), axis=2)
            win = (nearer >= 9) & ~oneself[:, :, k]
            best = np.where(win[:, :, None, :], dist[:, :, :, k], best); pick = np.where(win, c[:, :, k], pick)
        L[:, :, n * P:(n + 1) * P] = np.where(pick >= V, V, 0) + (n - 1) * P + (pick & (P - 1))
        R[:, :, :, n] = (me + np.roll(me, -1, axis=1)) >> 1
        n = n + 1
        for sweep in range(SW):
            e = o[:, :, :, :n] - np.clip(R[:, :, :, :n] - met(R, L[:, :, :n * P]), -256, 256)
            d = e.copy()
            for s in range(1, n): d[:, :, :, s] += 0.5 * al[..., s - 1, None] * d[:, :, :, s - 1]
            x = np.floor(d)
            for s in range(n - 2, -1, -1): x[:, :, :, s] += 0.5 * ga[..., s, None] * x[:, :, :, s + 1]
            R[:, :, :, :n] += np.floor(0.0625 * x).astype(np.int64)
    z = (R - met(R, L)) * 2.0 ** -8
    y = np.add.reduce(v * (0.5 + 0.5 * np.tanh(0.5 * z)), axis=3)
    return {"y": y.reshape(N, 128, P).astype(np.float32), "yr": R.reshape(N, 128, V).astype(np.float32), "yo": np.stack([gtable(b) for b in L[:, :, F * P:]]).astype(np.float32)}

def check_inputs(d):
    bad = list(check_ranges(d))
    if not bad:
        for name, y in reference(**d).items():
            for q in range(N):
                v = np.abs(np.asarray(y[q], np.float64)); s = np.sqrt(np.mean(v * v))
                if v.max() > 11 * s or s < 2.0 ** 0: bad.append('%s of rank %d is uneven or too small' % (name, q))
    return bad

@@ -1,0 +1,808 @@
+from concourse.mybir import AluOpType as A, ActivationFunctionType as F
+
+NC, CP = 4, 64
+MAG = float(3 * 2 ** 18)
+MAG1 = float(3 * 2 ** 22)
+KOFF = 1535.5
+ETA = 2.0 ** -22
+BIGV = 131072.0
+SENDS = [[0], [1], [2], [3]]
+VIA = [False, False, False, False]
+VIA0 = [False, False]
+FLOOR = "PHHP"
+GATHER_A, GATHER_A0, GATHER_AF = [1, 2, 3], [0, 1, 2, 3], [1]
+SPLIT, SPLIT0 = [0], [0, 1, 2, 3]
+SUM_V = [3]
+CYC, PCYC, RLAT, RATE, SYNC = 0.001, 0.0006, 2.2, 80e3, 0.06
+
+SCRATCH = {
+    "r0i": ("sbuf", [128, 768], "int32"), "oppi": ("sbuf", [128, 48], "int32"), "mub": ("sbuf", [128, 8], "bfloat16"),
+    "ocb": ("sbuf", [128, 1280], "bfloat16"), "stb": ("sbuf", [128, 1280], "bfloat16"), "stc": ("sbuf", [128, 1280], "bfloat16"),
+    "r16": ("sbuf", [128, 768], "float16"), "l0": ("sbuf", [128, 768], "float16"),
+    "W": ("sbuf", [128, 2056], "float32"), "H4": ("sbuf", [128, 256], "float32"), "ME": ("sbuf", [128, 256], "float32"),
+    "tb": ("sbuf", [128, 128], "bfloat16"), "io2": ("sbuf", [128, 144], "bfloat16"), "kcol": ("sbuf", [128, 4], "int32"),
+    "zs0": ("sbuf", [128, 48], "int32"), "zs": ("sbuf", [128, 48], "int32"), "k15": ("sbuf", [128, 4], "int32"),
+    "kf": ("sbuf", [128, 8], "float32"), "PL": ("sbuf", [128, 4], "uint16"),
+    "TM": ("sbuf", [128, 2048], "bfloat16"), "BM": ("sbuf", [128, 144], "bfloat16"), "I1": ("sbuf", [128, 144], "bfloat16"),
+    "I2": ("sbuf", [128, 128], "bfloat16"), "I32": ("sbuf", [128, 128], "float32"), "WD": ("sbuf", [128, 11 * 128], "bfloat16"),
+    "wc": ("sbuf", [128, 32], "float32"), "PAT3": ("sbuf", [128, 192], "float32"), "PAT4": ("sbuf", [128, 256], "float32"),
+    "CH": ("sbuf", [128, 7 * 256], "bfloat16"), "CL": ("sbuf", [128, 7 * 256], "float16"),
+    "o16": ("sbuf", [128, 48], "float16"), "aw": ("sbuf", [128, 48], "bfloat16"),
+    "LW": ("sbuf", [128, 768], "float32"), "REP": ("sbuf", [128, 768], "float16"),
+    "u1": ("sbuf", [128, 64], "uint16"), "OFF": ("sbuf", [128, 80], "uint16"), "CO": ("sbuf", [128, 64], "uint16"),
+    "RH": ("sbuf", [128, 1024], "float32"), "MP": ("sbuf", [128, 640], "bfloat16"),
+    "OP": ("sbuf", [128, 64], "int32"), "OQ": ("sbuf", [128, 64], "int32"),
+    "sa": ("sbuf", [128, 48 * 24], "int32"), "sf": ("sbuf", [128, 48 * 18], "float32"), "Z": ("sbuf", [128, 96], "int32"),
+    "TK": ("sbuf", [128, 1280], "float32"), "DS": ("sbuf", [128, 1280], "float32"), "LT": ("sbuf", [128, 1536], "bfloat16"),
+    "TT": ("sbuf", [128, 1280], "bfloat16"), "V": ("sbuf", [128, 1280], "float32"), "X": ("sbuf", [128, 1280], "float32"),
+    "ZC": ("sbuf", [128, 256], "float32"), "DF": ("sbuf", [128, 256], "float16"),
+    "NT": ("sbuf", [128, 256], "float32"), "S3": ("sbuf", [128, 1024], "float16"), "L3": ("sbuf", [128, 1024], "float16"),
+    "YR": ("sbuf", [128, 1280], "float32"), "YO": ("sbuf", [128, 32], "float32"), "Y": ("sbuf", [128, 256], "float32"),
+    "ph0": ("psum", [128, 512], "float32"), "ph1": ("psum", [128, 512], "float32"),
+    "pa0": ("psum", [128, 512], "float32"), "pa1": ("psum", [128, 512], "float32"),
+    "d0": ("psum", [128, 512], "float32"), "d1": ("psum", [128, 512], "float32"),
+    "d2": ("psum", [128, 512], "float32"), "d3": ("psum", [128, 512], "float32"),
+}
+for _k in range(6):
+    SCRATCH["dl%d" % _k] = ("sbuf", [128, 256 * (3 + _k // 3)], "float16")
+    SCRATCH["ld%d" % _k] = ("sbuf", [128, 256 * (3 + _k // 3)], "float16")
+SEMAPHORES = ["sv", "sa", "sp", "sg", "ls"] + ["dm%d" % i for i in range(12)] + ["ar%d" % i for i in range(4 + 6 * NC)]
+
+
+def _mask(engines):
+    m = 0
+    for e in engines:
+        m |= 1 << e
+    return m
+
+
+def _helper(core, T, topo):
+    return [c for c in topo.cores_of(core) if topo.die(c) != topo.die(core) and T.rank_of(c) is None][0]
+
+
+def _messages():
+    ms = [("r16", "l0", 0, 384, VIA0[0]), ("r16", "l0", 384, 768, VIA0[1])]
+    for k in range(6):
+        f = 3 + k // 3
+        for i, cs in enumerate(SENDS):
+            ms.append(("dl%d" % k, "ld%d" % k, CP * f * cs[0], CP * f * (cs[-1] + 1), VIA[i]))
+        if k == 1:
+            ms.append(("S3", "L3", 0, 768, False))
+        if k == 2:
+            ms.append(("S3", "L3", 768, 1024, False))
+    return ms
+
+
+def _helper_program(g, core, owner, T, topo):
+    n = len(T.cores)
+    prev = T.cores[(T.rank_of(owner) - 1) % n]
+    off = topo.engines(owner, prev)
+    near = [e for e in topo.engines(owner, core) if e not in off]
+    eng = topo.engines(core, prev)
+    rid, pid = topo.addr(prev, core)
+    sent = 0
+    for i, (src, dst, a, b, via) in enumerate(_messages()):
+        if via:
+            g.wait_ge(T.sem["ar%d" % i], len(near))
+            g.remote_dma(T[dst][:, a:b], T[dst][:, a:b], T.sem["ar%d" % i], T.sem.ls, pid, rid, _mask(eng))
+            sent += len(eng)
+    if sent:
+        g.wait_ge(T.sem.ls, sent)
+
+
+KEPT = {}
+PASSES, SHAKES, SEED, SHAKE, FIRST = 6, 900, 1, 0.7, 3.5
+
+
+def _order(ops, marks):
+    n = len(ops)
+    pred = [sorted(o["deps"]) for o in ops]
+    succ = [[] for o in ops]
+    for i in range(n):
+        for j in pred[i]:
+            succ[j].append(i)
+
+    def lag(a, b):
+        if ops[a]["q"] == "g" and ops[b]["q"] == "g":
+            return 0.0
+        return ops[a]["lat"] + (0.0 if ops[a]["q"] == "p" and ops[b]["q"] == "p" else SYNC)
+
+    def place(seq, back):
+        busy, end = {}, [0.0] * n
+        for i in seq:
+            o = ops[i]
+            if back:
+                t = max([end[j] + lag(i, j) for j in succ[i]] + [o["lat"]])
+            else:
+                t = max([end[j] + lag(j, i) for j in pred[i]] + [0.0])
+            if o["q"] != "r":
+                iv = busy.setdefault(o["q"], [])
+                lo, hi = 0, len(iv)
+                while lo < hi:
+                    m = (lo + hi) // 2
+                    if iv[m][1] <= t:
+                        lo = m + 1
+                    else:
+                        hi = m
+                while lo < len(iv) and iv[lo][0] < t + o["cost"] - 1e-9:
+                    t = max(t, iv[lo][1])
+                    lo += 1
+                iv.insert(lo, (t, t + o["cost"]))
+            end[i] = t + o["cost"]
+        return end
+
+    way = [0.0] * n
+    for i in range(n - 1, -1, -1):
+        way[i] = ops[i]["cost"] + max([way[j] + lag(i, j) for j in succ[i]] + [ops[i]["lat"]])
+    best, seed = None, SEED
+    for turn in range(PASSES):
+        end = place(sorted(range(n), key=lambda i: (-way[i], i)), False)
+        span = max(end[i] + ops[i]["lat"] for i in range(n))
+        if best is None or span < best[0]:
+            best = (span, sorted(range(n), key=lambda i: (end[i] - ops[i]["cost"], i)), list(way))
+        way = place(sorted(range(n), key=lambda i: (-end[i], -i)), True)
+
+
+    def run(w):
+        w = list(w)
+        for i in range(n - 1, -1, -1):
+            for j in succ[i]:
+                if w[j] + 1e-6 > w[i]:
+                    w[i] = w[j] + 1e-6
+        end = place(sorted(range(n), key=lambda i: (-w[i], i)), False)
+        t = [0.0] + [end[i] for i in marks] + [max(end[i] + ops[i]["lat"] for i in range(n))]
+        return w, end, t
+
+    way, end, t = run(best[2])
+    for turn in range(SHAKES):
+        part = [sum(1 for m in t[1:-1] if m < end[i]) for i in range(n)]
+        new = list(way)
+        for i in range(n):
+            seed = (seed * 1103515245 + 12345) % 2147483648
+            if seed % 1024 < 200:
+                new[i] += SHAKE * (seed / 1073741824 - 1.0)
+        new, e2, t2 = run(new)
+        back = place(sorted(range(n), key=lambda i: (-e2[i], -i)), True)
+        shift = max(way) - max(back)
+        new, e2, t2 = run([b + shift for b in back])
+        if t2[-1] < t[-1]:
+            way, end, t = new, e2, t2
+            continue
+        good = [t2[p + 1] - t2[p] < t[p + 1] - t[p] - 1e-9 for p in range(len(t) - 1)]
+        if any(good):
+            w3, e3, t3 = run([new[i] if good[part[i]] else way[i] for i in range(n)])
+            if t3[-1] < t[-1]:
+                way, end, t = w3, e3, t3
+    KEPT["span"] = t[-1]
+    return sorted(range(n), key=lambda i: (end[i] - ops[i]["cost"], i))
+
+
+def rank_program(g, core, T, topo):
+    rank = T.rank_of(core)
+    if rank is None:
+        for c in T.cores:
+            if _helper(c, T, topo) == core:
+                _helper_program(g, core, c, T, topo)
+        return
+    n = len(T.cores)
+    prev, nxt = T.cores[(rank - 1) % n], T.cores[(rank + 1) % n]
+    helper = _helper(core, T, topo)
+    far = topo.engines(core, prev)
+    near = [e for e in topo.engines(core, helper) if e not in far]
+    msgs = _messages()
+
+    ops, lastw, readers, banks = [], {}, {}, {}
+    ndma, nsent, sent, marks = [0], [0], {}, []
+
+    def add(q, fn, r=(), w=(), x=(), tok=None, cost=0.1, lat=0.0, after=()):
+        i = len(ops)
+        deps = set(after)
+        for k in r:
+            if k in lastw:
+                deps.add(lastw[k])
+        for k in w:
+            if k in lastw:
+                deps.add(lastw[k])
+            deps.update(readers.get(k, ()))
+        for k in x:
+            deps.update(banks.setdefault(k, {}).values())
+        for k in r:
+            readers.setdefault(k, []).append(i)
+        for k in w:
+            lastw[k] = i
+            readers[k] = []
+        for k in x:
+            banks[k][q] = i
+        ops.append({"q": q, "fn": fn, "deps": deps, "tok": tok, "cost": cost, "lat": lat})
+        return i
+
+    def cy(out, k=1.0):
+        return 0.05 + max(64, out.shape[1] * k) * CYC
+
+    def ts(out, in0, s1, op0, s2=None, op1=None, r=(), w=(), x=(), k=1.0):
+        if op1 is None:
+            add("v", lambda: g.vector.tensor_scalar(out, in0, s1, None, op0), r, w, x, cost=cy(out, k))
+        else:
+            add("v", lambda: g.vector.tensor_scalar(out, in0, s1, s2, op0, op1), r, w, x, cost=cy(out, k))
+
+    def tt(out, in0, in1, op, r=(), w=(), x=(), k=None):
+        add("v", lambda: g.vector.tensor_tensor(out, in0, in1, op), r, w, x, cost=cy(out, k or (1.0 if x else 2.0)))
+
+    def cp(out, in_, r=(), w=(), x=(), k=1.0):
+        add("v", lambda: g.vector.tensor_copy(out, in_), r, w, x, cost=cy(out, k))
+
+    def ms(out, val, w):
+        add("v", lambda: g.vector.memset(out, val), (), w, cost=cy(out))
+
+    def act(out, in_, func=F.Identity, bias=0.0, scale=1.0, r=(), w=(), x=(), more=0.0):
+        add("a", lambda: g.scalar.activation(out, in_, func, bias=bias, scale=scale), r, w, x, cost=cy(out) + 0.03 + more)
+
+    def mm(out, lhs, rhs, start, stop, r=(), x=(), k=1.0):
+        add("p", lambda: g.tensor.matmul(out, lhs, rhs, start, stop), r, (), x, cost=max(64, out.shape[1]) * k * PCYC)
+
+    def dma(q, out, in_, r=(), w=()):
+        s = "dm%d" % ndma[0]
+        ndma[0] += 1
+        eng = g.sync if q == "s" else g.scalar
+        add(q, lambda: eng.dma_start(out, in_), r, w, (), (s, 16, True), cost=0.1, lat=1.9 + out.shape[1] / 700)
+
+    def iota(out, pat, cm, key, small):
+        if small:
+            add("g", lambda: g.iota(out, pat, 0, cm, allow_small_or_imprecise_dtypes=True), (), [key], cost=0.13 + 2 * out.shape[1] * CYC)
+        else:
+            add("g", lambda: g.iota(out, pat, 0, cm), (), [key], cost=0.13 + 2 * out.shape[1] * CYC)
+
+    def send(i, keys):
+        src, dst, a, b, via = msgs[i]
+        to, eng = (helper, near) if via else (prev, far)
+        rid, pid = topo.addr(to, core)
+        nsent[0] += len(eng)
+        sent[i] = add("g", lambda: g.remote_dma(T[dst][:, a:b], T[src][:, a:b], T.sem["ar%d" % i], T.sem.ls, pid, rid, _mask(eng)),
+                      keys, (), (), ("ls", 0, False), cost=FIRST if i == 0 else 0.3 if via else max(0.3, (b - a) * 256 / RATE),
+                      lat=2 * RLAT + (b - a) * 512 / RATE if via else RLAT, after=[sent[i - 1]] if i else [])
+
+    def arrive(i, keys):
+        sender = _helper(nxt, T, topo) if msgs[i][4] else nxt
+        add("r", None, (), keys, (), ("ar%d" % i, len(topo.engines(sender, core)), False), cost=0.0, after=[sent[i]])
+
+    W, win = T.W, T.W[:, 0:2056]
+    HK = ["WH%d" % c for c in range(NC)]
+    AK = ["WA%d" % c for c in range(NC)]
+    MEK = ["ME%d" % c for c in range(NC)]
+    WIN = HK + AK + ["WB"]
+    I1 = T.I1[:, 0:128]
+
+    def hb(c):
+        return "ph%d" % (c // 2)
+
+    def ab(c):
+        return "pa%d" % (c // 2)
+
+    def reg(bank, c, s, m=1):
+        return T[bank][:, (c % 2) * 256 + 64 * s:(c % 2) * 256 + 64 * (s + m)]
+
+    def si(j, m=48):
+        return T.sa[:, 48 * j:48 * j + m]
+
+    def sfl(j, m=48, o=0):
+        return T.sf[:, 48 * j + o:48 * j + o + m]
+
+    def wd(s, t):
+        j = 10 if s == t else [0, 4, 7, 9][s - t - 1] + t
+        return T.WD[:, 128 * j:128 * j + 128], "WD%d" % j
+
+    def lookup_list(src, rk, col, ck, m, c0, away, ak):
+        ts(si(0, m), src, 15, A.bitwise_and, r=[rk], w=["sa0"])
+        ts(si(1, m), src, 4, A.logical_shift_right, r=[rk], w=["sa1"])
+        ts(si(2, m), si(0, m), 48.0, A.mult, r=["sa0"], w=["sa2"])
+        ts(sfl(0, m), src, 1024.0, A.is_lt, 0.0625, A.mult, [rk], ["sf0"])
+        tt(si(3, m), si(2, m), si(1, m), A.add, ["sa2", "sa1"], ["sa3"])
+        ts(T.u1[:, c0:c0 + m], si(3, m), 767.0, A.min, r=["sa3"], w=["u1"])
+        tt(sfl(2, m), away, col, A.mult, [ak, ck], ["sf2"])
+
+    def lookup_gather(m, c0, bank):
+        for j in range(m // 16):
+            cp(T.REP[:, 256 * j:256 * j + 256], T.LW[:, 0:768].indirect(T.u1[:, c0 + 16 * j:c0 + 16 * j + 16]),
+               ["LW0", "LW1", "u1"], ["REP%d" % j], k=1.5)
+        for r in range(16):
+            mm(T[bank][:, 0:m], T.BM[:, 15 - r:143 - r], T.REP[:, r:16 * m:16], r == 0, r == 15,
+               ["BM"] + ["REP%d" % j for j in range(m // 16)], [bank])
+
+    def lookup_finish(m, c0, bank):
+        tt(sfl(3, m), T[bank][:, 0:m], sfl(0, m), A.mult, ["sf0"], ["sf3"], [bank])
+        tt(si(4, m), sfl(3, m), sfl(2, m), A.add, ["sf3", "sf2"], ["sa4"])
+        ts(T.Z[:, c0:c0 + m], si(4, m), 0x73F, A.bitwise_and, r=["sa4"], w=["Z%d" % c0])
+        tt(sfl(4, m), T.Z[:, c0:c0 + m], T.zs[:, 0:m], A.is_equal, ["Z%d" % c0, "zs"], ["sf4"])
+        ts(sfl(5, m), sfl(4, m), 2048.0, A.mult, r=["sf4"], w=["sf5"])
+        tt(sfl(6, m), sfl(5, m), si(4, m), A.max, ["sf5", "sa4"], ["sf6"])
+        cp(T.CO[:, c0:c0 + m], sfl(6, m), ["sf6"], ["CO%d" % c0])
+
+    def const(j, s, bias, bank, tmp):
+        cs = slice(256 * j, 256 * j + 256)
+        for t in range(s + 1):
+            m, k = wd(s, t)
+            mm(T[bank][:, 0:256], m, T.ocb[:, 256 * t:256 * t + 256], t == 0, t == s, [k, "ocb"], [bank])
+        act(T.CH[:, cs], T[bank][:, 0:256], bias=bias, r=["wc"], w=["CH%d" % j], x=[bank])
+        act(T[tmp][:, 0:256], T[bank][:, 0:256], bias=bias, r=["wc"], x=[bank, tmp])
+        tt(T.CL[:, cs], T[tmp][:, 0:256], T.CH[:, cs], A.subtract, ["CH%d" % j], ["CL%d" % j], [tmp])
+
+    CV = {3: [0, 1, 2, 3], 4: [0, 1, 4, 5, 6]}
+    BK, B0 = KOFF - 15.0 / 512, -15.0 / 512
+
+    def dreg(c, f, s):
+        d = T["d%d" % c]
+        return d[:, 64 * f:64 * f + 64] if s == f else d[:, f - 1 - s:64 * f:f]
+
+    def preload(c, f):
+        for s in range(f + 1):
+            j = CV[f][s]
+            cs = slice(256 * j + 64 * c, 256 * j + 64 * c + 64)
+            mm(dreg(c, f, s), I1, T.CH[:, cs], s == 0, False, ["I1", "CH%d" % j], ["d%d" % c])
+            mm(dreg(c, f, s), I1, T.CL[:, cs], False, False, ["I1", "CL%d" % j], ["d%d" % c])
+
+    def gather(out, ok, c, f, part, scalar):
+        b = 320 * c
+        lo = 0 if part != "new" else f
+        hi = min(4, f if part == "old" else f + 1)
+        if lo < hi:
+            r = WIN + ["OFF"] + (["OFF3_%d" % c] if hi == 4 else [])
+            q, w = win.indirect(T.OFF[:, 16 * c + 4 * lo:16 * c + 4 * hi]), [ok + "%d_%d" % (c, s) for s in range(lo, hi)]
+            if c in scalar and part != "new":
+                qb = T.V[:, b + 64 * lo:b + 64 * hi]
+                act(qb, q, r=r, w=["V%d" % c], more=32 * (hi - lo) * CYC)
+                tt(out[:, b + 64 * lo:b + 64 * hi], qb, reg(hb(c), c, lo, hi - lo), A.subtract, ["V%d" % c], w, [hb(c)])
+            elif part == "new":
+                tt(out[:, b + 64 * lo:b + 64 * hi], win.indirect(T.OFF[:, 64 + 4 * c:68 + 4 * c]), T.S3[:, 64 * c:64 * c + 64],
+                   A.subtract, WIN + ["OFF4", "N3"], w, k=1.5)
+            else:
+                tt(out[:, b + 64 * lo:b + 64 * hi], q, T.RH[:, 256 * c + 64 * lo:256 * c + 64 * hi], A.subtract, r + ["RH%d" % c], w, k=1.5)
+        if f == 4 and part != "old":
+            tt(out[:, b + 256:b + 320], win.indirect(T.OFF[:, 64 + 4 * c:68 + 4 * c]), T.H4[:, 64 * c:64 * c + 64],
+               A.subtract, WIN + ["OFF4", "H4"], [ok + "%d_4" % c], k=1.5)
+
+    def new_rating(parts, keys, bank, out, ok):
+        lhs = [(I1, "I1"), (T.I1[:, 16:144], "I1"), (T.I2[:, :], "I2")]
+        jobs = [(m, k, p) for p in parts for m, k in lhs]
+        for i, (m, k, (o0, o1, rhs)) in enumerate(jobs):
+            mm(T[bank][:, o0:o1], m, rhs, i == 0, i == len(jobs) - 1, [k] + keys, [bank])
+        act(T.NT[:, :], T[bank][:, 0:256], bias=-0.25, scale=0.5, w=["NT"], x=[bank])
+        ts(out, T.NT[:, :], MAG1, A.add, -MAG1, A.add, ["NT"], [ok])
+
+    def away_copy(c, m, scalar):
+        o = W[:, 1024 + 256 * c:1024 + 256 * c + 64 * m]
+        if scalar:
+            act(o, reg(ab(c), c, 0, m), w=[AK[c]], x=[ab(c)])
+        else:
+            cp(o, reg(ab(c), c, 0, m), w=[AK[c]], x=[ab(c)])
+
+    dma("s", T.r0i[:, 0:384], T.r0[:, 0:384], w=["r0a"])
+    dma("a", T.r0i[:, 384:768], T.r0[:, 384:768], w=["r0b"])
+    dma("s", T.oppi[:, :], T.opp[:, :], w=["opp"])
+    dma("a", T.mub[:, :], T.mu[:, :], w=["mu"])
+    dma("s", T.ocb[:, :], T.oc[:, :], w=["ocb"])
+    dma("s", T.stb[:, :], T.stake[:, :], w=["stb"])
+    iota(T.tb[:, :], [[-16, 8], [0, 16]], 1, "tb", True)
+    iota(T.io2[:, :], [[1, 144]], -1, "io2", True)
+    iota(T.kcol[:, :], [[0, 4]], 1, "kcol", False)
+    iota(T.zs0[:, :], [[0, 3], [256, 4], [16, 4]], 0, "zs0", False)
+    act(W[:, 2048:2056], T.tb[:, 0:8], scale=0.0, bias=BIGV, r=["tb"], w=["WB"])
+    ms(T.OP[:, 48:64], 0, ["OPz"])
+    ms(T.PAT3[:, 0:192:3], ETA, ["PAT3_0"])
+    ms(T.PAT4[:, 0:256:4], ETA, ["PAT4_0"])
+    for c in range(NC):
+        act(W[:, 1024 + 256 * c + 192:1024 + 256 * c + 256], T.tb[:, 0:64], scale=0.0, r=["tb"], w=[AK[c]])
+    for r in range(16):
+        ts(T.TM[:, 128 * r:128 * r + 128], T.tb[:, :], float(r), A.is_equal, r=["tb"], w=["TM%d" % r], k=0.5)
+    act(T.MP[:, 0:320], T.TM[:, 0:320], scale=0.0, bias=MAG, r=["TM0", "TM1", "TM2"], w=["MP"])
+    act(T.MP[:, 320:640], T.TM[:, 0:320], scale=0.0, bias=-MAG, r=["TM0", "TM1", "TM2"], w=["MN"])
+    ts(T.I1[:, :], T.io2[:, :], 0.0, A.is_equal, r=["io2"], w=["I1"], k=0.5)
+    for h in range(2):
+        for s in range(3):
+            cp(T.r16[:, 384 * h + 128 * s:384 * h + 128 * s + 128], T.r0i[:, 256 * s + 128 * h:256 * s + 128 * h + 128],
+               ["r0a", "r0b"], ["r16_%d%d" % (h, s)])
+        send(h, ["r16_%d%d" % (h, s) for s in range(3)])
+    ts(T.aw[:, :], T.oppi[:, :], 1024.0, A.is_ge, r=["opp"], w=["aw"])
+    src, oo = T.oppi[:, :], T.OP[:, 0:48]
+    ts(si(12), src, 6, A.logical_shift_right, 3, A.bitwise_and, ["opp"], ["sa12"])
+    ts(si(13), src, 8, A.logical_shift_right, r=["opp"], w=["sa13"])
+    ts(si(14), src, 1024.0, A.is_ge, 704.0, A.mult, ["opp"], ["sa14"])
+    tt(si(15), si(12), si(13), A.subtract, ["sa12", "sa13"], ["sa15"])
+    tt(si(16), src, si(14), A.add, ["opp", "sa14"], ["sa16"])
+    ts(si(17), si(15), 192.0, A.mult, r=["sa15"], w=["sa17"])
+    tt(T.o16[:, :], si(17), si(16), A.add, ["sa16", "sa17"], ["o16"])
+    tt(oo, si(17), si(16), A.add, ["sa16", "sa17"], ["OP"])
+    for r in range(16):
+        b = "d%d" % (r // 8)
+        mm(T[b][:, 48 * (r % 8):48 * (r % 8) + 48], T.TM[:, 128 * r:128 * r + 128], T.o16[:, :], r % 8 == 0, r % 8 == 7,
+           ["TM%d" % r, "o16"], [b])
+        if r % 8 == 7:
+            act(T.LW[:, 384 * (r // 8):384 * (r // 8) + 384], T[b][:, 0:384], w=["LW%d" % (r // 8)], x=[b])
+    lookup_list(src, "opp", oo, "OP", 48, 0, T.aw[:, :], "aw")
+    ts(T.k15[:, 0:1], T.kcol[:, 0:1], 15, A.bitwise_and, r=["kcol"], w=["k15"])
+    ts(T.k15[:, 1:2], T.kcol[:, 0:1], 3, A.bitwise_and, r=["kcol"], w=["k3"])
+    ts(T.I2[:, :], T.io2[:, 16:144], 128.0, A.is_equal, r=["io2"], w=["I2"], k=0.5)
+    ts(T.kf[:, 0:1], T.k15[:, 0:1], -1.0, A.mult, 15.0, A.add, ["k15"], ["kf0"])
+    cp(T.kf[:, 1:2], T.k15[:, 0:1], ["k15"], ["kf1"])
+    ts(T.BM[:, :], T.io2[:, :], T.kf[:, 0:1], A.is_equal, r=["io2", "kf0"], w=["BM"], k=0.5)
+    ts(T.zs[:, :], T.zs0[:, :], T.kf[:, 1:2], A.add, r=["zs0", "kf1"], w=["zs"])
+    ts(T.kf[:, 2:3], T.k15[:, 1:2], -0.75, A.mult, T.kf[:, 1:2], A.add, ["k3", "kf1"], ["kf2"])
+    ts(T.kf[:, 4:8], T.zs0[:, 0:4], 0.0625, A.mult, T.kf[:, 2:3], A.add, ["zs0", "kf2"], ["kf4"])
+    ts(T.PL[:, :], T.kf[:, 4:8], 4.0, A.mult, r=["kf4"], w=["PL"])
+    cp(T.OQ[:, :], T.OP[:, 0:64].indirect(T.PL[:, :]), ["OP", "OPz", "PL"], ["OQ"], k=1.5)
+    cp(T.OFF[:, 0:64], T.OQ[:, :], ["OQ"], ["OFF"] + ["OFF3_%d" % c for c in range(NC)])
+    act(T.wc[:, 0:4], T.mub[:, 0:4], scale=1.0 / 32, r=["mu"], w=["w1"])
+    act(T.wc[:, 12:16], T.mub[:, 0:4], scale=0.5, r=["mu"], w=["wa"])
+    tt(T.wc[:, 4:7], T.wc[:, 0:3], T.wc[:, 13:16], A.mult, ["w1", "wa"], ["w2"])
+    tt(T.wc[:, 7:9], T.wc[:, 4:6], T.wc[:, 14:16], A.mult, ["w2", "wa"], ["w3"])
+    lookup_gather(48, 0, "d2")
+    for c in range(NC):
+        for s in range(3):
+            o = 384 * (c // 2) + 128 * s + 64 * (c % 2)
+            mm(reg(hb(c), c, s), I1, T.r16[:, o:o + 64], c % 2 == 0 and s == 0, False, ["I1", "r16_%d%d" % (c // 2, s)], [hb(c)])
+    new_rating([(128 * h, 128 * h + 128, T.r16[:, 384 * h + 256:384 * h + 384]) for h in range(2)], ["r16_02", "r16_12"],
+               "d3", T.S3[:, 0:256], "N3")
+
+    def diag(j):
+        k = "w1" if j < 4 else "w2" if j < 7 else "w3" if j < 9 else "w4"
+        act(T.WD[:, 128 * j:128 * j + 128], I1, scale=T.wc[:, j:j + 1], r=["I1", k], w=["WD%d" % j])
+
+    act(T.WD[:, 1280:1408], I1, scale=0.0625, r=["I1"], w=["WD10"])
+    for j in (0, 1, 2, 4, 5, 7):
+        diag(j)
+    act(T.wc[:, 16:20], T.mub[:, 4:8], scale=-KOFF / 2, bias=BK, r=["mu"], w=["wc"])
+    act(T.wc[:, 20:24], T.mub[:, 4:8], scale=0.5, bias=ETA, r=["mu"], w=["wce"])
+    act(T.wc[:, 24:28], T.mub[:, 4:8], scale=0.5, r=["mu"], w=["wch"])
+    act(T.wc[:, 28:32], T.mub[:, 4:8], scale=-MAG / 2, r=["mu"], w=["wcm"])
+    for c in range(NC):
+        mm(reg(hb(c), c, 3), I1, T.S3[:, 64 * c:64 * c + 64], False, c % 2 == 1, ["I1", "N3"], [hb(c)])
+    lookup_finish(48, 0, "d2")
+    for h in range(2):
+        act(W[:, 512 * h:512 * h + 512], T["ph%d" % h][:, :], w=HK[2 * h:2 * h + 2], x=["ph%d" % h])
+    for h in range(2):
+        mm(T.pa1[:, 128 * h:128 * h + 128], I1, T.r16[:, 384 * h + 256:384 * h + 384], h == 0, h == 1, ["I1", "r16_%d2" % h], ["pa1"])
+    act(T.ME[:, :], T.pa1[:, 0:256], w=MEK, x=["pa1"])
+    const(0, 0, T.wc[:, 16:17], "d0", "d1")
+    const(1, 1, T.wc[:, 17:18], "d0", "d1")
+    ts(T.Z[:, 64:80], T.OP[:, 0:16], 0x73F, A.bitwise_and, r=["OP"], w=["Z64"])
+    const(2, 2, BK, "d0", "d3")
+    const(3, 3, B0, "d1", "d3")
+    tt(sfl(7, 16), T.Z[:, 64:80], T.Z[:, 0:16], A.subtract, ["Z64", "Z0"], ["sf7"])
+    tt(sfl(8, 16), sfl(7, 16), sfl(4, 16), A.mult, ["sf7", "sf4"], ["sf8"])
+    tt(T.Z[:, 80:96], sfl(8, 16), T.Z[:, 0:16], A.add, ["sf8", "Z0"], ["Z80"])
+    tt(sfl(9, 16), T.Z[:, 16:32], T.Z[:, 80:96], A.subtract, ["Z80", "Z0"], ["sf9"])
+
+    def pattern(f):
+        for j in range(1, f):
+            s = f - 1 - j
+            act(T["PAT%d" % f][:, j:64 * f:f], T.io2[:, 0:64], bias=T.wc[:, 20 + s:21 + s], scale=0.0, r=["io2", "wce"], w=["PAT%d_%d" % (f, j)])
+
+    pattern(3)
+    for h in range(2):
+        arrive(h, ["l0_%d" % h])
+        for c in (2 * h, 2 * h + 1):
+            for s in range(3):
+                o = 384 * h + 128 * s + 64 * (c % 2)
+                mm(reg(ab(c), c, s), I1, T.l0[:, o:o + 64], c % 2 == 0 and s == 0, c % 2 == 1 and s == 2, ["I1", "l0_%d" % h], [ab(c)])
+        for c in (2 * h, 2 * h + 1):
+            away_copy(c, 3, h == 0)
+
+    def slot3_in():
+        arrive(2 + 2 * len(SENDS), ["L3a"])
+        arrive(3 + 3 * len(SENDS), ["L3b"])
+        for c in range(NC):
+            for h in range(4):
+                mm(reg(ab(c), c, 3), I1, T.L3[:, 256 * h + 64 * c:256 * h + 64 * c + 64], c % 2 == 0 and h == 0, c % 2 == 1 and h == 3,
+                   ["I1", "L3b" if h == 3 else "L3a"], [ab(c)])
+            if c % 2 == 1:
+                for q in (c - 1, c):
+                    act(W[:, 1024 + 256 * q + 192:1024 + 256 * q + 256], reg(ab(q), q, 3), w=[AK[q]], x=[ab(q)])
+
+    def part1(f):
+        pair = {(1, 0): 0, (2, 0): 1, (2, 1): 2, (3, 0): 3, (3, 1): 4, (3, 2): 5}
+
+        def gk(k):
+            ck = "CO48" if k == 3 else "CO0"
+            tk = T.TK[:, 256 * k:256 * k + 256]
+            tt(tk, win.indirect(T.CO[:, 16 * k:16 * k + 16]), T.ME[:, :], A.subtract, WIN + [ck] + MEK, ["TK%d" % k], k=1.5)
+            if k > 0:
+                act(T.DS[:, 256 * k:256 * k + 256], tk, F.Abs, r=["TK%d" % k], w=["DS%d" % k])
+            if k < f - 1:
+                act(T["d%d" % k][:, 0:256], tk, F.Abs, r=["TK%d" % k], x=["d%d" % k])
+
+        def lt(k, j):
+            i = pair[(k, j)]
+            tt(T.LT[:, 256 * i:256 * i + 256], T.DS[:, 256 * k:256 * k + 256], T["d%d" % j][:, 0:256], A.is_lt, ["DS%d" % k], ["LT%d" % i], ["d%d" % j])
+
+        def count(b, bank):
+            for r in range(16):
+                mm(T[bank][:, 0:48], T.BM[:, 15 - r:143 - r], T.LT[:, 768 * b + r:768 * b + 768:16], r == 0, r == 15,
+                   ["BM"] + ["LT%d" % (3 * b + i) for i in range(3)], [bank])
+
+        for k in range(f):
+            gk(k)
+        lt(1, 0); lt(2, 0); lt(2, 1)
+        count(0, "d3")
+        if f == 4:
+            slot3_in()
+            lt(3, 0); lt(3, 1); lt(3, 2)
+            count(1, "d0")
+        b1, w20, w21 = sfl(10, 16), sfl(10, 16, 16), sfl(10, 16, 32)
+        e = [sfl(11 + j // 3, 16, 16 * (j % 3)) for j in range(9)]
+        ts(sfl(10), T.d3[:, 0:48], 9.0, A.is_ge, w=["wt"], x=["d3"])
+        tt(e[0], w21, w20, A.subtract, ["wt"], ["e0"])
+        tt(e[1], b1, sfl(9, 16), A.mult, ["wt", "sf9"], ["e1"])
+        tt(e[2], e[0], b1, A.mult, ["e0", "wt"], ["e2"])
+        tt(e[3], e[1], T.Z[:, 80:96], A.add, ["e1", "Z80"], ["e3"])
+        tt(e[4], e[2], w20, A.add, ["e2", "wt"], ["e4"])
+        tt(e[5], T.Z[:, 32:48], e[3], A.subtract, ["e3", "Z0"], ["e5"])
+        tt(e[6], e[5], e[4], A.mult, ["e5", "e4"], ["e6"])
+        tt(e[7], e[6], e[3], A.add, ["e6", "e3"], ["e7"])
+        z, zk = e[7], "e7"
+        if f == 4:
+            h = [sfl(16 + j // 3, 16, 16 * (j % 3)) for j in range(6)]
+            cp(sfl(14, 16, 32), e[4], ["e4"], ["s2"])
+            ts(e[8], e[4], -1.0, A.mult, 1.0, A.add, ["e4"], ["e8"])
+            tt(sfl(14, 16, 16), e[8], b1, A.mult, ["e8", "wt"], ["s1"])
+            tt(h[0], T.Z[:, 48:64], e[7], A.subtract, ["Z48", "e7"], ["h0"])
+            tt(sfl(14, 16), e[8], sfl(14, 16, 16), A.subtract, ["e8", "s1"], ["s0"])
+            tt(sfl(15), T.d0[:, 0:48], sfl(14), A.mult, ["s0", "s1", "s2"], ["m"], ["d0"])
+            tt(h[1], sfl(15, 16), sfl(15, 16, 16), A.add, ["m"], ["h1"])
+            tt(h[2], h[1], sfl(15, 16, 32), A.add, ["m", "h1"], ["h2"])
+            ts(h[3], h[2], 9.0, A.is_ge, r=["h2"], w=["h3"])
+            tt(h[4], h[3], h[0], A.mult, ["h3", "h0"], ["h4"])
+            tt(h[5], h[4], e[7], A.add, ["h4", "e7"], ["h5"])
+            z, zk = h[5], "h5"
+        ts(T.OFF[:, 64:80], z, 64.0 * (f - 1), A.add, r=[zk], w=["OFF4"])
+        if f == 3:
+            for c in range(NC):
+                ts(T.OFF[:, 16 * c + 12:16 * c + 16], T.sf[:, 48 * 13 + 16 + 4 * c:48 * 13 + 20 + 4 * c], 64.0 * (f - 1), A.add,
+                   r=[zk], w=["OFF3_%d" % c])
+        for c in range(NC):
+            preload(c, f)
+            gather(T.TT, "TT", c, f, "old", GATHER_A0)
+        return z, zk
+
+    def node_numbers(f, z, zk):
+        cp(si(19, 16), z, [zk], ["sa19"])
+        ts(si(21, 16), si(19, 16), 63, A.bitwise_and, r=["sa19"], w=["sa21"])
+        ts(si(22, 16), si(19, 16), 2, A.logical_shift_right, 192, A.bitwise_and, ["sa19"], ["sa22"])
+        ts(si(23, 16), si(19, 16), 1024.0, A.is_ge, 1280.0, A.mult, ["sa19"], ["sa23"])
+        tt(si(6, 16), si(21, 16), si(22, 16), A.add, ["sa21", "sa22"], ["sa6"])
+        tt(si(7, 16), si(6, 16), si(23, 16), A.add, ["sa6", "sa23"], ["sa7"])
+        if f == 3:
+            ts(si(20, 16), si(7, 16), 256.0 * (f - 1), A.add, r=["sa7"], w=["sa20"])
+        ts(T.YO[:, 16 * (f - 3):16 * (f - 2)], si(7, 16), 256.0 * (f - 1), A.add, r=["sa7"], w=["YO%d" % f])
+
+    def sweep(k, idle):
+        f = 3 + k // 3
+        first, last = k % 3 == 0, k % 3 == 2
+        nn = 64 * (f + 1)
+        dl, ld = T["dl%d" % k], T["ld%d" % k]
+        m0 = 2 + len(SENDS) * k + (1 if k > 1 else 0) + (1 if k > 2 else 0)
+        for c in range(NC):
+            b, d, dk, xk = 320 * c, T["d%d" % c], "d%d" % c, "X%d" % c
+            gather(T.TT, "TT", c, f, "new" if first else "all", GATHER_A)
+            tk = ["TT%d_%d" % (c, s) for s in range(f + 1)]
+            for lo, hi in ([(0, f), (f, f + 1)] if (c in SPLIT0 if first else f == 4 and c in SPLIT) else [(0, f + 1)]):
+                v = T.TT[:, b + 64 * lo:b + 64 * hi]
+                ts(v, v, 256.0, A.min, -256.0, A.max, tk[lo:hi], tk[lo:hi], k=0.5)
+            for s in range(f + 1):
+                for t in range(s + 1):
+                    m, mk = wd(s, t)
+                    mm(dreg(c, f, s), m, T.TT[:, b + 64 * t:b + 64 * t + 64], False, s == f and t == s and FLOOR[c] in "AV", [mk, tk[t]], [dk])
+            x0 = T.X[:, b:b + 64 * f:f]
+            if FLOOR[c] in "PQ":
+                mm(d[:, 0:nn], I1, T.MP[:, 0:nn], False, False, ["I1", "MP"], [dk])
+                mm(d[:, 0:nn], I1, T.MP[:, 320:320 + nn], False, True, ["I1", "MN"], [dk])
+                zc, x0 = T.ZC[:, 64 * c:64 * c + 64], d[:, 0:64 * f:f]
+                if FLOOR[c] == "Q":
+                    ts(zc, d[:, 64 * f:nn], T.wc[:, 23 + f:24 + f], A.mult, r=["wch"], w=["ZC%d" % c], x=[dk])
+                else:
+                    act(zc, d[:, 64 * f:nn], scale=T.wc[:, 23 + f:24 + f], r=["wch"], w=["ZC%d" % c], x=[dk])
+                tt(x0, x0, zc, A.add, ["ZC%d" % c], [], [dk])
+                add("v", lambda c=c, d=d: g.vector.tensor_tensor_scan(dl[:, 64 * f * c:64 * f * (c + 1)], T["PAT%d" % f][:, :],
+                                                                      d[:, 0:64 * f], 1536.0, A.mult, A.add),
+                    ["PAT%d_%d" % (f, j) for j in range(f)], ["dl%d_%d" % (k, c)], [dk], cost=0.05 + 64 * f * CYC)
+                for i, cs in enumerate(SENDS):
+                    if cs[-1] == c:
+                        send(m0 + i, ["dl%d_%d" % (k, q) for q in cs])
+                continue
+            if FLOOR[c] == "H":
+                mm(d[:, 0:nn], I1, T.MP[:, 0:nn], False, True, ["I1", "MP"], [dk])
+                act(T.X[:, b:b + nn], d[:, 0:nn], bias=-MAG, w=[xk], x=[dk])
+                act(d[:, 320:384], d[:, 64 * f:nn], bias=T.wc[:, 27 + f:28 + f], scale=T.wc[:, 23 + f:24 + f], r=["wch", "wcm"], x=[dk])
+                tt(x0, x0, d[:, 320:384], A.add, [xk], [xk], [dk])
+            elif FLOOR[c] == "A":
+                act(T.V[:, b:b + nn], d[:, 0:nn], bias=MAG, w=["V%d" % c], x=[dk])
+                act(d[:, 320:384], T.V[:, b + 64 * f:b + nn], bias=T.wc[:, 27 + f:28 + f], scale=T.wc[:, 23 + f:24 + f],
+                    r=["V%d" % c, "wch", "wcm"], x=[dk])
+                act(T.X[:, b:b + nn], T.V[:, b:b + nn], bias=-MAG, r=["V%d" % c], w=[xk])
+                tt(x0, x0, d[:, 320:384], A.add, [xk], [xk], [dk])
+            else:
+                ts(T.X[:, b:b + nn], d[:, 0:nn], MAG, A.add, -MAG, A.add, w=[xk], x=[dk])
+                ts(d[:, 320:384], T.X[:, b + 64 * f:b + nn], T.wc[:, 23 + f:24 + f], A.mult, r=[xk, "wch"], x=[dk])
+                tt(x0, x0, d[:, 320:384], A.add, [xk], [xk], [dk])
+            add("v", lambda c=c, b=b: g.vector.tensor_tensor_scan(dl[:, 64 * f * c:64 * f * (c + 1)], T["PAT%d" % f][:, :],
+                                                                  T.X[:, b:b + 64 * f], 1536.0, A.mult, A.add),
+                [xk] + ["PAT%d_%d" % (f, j) for j in range(f)], ["dl%d_%d" % (k, c)], cost=0.05 + 64 * f * CYC)
+            for i, cs in enumerate(SENDS):
+                if cs[-1] == c:
+                    send(m0 + i, ["dl%d_%d" % (k, q) for q in cs])
+        for c in range(NC):
+            df = T.DF[:, 64 * c:64 * c + 64] if f == 4 else T.S3[:, 256 * (k + 1) + 64 * c:256 * (k + 1) + 64 * c + 64]
+            dfk = "DF%d" % c if f == 4 else "S3_%d%d" % (k, c)
+            if FLOOR[c] in "PQ":
+                ts(df, T["d%d" % c][:, 64 * f:nn], 1536.0 - 15.0 / 32, A.add, w=[dfk], x=["d%d" % c])
+            else:
+                ts(df, T.X[:, 320 * c + 64 * f:320 * c + nn], 1536.0 - 15.0 / 32, A.add, r=["X%d" % c], w=[dfk])
+            for s in range(f):
+                mm(reg(hb(c), c, s), I1, dl[:, 64 * f * c + f - 1 - s:64 * f * (c + 1):f], c % 2 == 0 and s == 0, c % 2 == 1 and s == 3,
+                   ["I1", "dl%d_%d" % (k, c)], [hb(c)])
+            if f == 3:
+                mm(reg(hb(c), c, 3), I1, df, False, c % 2 == 1, ["I1", dfk], [hb(c)])
+            if c % 2 == 1:
+                h = c // 2
+                after = GATHER_AF if k == 5 else GATHER_A0 if k == 2 else GATHER_A
+                for cs in ([[c - 1, c]] if (c - 1 in after) == (c in after) else [[c - 1], [c]]):
+                    a0, a1 = 256 * cs[0], 256 * cs[-1] + 256
+                    ph, wh, hk = T["ph%d" % h][:, a0 - 512 * h:a1 - 512 * h], W[:, a0:a1], [HK[q] for q in cs]
+                    if cs[0] in after:
+                        tt(ph, ph, wh, A.add, hk, [], ["ph%d" % h])
+                        act(wh, ph, w=hk, x=["ph%d" % h])
+                    else:
+                        tt(T.RH[:, a0:a1], ph, wh, A.add, hk, ["RH%d" % q for q in cs], ["ph%d" % h])
+                        act(wh, T.RH[:, a0:a1], r=["RH%d" % q for q in cs], w=hk)
+        if f == 4:
+            tt(T.H4[:, :], T.H4[:, :], T.DF[:, :], A.add, ["H4"] + ["DF%d" % c for c in range(NC)], ["H4"])
+        idle()
+        if not last:
+            for c in range(NC):
+                preload(c, f)
+        for i, cs in enumerate(SENDS):
+            arrive(m0 + i, ["ld%d_%d" % (k, c) for c in cs])
+            for c in cs:
+                for s in range(f):
+                    mm(reg(ab(c), c, s), I1, ld[:, 64 * f * c + f - 1 - s:64 * f * (c + 1):f], s == 0, s == f - 1,
+                       ["I1", "ld%d_%d" % (k, c)], [ab(c)])
+                wa = W[:, 1024 + 256 * c:1024 + 256 * c + 64 * f]
+                tt(wa, wa, reg(ab(c), c, 0, f), A.add, [AK[c]], [AK[c]], [ab(c)])
+        marks.append(len(ops) - 1)
+
+    def stakes(cs):
+        for c in cs:
+            for s in range(5):
+                act(T.stc[:, 320 * c + 64 * s:320 * c + 64 * s + 64], T.stb[:, 256 * s + 64 * c:256 * s + 64 * c + 64],
+                    r=["stb", HK[3]], w=["stc%d_%d" % (c, s)])
+
+    z3, z3k = part1(3)
+
+    def idle0():
+        node_numbers(3, z3, z3k)
+        ts(si(5, 16), z3, 128.0, A.add, r=[z3k], w=["sa5"])
+        act(T.aw[:, 0:16], z3, F.Sigmoid, bias=-1856.0, scale=2.0, r=[z3k, HK[3]], w=["aw"], more=1.3)
+        lookup_list(si(20, 16), "sa20", si(5, 16), "sa5", 16, 48, T.aw[:, 0:16], "aw")
+        tt(T.wc[:, 9:10], T.wc[:, 7:8], T.wc[:, 15:16], A.mult, ["w3", "wa"], ["w4"])
+        for j in (3, 6, 8, 9):
+            diag(j)
+        const(4, 2, T.wc[:, 18:19], "d0", "d1")
+
+    S3K = ["N3"] + ["S3_%d%d" % (k, c) for k in range(3) for c in range(NC)]
+
+    def idle1():
+        send(2 + 2 * len(SENDS), S3K[:9])
+        lookup_gather(16, 48, "d2")
+        lookup_finish(16, 48, "d2")
+        const(5, 3, BK, "d0", "d1")
+        const(6, 4, B0, "d0", "d1")
+
+    def idle2():
+        send(3 + 3 * len(SENDS), S3K[9:])
+        for h in range(4):
+            mm(T.d2[:, 0:256], I1, T.S3[:, 256 * h:256 * h + 256], h == 0, h == 3, ["I1"] + S3K, ["d2"])
+        act(T.ME[:, :], T.d2[:, 0:256], w=MEK, x=["d2"])
+        new_rating([(0, 256, T.S3[:, 256 * h:256 * h + 256]) for h in range(4)], S3K, "d3", T.H4[:, :], "H4")
+        pattern(4)
+
+    sweep(0, idle0)
+    sweep(1, idle1)
+    sweep(2, idle2)
+    z4, z4k = part1(4)
+
+    def idle3():
+        node_numbers(4, z4, z4k)
+        dma("s", T.yo[:, :], T.YO[:, :], r=["YO3", "YO4"])
+        stakes([0, 1])
+
+    def idle4():
+        act(T.I32[:, :], I1, r=["I1"], w=["I32"])
+        stakes([2, 3])
+
+    def idle5():
+        ts(T.YR[:, 1024:1280], T.H4[:, :], -9216.0, A.add, r=["H4"], w=["YR4"])
+        for c in range(NC):
+            for s in range(4):
+                o = T.YR[:, 256 * s + 64 * c:256 * s + 64 * c + 64]
+                if c < 2:
+                    ts(o, W[:, 256 * c + 64 * s:256 * c + 64 * s + 64], -9216.0, A.add, r=[HK[c]], w=["YR%d%d" % (c, s)])
+                else:
+                    act(o, W[:, 256 * c + 64 * s:256 * c + 64 * s + 64], bias=-9216.0, r=[HK[c]], w=["YR%d%d" % (c, s)])
+        dma("s", T.yr[:, :], T.YR[:, :], r=["YR4"] + ["YR%d%d" % (c, s) for c in range(NC) for s in range(4)])
+
+    sweep(3, idle3)
+    sweep(4, idle4)
+    sweep(5, idle5)
+
+    for c in range(NC):
+        b, d, dk = 320 * c, T["d%d" % c], "d%d" % c
+        gather(T.TK, "TF", c, 4, "all", GATHER_AF)
+        act(d[:, 0:320], T.TK[:, b:b + 320], F.Sigmoid, scale=-1.0 / 256, r=["TF%d_%d" % (c, s) for s in range(5)], x=[dk])
+        sk = ["stc%d_%d" % (c, s) for s in range(5)]
+        if c in SUM_V:
+            tt(T.DS[:, b:b + 192], d[:, 0:192], T.stc[:, b:b + 192], A.mult, sk, ["PR%d" % c], [dk])
+            tt(d[:, 192:320], d[:, 192:320], T.stc[:, b + 192:b + 320], A.mult, sk, [], [dk])
+            tt(d[:, 0:128], d[:, 192:320], T.DS[:, b:b + 128], A.add, ["PR%d" % c], [], [dk])
+            tt(T.DS[:, b:b + 64], d[:, 0:64], T.DS[:, b + 128:b + 192], A.add, ["PR%d" % c], ["PR%d" % c], [dk])
+            tt(T.Y[:, 64 * c:64 * c + 64], d[:, 64:128], T.DS[:, b:b + 64], A.add, ["PR%d" % c], ["Y%d" % c], [dk])
+        else:
+            tt(T.DS[:, b:b + 320], d[:, 0:320], T.stc[:, b:b + 320], A.mult, sk, ["PR%d" % c], [dk])
+            for s in range(5):
+                mm(d[:, 320:384], T.I32[:, :], T.DS[:, b + 64 * s:b + 64 * s + 64], s == 0, s == 4, ["I32", "PR%d" % c], [dk], k=4.0)
+            act(T.Y[:, 64 * c:64 * c + 64], d[:, 320:384], w=["Y%d" % c], x=[dk])
+        if c % 2 == 1:
+            dma("s", T.y[:, 64 * c - 64:64 * c + 64], T.Y[:, 64 * c - 64:64 * c + 64], r=["Y%d" % (c - 1), "Y%d" % c])
+
+    if "order" not in KEPT:
+        KEPT["order"] = _order(ops, marks)
+    order = KEPT["order"]
+    place = {i: p for p, i in enumerate(order)}
+
+    queue = {"v": g.vector, "a": g.scalar, "p": g.tensor, "g": g, "s": g.sync}
+    semof = {"v": "sv", "a": "sa", "p": "sp", "g": "sg"}
+    needed = set()
+    for o in ops:
+        newest, keep = {}, []
+        for j in o["deps"]:
+            qj = ops[j]["q"]
+            if ops[j]["tok"] is not None:
+                keep.append(j)
+            elif not (qj == "p" and o["q"] == "p") and place[j] > place.get(newest.get(qj), -1):
+                newest[qj] = j
+        o["wait"] = keep + list(newest.values())
+        needed.update(o["wait"])
+    cnt, known, clock, top = {}, {q: {} for q in queue}, {}, {}
+    for i in order:
+        o = ops[i]
+        q = o["q"]
+        if q == "r":
+            clock[i] = {o["tok"][0]: o["tok"][1]}
+            top[o["tok"][0]] = o["tok"][1]
+            o["own"] = o["tok"][:2]
+            continue
+        kn = known[q]
+        for j in sorted(o["wait"], key=lambda j: -place[j]):
+            own = ops[j]["own"]
+            if own is not None and kn.get(own[0], 0) < own[1]:
+                queue[q].wait_ge(T.sem[own[0]], own[1])
+            for s, v in clock[j].items():
+                if kn.get(s, 0) < v:
+                    kn[s] = v
+        ck = dict(kn)
+        o["own"] = None
+        ins = o["fn"]()
+        if o["tok"] is not None:
+            if o["tok"][2]:
+                ins.then_inc(T.sem[o["tok"][0]], 16)
+                o["own"] = o["tok"][:2]
+        elif q != "p" or i in needed:
+            s = semof[q]
+            cnt[s] = cnt.get(s, 0) + 1
+            ins.then_inc(T.sem[s], 1)
+            o["own"] = (s, cnt[s])
+        if o["own"] is not None:
+            ck[o["own"][0]] = o["own"][1]
+            top[o["own"][0]] = o["own"][1]
+        clock[i] = ck
+    top["ls"] = nsent[0]
+    for s, v in top.items():
+        if known["g"].get(s, 0) < v:
+            g.wait_ge(T.sem[s], v)

@@ -13,7 +13,7 @@ FLOOR = "PHHP"
 GATHER_A, GATHER_A0, GATHER_AF = [1, 2, 3], [0, 1, 2, 3], [1]
 SPLIT, SPLIT0 = [0], [0, 1, 2, 3]
 SUM_V = [3]
-CYC, PCYC, RLAT, RATE, SYNC = 0.001, 0.0006, 2.2, 80e3, 0.06
+CYC, PCYC, PFIX, RLAT, RATE, SYNC = 0.0009, 0.00065, 0.0, 2.0, 100e3, 0.09
 
 SCRATCH = {
     "r0i": ("sbuf", [128, 768], "int32"), "oppi": ("sbuf", [128, 48], "int32"), "mub": ("sbuf", [128, 8], "bfloat16"),
@@ -25,18 +25,19 @@ SCRATCH = {
     "kf": ("sbuf", [128, 8], "float32"), "PL": ("sbuf", [128, 4], "uint16"),
     "TM": ("sbuf", [128, 2048], "bfloat16"), "BM": ("sbuf", [128, 144], "bfloat16"), "I1": ("sbuf", [128, 144], "bfloat16"),
     "I2": ("sbuf", [128, 128], "bfloat16"), "I32": ("sbuf", [128, 128], "float32"), "WD": ("sbuf", [128, 11 * 128], "bfloat16"),
-    "wc": ("sbuf", [128, 32], "float32"), "PAT3": ("sbuf", [128, 192], "float32"), "PAT4": ("sbuf", [128, 256], "float32"),
-    "CH": ("sbuf", [128, 7 * 256], "bfloat16"), "CL": ("sbuf", [128, 7 * 256], "float16"),
+    "wc": ("sbuf", [128, 32], "float32"), "PAT3": ("sbuf", [128, 256], "float32"), "PAT4": ("sbuf", [128, 320], "float32"),
+    "CH": ("sbuf", [128, 9 * 256], "bfloat16"), "CL": ("sbuf", [128, 9 * 256], "float16"),
     "o16": ("sbuf", [128, 48], "float16"), "aw": ("sbuf", [128, 48], "bfloat16"),
     "LW": ("sbuf", [128, 768], "float32"), "REP": ("sbuf", [128, 768], "float16"),
     "u1": ("sbuf", [128, 64], "uint16"), "OFF": ("sbuf", [128, 80], "uint16"), "CO": ("sbuf", [128, 64], "uint16"),
+    "WT": ("sbuf", [128, 48], "bfloat16"), "WI": ("sbuf", [128, 64], "bfloat16"), "UI": ("sbuf", [128, 64], "float32"),
+    "VI": ("sbuf", [128, 64], "float32"), "ZI": ("sbuf", [128, 64], "float32"), "SC": ("sbuf", [128, 128], "float32"),
     "RH": ("sbuf", [128, 1024], "float32"), "MP": ("sbuf", [128, 640], "bfloat16"),
     "OP": ("sbuf", [128, 64], "int32"), "OQ": ("sbuf", [128, 64], "int32"),
     "sa": ("sbuf", [128, 48 * 24], "int32"), "sf": ("sbuf", [128, 48 * 18], "float32"), "Z": ("sbuf", [128, 96], "int32"),
     "TK": ("sbuf", [128, 1280], "float32"), "DS": ("sbuf", [128, 1280], "float32"), "LT": ("sbuf", [128, 1536], "bfloat16"),
     "TT": ("sbuf", [128, 1280], "bfloat16"), "V": ("sbuf", [128, 1280], "float32"), "X": ("sbuf", [128, 1280], "float32"),
-    "ZC": ("sbuf", [128, 256], "float32"), "DF": ("sbuf", [128, 256], "float16"),
-    "NT": ("sbuf", [128, 256], "float32"), "S3": ("sbuf", [128, 1024], "float16"), "L3": ("sbuf", [128, 1024], "float16"),
+    "NT": ("sbuf", [128, 256], "float32"), "S3": ("sbuf", [128, 256], "float16"),
     "YR": ("sbuf", [128, 1280], "float32"), "YO": ("sbuf", [128, 32], "float32"), "Y": ("sbuf", [128, 256], "float32"),
     "ph0": ("psum", [128, 512], "float32"), "ph1": ("psum", [128, 512], "float32"),
     "pa0": ("psum", [128, 512], "float32"), "pa1": ("psum", [128, 512], "float32"),
@@ -44,8 +45,8 @@ SCRATCH = {
     "d2": ("psum", [128, 512], "float32"), "d3": ("psum", [128, 512], "float32"),
 }
 for _k in range(6):
-    SCRATCH["dl%d" % _k] = ("sbuf", [128, 256 * (3 + _k // 3)], "float16")
-    SCRATCH["ld%d" % _k] = ("sbuf", [128, 256 * (3 + _k // 3)], "float16")
+    SCRATCH["dl%d" % _k] = ("sbuf", [128, 256 * (4 + _k // 3)], "float16")
+    SCRATCH["ld%d" % _k] = ("sbuf", [128, 256 * (4 + _k // 3)], "float16")
 SEMAPHORES = ["sv", "sa", "sp", "sg", "ls"] + ["dm%d" % i for i in range(12)] + ["ar%d" % i for i in range(4 + 6 * NC)]
 
 
@@ -65,11 +66,7 @@ def _messages():
     for k in range(6):
         f = 3 + k // 3
         for i, cs in enumerate(SENDS):
-            ms.append(("dl%d" % k, "ld%d" % k, CP * f * cs[0], CP * f * (cs[-1] + 1), VIA[i]))
-        if k == 1:
-            ms.append(("S3", "L3", 0, 768, False))
-        if k == 2:
-            ms.append(("S3", "L3", 768, 1024, False))
+            ms.append(("dl%d" % k, "ld%d" % k, CP * (f + 1) * cs[0], CP * (f + 1) * (cs[-1] + 1), VIA[i]))
     return ms
 
 
@@ -238,13 +235,13 @@ def rank_program(g, core, T, topo):
         add("a", lambda: g.scalar.activation(out, in_, func, bias=bias, scale=scale), r, w, x, cost=cy(out) + 0.03 + more)
 
     def mm(out, lhs, rhs, start, stop, r=(), x=(), k=1.0):
-        add("p", lambda: g.tensor.matmul(out, lhs, rhs, start, stop), r, (), x, cost=max(64, out.shape[1]) * k * PCYC)
+        add("p", lambda: g.tensor.matmul(out, lhs, rhs, start, stop), r, (), x, cost=PFIX + max(64, out.shape[1]) * k * PCYC)
 
     def dma(q, out, in_, r=(), w=()):
         s = "dm%d" % ndma[0]
         ndma[0] += 1
         eng = g.sync if q == "s" else g.scalar
-        add(q, lambda: eng.dma_start(out, in_), r, w, (), (s, 16, True), cost=0.1, lat=1.9 + out.shape[1] / 700)
+        add(q, lambda: eng.dma_start(out, in_), r, w, (), (s, 16, True), cost=0.1, lat=1.9 + out.shape[1] / 400)
 
     def iota(out, pat, cm, key, small):
         if small:
@@ -318,7 +315,9 @@ def rank_program(g, core, T, topo):
         cp(T.CO[:, c0:c0 + m], sfl(6, m), ["sf6"], ["CO%d" % c0])
 
     def const(j, s, bias, bank, tmp):
-        cs = slice(256 * j, 256 * j + 256)
+        f = 3 if j < 4 else 4
+        o = 1024 * (f - 3)
+        cs = slice(o + f - s, o + 256 * (f + 1), f + 1)
         for t in range(s + 1):
             m, k = wd(s, t)
             mm(T[bank][:, 0:256], m, T.ocb[:, 256 * t:256 * t + 256], t == 0, t == s, [k, "ocb"], [bank])
@@ -326,24 +325,23 @@ def rank_program(g, core, T, topo):
         act(T[tmp][:, 0:256], T[bank][:, 0:256], bias=bias, r=["wc"], x=[bank, tmp])
         tt(T.CL[:, cs], T[tmp][:, 0:256], T.CH[:, cs], A.subtract, ["CH%d" % j], ["CL%d" % j], [tmp])
 
-    CV = {3: [0, 1, 2, 3], 4: [0, 1, 4, 5, 6]}
+    CV = {3: [0, 1, 2, 3], 4: [7, 8, 4, 5, 6]}
     BK, B0 = KOFF - 15.0 / 512, -15.0 / 512
 
     def dreg(c, f, s):
         d = T["d%d" % c]
-        return d[:, 64 * f:64 * f + 64] if s == f else d[:, f - 1 - s:64 * f:f]
+        return d[:, f - s:64 * (f + 1):f + 1]
 
     def preload(c, f):
-        for s in range(f + 1):
-            j = CV[f][s]
-            cs = slice(256 * j + 64 * c, 256 * j + 64 * c + 64)
-            mm(dreg(c, f, s), I1, T.CH[:, cs], s == 0, False, ["I1", "CH%d" % j], ["d%d" % c])
-            mm(dreg(c, f, s), I1, T.CL[:, cs], False, False, ["I1", "CL%d" % j], ["d%d" % c])
+        o, d = 1024 * (f - 3), T["d%d" % c]
+        for out, a0, m, js in ((d[:, 0:64 * f + 64], o + (64 * f + 64) * c, 64 * f + 64, CV[f]),):
+            mm(out, I1, T.CH[:, a0:a0 + m], m > 64, False, ["I1"] + ["CH%d" % j for j in js], ["d%d" % c])
+            mm(out, I1, T.CL[:, a0:a0 + m], False, False, ["I1"] + ["CL%d" % j for j in js], ["d%d" % c])
 
     def gather(out, ok, c, f, part, scalar):
         b = 320 * c
-        lo = 0 if part != "new" else f
-        hi = min(4, f if part == "old" else f + 1)
+        lo = f if part == "new" else 2 if part == "high" else 0
+        hi = 2 if part == "low" else min(4, f if part == "old" else f + 1)
         if lo < hi:
             r = WIN + ["OFF"] + (["OFF3_%d" % c] if hi == 4 else [])
             q, w = win.indirect(T.OFF[:, 16 * c + 4 * lo:16 * c + 4 * hi]), [ok + "%d_%d" % (c, s) for s in range(lo, hi)]
@@ -356,7 +354,7 @@ def rank_program(g, core, T, topo):
                    A.subtract, WIN + ["OFF4", "N3"], w, k=1.5)
             else:
                 tt(out[:, b + 64 * lo:b + 64 * hi], q, T.RH[:, 256 * c + 64 * lo:256 * c + 64 * hi], A.subtract, r + ["RH%d" % c], w, k=1.5)
-        if f == 4 and part != "old":
+        if f == 4 and part not in ("old", "low"):
             tt(out[:, b + 256:b + 320], win.indirect(T.OFF[:, 64 + 4 * c:68 + 4 * c]), T.H4[:, 64 * c:64 * c + 64],
                A.subtract, WIN + ["OFF4", "H4"], [ok + "%d_4" % c], k=1.5)
 
@@ -366,7 +364,12 @@ def rank_program(g, core, T, topo):
         for i, (m, k, (o0, o1, rhs)) in enumerate(jobs):
             mm(T[bank][:, o0:o1], m, rhs, i == 0, i == len(jobs) - 1, [k] + keys, [bank])
         act(T.NT[:, :], T[bank][:, 0:256], bias=-0.25, scale=0.5, w=["NT"], x=[bank])
-        ts(out, T.NT[:, :], MAG1, A.add, -MAG1, A.add, ["NT"], [ok])
+        if out is not None:
+            ts(out, T.NT[:, :], MAG1, A.add, -MAG1, A.add, ["NT"], [ok])
+            return
+        act(T.ME[:, :], T.NT[:, :], bias=MAG1, r=["NT"], w=MEK)
+        for c in range(NC):
+            act(W[:, 1024 + 256 * c + 192:1024 + 256 * c + 256], T.ME[:, 64 * c:64 * c + 64], bias=-MAG1, r=MEK, w=[AK[c]])
 
     def away_copy(c, m, scalar):
         o = W[:, 1024 + 256 * c:1024 + 256 * c + 64 * m]
@@ -387,8 +390,8 @@ def rank_program(g, core, T, topo):
     iota(T.zs0[:, :], [[0, 3], [256, 4], [16, 4]], 0, "zs0", False)
     act(W[:, 2048:2056], T.tb[:, 0:8], scale=0.0, bias=BIGV, r=["tb"], w=["WB"])
     ms(T.OP[:, 48:64], 0, ["OPz"])
-    ms(T.PAT3[:, 0:192:3], ETA, ["PAT3_0"])
-    ms(T.PAT4[:, 0:256:4], ETA, ["PAT4_0"])
+    ms(T.PAT3[:, 0:256:4], ETA, ["PAT3_0"])
+    ms(T.PAT4[:, 0:320:5], ETA, ["PAT4_0"])
     for c in range(NC):
         act(W[:, 1024 + 256 * c + 192:1024 + 256 * c + 256], T.tb[:, 0:64], scale=0.0, r=["tb"], w=[AK[c]])
     for r in range(16):
@@ -451,8 +454,6 @@ def rank_program(g, core, T, topo):
         diag(j)
     act(T.wc[:, 16:20], T.mub[:, 4:8], scale=-KOFF / 2, bias=BK, r=["mu"], w=["wc"])
     act(T.wc[:, 20:24], T.mub[:, 4:8], scale=0.5, bias=ETA, r=["mu"], w=["wce"])
-    act(T.wc[:, 24:28], T.mub[:, 4:8], scale=0.5, r=["mu"], w=["wch"])
-    act(T.wc[:, 28:32], T.mub[:, 4:8], scale=-MAG / 2, r=["mu"], w=["wcm"])
     for c in range(NC):
         mm(reg(hb(c), c, 3), I1, T.S3[:, 64 * c:64 * c + 64], False, c % 2 == 1, ["I1", "N3"], [hb(c)])
     lookup_finish(48, 0, "d2")
@@ -464,17 +465,21 @@ def rank_program(g, core, T, topo):
     const(0, 0, T.wc[:, 16:17], "d0", "d1")
     const(1, 1, T.wc[:, 17:18], "d0", "d1")
     ts(T.Z[:, 64:80], T.OP[:, 0:16], 0x73F, A.bitwise_and, r=["OP"], w=["Z64"])
-    const(2, 2, BK, "d0", "d3")
-    const(3, 3, B0, "d1", "d3")
+    const(2, 2, T.wc[:, 18:19], "d0", "d3")
+    const(3, 3, BK, "d1", "d3")
     tt(sfl(7, 16), T.Z[:, 64:80], T.Z[:, 0:16], A.subtract, ["Z64", "Z0"], ["sf7"])
     tt(sfl(8, 16), sfl(7, 16), sfl(4, 16), A.mult, ["sf7", "sf4"], ["sf8"])
-    tt(T.Z[:, 80:96], sfl(8, 16), T.Z[:, 0:16], A.add, ["sf8", "Z0"], ["Z80"])
-    tt(sfl(9, 16), T.Z[:, 16:32], T.Z[:, 80:96], A.subtract, ["Z80", "Z0"], ["sf9"])
+    tt(T.ZI[:, 0:64:4], sfl(8, 16), T.Z[:, 0:16], A.add, ["sf8", "Z0"], ["ZI0"])
+    for j in (1, 2):
+        cp(T.ZI[:, j:64:4], T.Z[:, 16 * j:16 * j + 16], ["Z0"], ["ZI%d" % j])
+    act(T.ZI[:, 3:64:4], T.tb[:, 0:16], scale=0.0, r=["tb"], w=["ZI3"])
+    act(T.WI[:, 0:64:4], T.tb[:, 0:16], scale=0.0, bias=1.0, r=["tb"], w=["WI0"])
+    act(T.WI[:, 3:64:4], T.tb[:, 0:16], scale=0.0, r=["tb"], w=["WI3"])
 
     def pattern(f):
-        for j in range(1, f):
-            s = f - 1 - j
-            act(T["PAT%d" % f][:, j:64 * f:f], T.io2[:, 0:64], bias=T.wc[:, 20 + s:21 + s], scale=0.0, r=["io2", "wce"], w=["PAT%d_%d" % (f, j)])
+        for j in range(1, f + 1):
+            s = f - j
+            act(T["PAT%d" % f][:, j:64 * f + 64:f + 1], T.io2[:, 0:64], bias=T.wc[:, 20 + s:21 + s], scale=0.0, r=["io2", "wce"], w=["PAT%d_%d" % (f, j)])
 
     pattern(3)
     for h in range(2):
@@ -485,17 +490,6 @@ def rank_program(g, core, T, topo):
                 mm(reg(ab(c), c, s), I1, T.l0[:, o:o + 64], c % 2 == 0 and s == 0, c % 2 == 1 and s == 2, ["I1", "l0_%d" % h], [ab(c)])
         for c in (2 * h, 2 * h + 1):
             away_copy(c, 3, h == 0)
-
-    def slot3_in():
-        arrive(2 + 2 * len(SENDS), ["L3a"])
-        arrive(3 + 3 * len(SENDS), ["L3b"])
-        for c in range(NC):
-            for h in range(4):
-                mm(reg(ab(c), c, 3), I1, T.L3[:, 256 * h + 64 * c:256 * h + 64 * c + 64], c % 2 == 0 and h == 0, c % 2 == 1 and h == 3,
-                   ["I1", "L3b" if h == 3 else "L3a"], [ab(c)])
-            if c % 2 == 1:
-                for q in (c - 1, c):
-                    act(W[:, 1024 + 256 * q + 192:1024 + 256 * q + 256], reg(ab(q), q, 3), w=[AK[q]], x=[ab(q)])
 
     def part1(f):
         pair = {(1, 0): 0, (2, 0): 1, (2, 1): 2, (3, 0): 3, (3, 1): 4, (3, 2): 5}
@@ -523,40 +517,35 @@ def rank_program(g, core, T, topo):
         lt(1, 0); lt(2, 0); lt(2, 1)
         count(0, "d3")
         if f == 4:
-            slot3_in()
             lt(3, 0); lt(3, 1); lt(3, 2)
             count(1, "d0")
-        b1, w20, w21 = sfl(10, 16), sfl(10, 16, 16), sfl(10, 16, 32)
-        e = [sfl(11 + j // 3, 16, 16 * (j % 3)) for j in range(9)]
-        ts(sfl(10), T.d3[:, 0:48], 9.0, A.is_ge, w=["wt"], x=["d3"])
+        b1, w20, w21 = T.WT[:, 0:16], T.WT[:, 16:32], T.WT[:, 32:48]
+        e = [sfl(11 + j // 3, 16, 16 * (j % 3)) for j in range(6)]
+        ts(T.WT[:, :], T.d3[:, 0:48], 9.0, A.is_ge, w=["wt"], x=["d3"])
+        act(T.WI[:, 1:64:4], b1, r=["wt"], w=["WI1"])
         tt(e[0], w21, w20, A.subtract, ["wt"], ["e0"])
-        tt(e[1], b1, sfl(9, 16), A.mult, ["wt", "sf9"], ["e1"])
         tt(e[2], e[0], b1, A.mult, ["e0", "wt"], ["e2"])
-        tt(e[3], e[1], T.Z[:, 80:96], A.add, ["e1", "Z80"], ["e3"])
-        tt(e[4], e[2], w20, A.add, ["e2", "wt"], ["e4"])
-        tt(e[5], T.Z[:, 32:48], e[3], A.subtract, ["e3", "Z0"], ["e5"])
-        tt(e[6], e[5], e[4], A.mult, ["e5", "e4"], ["e6"])
-        tt(e[7], e[6], e[3], A.add, ["e6", "e3"], ["e7"])
-        z, zk = e[7], "e7"
+        tt(T.WI[:, 2:64:4], e[2], w20, A.add, ["e2", "wt"], ["WI2"])
         if f == 4:
-            h = [sfl(16 + j // 3, 16, 16 * (j % 3)) for j in range(6)]
-            cp(sfl(14, 16, 32), e[4], ["e4"], ["s2"])
-            ts(e[8], e[4], -1.0, A.mult, 1.0, A.add, ["e4"], ["e8"])
-            tt(sfl(14, 16, 16), e[8], b1, A.mult, ["e8", "wt"], ["s1"])
-            tt(h[0], T.Z[:, 48:64], e[7], A.subtract, ["Z48", "e7"], ["h0"])
-            tt(sfl(14, 16), e[8], sfl(14, 16, 16), A.subtract, ["e8", "s1"], ["s0"])
+            act(sfl(14, 16, 32), T.WI[:, 2:64:4], r=["WI2"], w=["s2"])
+            act(e[3], T.WI[:, 2:64:4], scale=-1.0, bias=1.0, r=["WI2"], w=["e3"])
+            tt(sfl(14, 16, 16), e[3], b1, A.mult, ["e3", "wt"], ["s1"])
+            tt(sfl(14, 16), e[3], sfl(14, 16, 16), A.subtract, ["e3", "s1"], ["s0"])
             tt(sfl(15), T.d0[:, 0:48], sfl(14), A.mult, ["s0", "s1", "s2"], ["m"], ["d0"])
-            tt(h[1], sfl(15, 16), sfl(15, 16, 16), A.add, ["m"], ["h1"])
-            tt(h[2], h[1], sfl(15, 16, 32), A.add, ["m", "h1"], ["h2"])
-            ts(h[3], h[2], 9.0, A.is_ge, r=["h2"], w=["h3"])
-            tt(h[4], h[3], h[0], A.mult, ["h3", "h0"], ["h4"])
-            tt(h[5], h[4], e[7], A.add, ["h4", "e7"], ["h5"])
-            z, zk = h[5], "h5"
+            tt(e[4], sfl(15, 16), sfl(15, 16, 16), A.add, ["m"], ["e4"])
+            tt(e[5], e[4], sfl(15, 16, 32), A.add, ["m", "e4"], ["e5"])
+            ts(T.WI[:, 3:64:4], e[5], 9.0, A.is_ge, r=["e5"], w=["WI3"])
+        wk = ["WI%d" % j for j in range(4)]
+        act(T.UI[:, :], T.WI[:, :], scale=-1.0, bias=1.0, r=wk, w=["UI"])
+        tt(T.VI[:, :], T.WI[:, :], T.ZI[:, :], A.mult, wk + ["ZI%d" % j for j in range(4)], ["VI"], k=1.0)
+        o = 64 * (f - 3)
+        zk = "SC%d" % f
+        add("v", lambda: g.vector.tensor_tensor_scan(T.SC[:, o:o + 64], T.UI[:, :], T.VI[:, :], 0.0, A.mult, A.add), ["UI", "VI"], [zk], cost=0.11)
+        z = T.SC[:, o + 3:o + 64:4]
         ts(T.OFF[:, 64:80], z, 64.0 * (f - 1), A.add, r=[zk], w=["OFF4"])
         if f == 3:
             for c in range(NC):
-                ts(T.OFF[:, 16 * c + 12:16 * c + 16], T.sf[:, 48 * 13 + 16 + 4 * c:48 * 13 + 20 + 4 * c], 64.0 * (f - 1), A.add,
-                   r=[zk], w=["OFF3_%d" % c])
+                ts(T.OFF[:, 16 * c + 12:16 * c + 16], T.SC[:, 16 * c + 3:16 * c + 16:4], 64.0 * (f - 1), A.add, r=[zk], w=["OFF3_%d" % c])
         for c in range(NC):
             preload(c, f)
             gather(T.TT, "TT", c, f, "old", GATHER_A0)
@@ -578,68 +567,43 @@ def rank_program(g, core, T, topo):
         first, last = k % 3 == 0, k % 3 == 2
         nn = 64 * (f + 1)
         dl, ld = T["dl%d" % k], T["ld%d" % k]
-        m0 = 2 + len(SENDS) * k + (1 if k > 1 else 0) + (1 if k > 2 else 0)
+        m0 = 2 + len(SENDS) * k
         for c in range(NC):
             b, d, dk, xk = 320 * c, T["d%d" % c], "d%d" % c, "X%d" % c
-            gather(T.TT, "TT", c, f, "new" if first else "all", GATHER_A)
+            cut = not first and c in SPLIT
+            if cut:
+                gather(T.TT, "TT", c, f, "low", GATHER_A)
+            gather(T.TT, "TT", c, f, "new" if first else "high" if cut else "all", GATHER_A)
             tk = ["TT%d_%d" % (c, s) for s in range(f + 1)]
-            for lo, hi in ([(0, f), (f, f + 1)] if (c in SPLIT0 if first else f == 4 and c in SPLIT) else [(0, f + 1)]):
+            for lo, hi in ([(0, 2), (2, f + 1)] if cut else [(0, f), (f, f + 1)] if first and c in SPLIT0 else [(0, f + 1)]):
                 v = T.TT[:, b + 64 * lo:b + 64 * hi]
                 ts(v, v, 256.0, A.min, -256.0, A.max, tk[lo:hi], tk[lo:hi], k=0.5)
-            for s in range(f + 1):
-                for t in range(s + 1):
+            for t in range(f + 1):
+                for s in range(t, f + 1):
                     m, mk = wd(s, t)
                     mm(dreg(c, f, s), m, T.TT[:, b + 64 * t:b + 64 * t + 64], False, s == f and t == s and FLOOR[c] in "AV", [mk, tk[t]], [dk])
-            x0 = T.X[:, b:b + 64 * f:f]
-            if FLOOR[c] in "PQ":
+            src, r, x = T.X[:, b:b + nn], [xk], []
+            if FLOOR[c] == "P":
                 mm(d[:, 0:nn], I1, T.MP[:, 0:nn], False, False, ["I1", "MP"], [dk])
                 mm(d[:, 0:nn], I1, T.MP[:, 320:320 + nn], False, True, ["I1", "MN"], [dk])
-                zc, x0 = T.ZC[:, 64 * c:64 * c + 64], d[:, 0:64 * f:f]
-                if FLOOR[c] == "Q":
-                    ts(zc, d[:, 64 * f:nn], T.wc[:, 23 + f:24 + f], A.mult, r=["wch"], w=["ZC%d" % c], x=[dk])
-                else:
-                    act(zc, d[:, 64 * f:nn], scale=T.wc[:, 23 + f:24 + f], r=["wch"], w=["ZC%d" % c], x=[dk])
-                tt(x0, x0, zc, A.add, ["ZC%d" % c], [], [dk])
-                add("v", lambda c=c, d=d: g.vector.tensor_tensor_scan(dl[:, 64 * f * c:64 * f * (c + 1)], T["PAT%d" % f][:, :],
-                                                                      d[:, 0:64 * f], 1536.0, A.mult, A.add),
-                    ["PAT%d_%d" % (f, j) for j in range(f)], ["dl%d_%d" % (k, c)], [dk], cost=0.05 + 64 * f * CYC)
-                for i, cs in enumerate(SENDS):
-                    if cs[-1] == c:
-                        send(m0 + i, ["dl%d_%d" % (k, q) for q in cs])
-                continue
-            if FLOOR[c] == "H":
+                src, r, x = d[:, 0:nn], [], [dk]
+            elif FLOOR[c] == "H":
                 mm(d[:, 0:nn], I1, T.MP[:, 0:nn], False, True, ["I1", "MP"], [dk])
-                act(T.X[:, b:b + nn], d[:, 0:nn], bias=-MAG, w=[xk], x=[dk])
-                act(d[:, 320:384], d[:, 64 * f:nn], bias=T.wc[:, 27 + f:28 + f], scale=T.wc[:, 23 + f:24 + f], r=["wch", "wcm"], x=[dk])
-                tt(x0, x0, d[:, 320:384], A.add, [xk], [xk], [dk])
+                act(src, d[:, 0:nn], bias=-MAG, w=[xk], x=[dk])
             elif FLOOR[c] == "A":
                 act(T.V[:, b:b + nn], d[:, 0:nn], bias=MAG, w=["V%d" % c], x=[dk])
-                act(d[:, 320:384], T.V[:, b + 64 * f:b + nn], bias=T.wc[:, 27 + f:28 + f], scale=T.wc[:, 23 + f:24 + f],
-                    r=["V%d" % c, "wch", "wcm"], x=[dk])
-                act(T.X[:, b:b + nn], T.V[:, b:b + nn], bias=-MAG, r=["V%d" % c], w=[xk])
-                tt(x0, x0, d[:, 320:384], A.add, [xk], [xk], [dk])
+                act(src, T.V[:, b:b + nn], bias=-MAG, r=["V%d" % c], w=[xk])
             else:
-                ts(T.X[:, b:b + nn], d[:, 0:nn], MAG, A.add, -MAG, A.add, w=[xk], x=[dk])
-                ts(d[:, 320:384], T.X[:, b + 64 * f:b + nn], T.wc[:, 23 + f:24 + f], A.mult, r=[xk, "wch"], x=[dk])
-                tt(x0, x0, d[:, 320:384], A.add, [xk], [xk], [dk])
-            add("v", lambda c=c, b=b: g.vector.tensor_tensor_scan(dl[:, 64 * f * c:64 * f * (c + 1)], T["PAT%d" % f][:, :],
-                                                                  T.X[:, b:b + 64 * f], 1536.0, A.mult, A.add),
-                [xk] + ["PAT%d_%d" % (f, j) for j in range(f)], ["dl%d_%d" % (k, c)], cost=0.05 + 64 * f * CYC)
+                ts(src, d[:, 0:nn], MAG, A.add, -MAG, A.add, w=[xk], x=[dk])
+            add("v", lambda c=c, src=src: g.vector.tensor_tensor_scan(dl[:, nn * c:nn * (c + 1)], T["PAT%d" % f][:, :], src, 1536.0, A.mult, A.add),
+                r + ["PAT%d_%d" % (f, j) for j in range(f + 1)], ["dl%d_%d" % (k, c)], x, cost=0.05 + nn * CYC)
             for i, cs in enumerate(SENDS):
                 if cs[-1] == c:
                     send(m0 + i, ["dl%d_%d" % (k, q) for q in cs])
         for c in range(NC):
-            df = T.DF[:, 64 * c:64 * c + 64] if f == 4 else T.S3[:, 256 * (k + 1) + 64 * c:256 * (k + 1) + 64 * c + 64]
-            dfk = "DF%d" % c if f == 4 else "S3_%d%d" % (k, c)
-            if FLOOR[c] in "PQ":
-                ts(df, T["d%d" % c][:, 64 * f:nn], 1536.0 - 15.0 / 32, A.add, w=[dfk], x=["d%d" % c])
-            else:
-                ts(df, T.X[:, 320 * c + 64 * f:320 * c + nn], 1536.0 - 15.0 / 32, A.add, r=["X%d" % c], w=[dfk])
-            for s in range(f):
-                mm(reg(hb(c), c, s), I1, dl[:, 64 * f * c + f - 1 - s:64 * f * (c + 1):f], c % 2 == 0 and s == 0, c % 2 == 1 and s == 3,
+            for s in range(4):
+                mm(reg(hb(c), c, s), I1, dl[:, nn * c + f - s:nn * (c + 1):f + 1], c % 2 == 0 and s == 0, c % 2 == 1 and s == 3,
                    ["I1", "dl%d_%d" % (k, c)], [hb(c)])
-            if f == 3:
-                mm(reg(hb(c), c, 3), I1, df, False, c % 2 == 1, ["I1", dfk], [hb(c)])
             if c % 2 == 1:
                 h = c // 2
                 after = GATHER_AF if k == 5 else GATHER_A0 if k == 2 else GATHER_A
@@ -653,7 +617,7 @@ def rank_program(g, core, T, topo):
                         tt(T.RH[:, a0:a1], ph, wh, A.add, hk, ["RH%d" % q for q in cs], ["ph%d" % h])
                         act(wh, T.RH[:, a0:a1], r=["RH%d" % q for q in cs], w=hk)
         if f == 4:
-            tt(T.H4[:, :], T.H4[:, :], T.DF[:, :], A.add, ["H4"] + ["DF%d" % c for c in range(NC)], ["H4"])
+            tt(T.H4[:, :], T.H4[:, :], dl[:, 0:1280:5], A.add, ["H4"] + ["dl%d_%d" % (k, c) for c in range(NC)], ["H4"])
         idle()
         if not last:
             for c in range(NC):
@@ -661,11 +625,11 @@ def rank_program(g, core, T, topo):
         for i, cs in enumerate(SENDS):
             arrive(m0 + i, ["ld%d_%d" % (k, c) for c in cs])
             for c in cs:
-                for s in range(f):
-                    mm(reg(ab(c), c, s), I1, ld[:, 64 * f * c + f - 1 - s:64 * f * (c + 1):f], s == 0, s == f - 1,
+                for s in range(4):
+                    mm(reg(ab(c), c, s), I1, ld[:, nn * c + f - s:nn * (c + 1):f + 1], s == 0, s == 3,
                        ["I1", "ld%d_%d" % (k, c)], [ab(c)])
-                wa = W[:, 1024 + 256 * c:1024 + 256 * c + 64 * f]
-                tt(wa, wa, reg(ab(c), c, 0, f), A.add, [AK[c]], [AK[c]], [ab(c)])
+                wa = W[:, 1024 + 256 * c:1024 + 256 * c + 256]
+                tt(wa, wa, reg(ab(c), c, 0, 4), A.add, [AK[c]], [AK[c]], [ab(c)])
         marks.append(len(ops) - 1)
 
     def stakes(cs):
@@ -677,6 +641,7 @@ def rank_program(g, core, T, topo):
     z3, z3k = part1(3)
 
     def idle0():
+        new_rating([(128 * h, 128 * h + 128, T.l0[:, 384 * h + 256:384 * h + 384]) for h in range(2)], ["l0_0", "l0_1"], "d3", None, None)
         node_numbers(3, z3, z3k)
         ts(si(5, 16), z3, 128.0, A.add, r=[z3k], w=["sa5"])
         act(T.aw[:, 0:16], z3, F.Sigmoid, bias=-1856.0, scale=2.0, r=[z3k, HK[3]], w=["aw"], more=1.3)
@@ -685,22 +650,24 @@ def rank_program(g, core, T, topo):
         for j in (3, 6, 8, 9):
             diag(j)
         const(4, 2, T.wc[:, 18:19], "d0", "d1")
+        const(7, 0, T.wc[:, 16:17], "d2", "d3")
+        const(8, 1, T.wc[:, 17:18], "d2", "d3")
 
-    S3K = ["N3"] + ["S3_%d%d" % (k, c) for k in range(3) for c in range(NC)]
+    S3K = ["N3"] + ["dl%d_%d" % (k, c) for k in range(3) for c in range(NC)]
+    S3P = [T.S3[:, :]] + [T["dl%d" % k][:, 0:1024:4] for k in range(3)]
 
     def idle1():
-        send(2 + 2 * len(SENDS), S3K[:9])
         lookup_gather(16, 48, "d2")
         lookup_finish(16, 48, "d2")
-        const(5, 3, BK, "d0", "d1")
-        const(6, 4, B0, "d0", "d1")
+        cp(T.ZI[:, 3:64:4], T.Z[:, 48:64], ["Z48"], ["ZI3"])
+        const(5, 3, T.wc[:, 19:20], "d0", "d1")
+        const(6, 4, BK, "d0", "d1")
 
     def idle2():
-        send(3 + 3 * len(SENDS), S3K[9:])
         for h in range(4):
-            mm(T.d2[:, 0:256], I1, T.S3[:, 256 * h:256 * h + 256], h == 0, h == 3, ["I1"] + S3K, ["d2"])
+            mm(T.d2[:, 0:256], I1, S3P[h], h == 0, h == 3, ["I1"] + S3K, ["d2"])
         act(T.ME[:, :], T.d2[:, 0:256], w=MEK, x=["d2"])
-        new_rating([(0, 256, T.S3[:, 256 * h:256 * h + 256]) for h in range(4)], S3K, "d3", T.H4[:, :], "H4")
+        new_rating([(0, 256, S3P[h]) for h in range(4)], S3K, "d3", T.H4[:, :], "H4")
         pattern(4)
 
     sweep(0, idle0)

@@ -6,89 +6,62 @@ MAG1 = float(3 * 2 ** 22)
 KOFF = 1535.5
 ETA = 2.0 ** -22
 BIGV = 131072.0
-SENDS = [[0], [1], [2], [3]]
-VIA = [False, False, False, False]
-VIA0 = [False, False]
-FLOOR = "PHHP"
-GATHER_A, GATHER_A0, GATHER_AF = [1, 2, 3], [0, 1, 2, 3], [1]
-SPLIT, SPLIT0 = [0], [0, 1, 2, 3]
-SUM_V = [3]
-CYC, PCYC, PFIX, RLAT, RATE, SYNC = 0.0009, 0.00065, 0.0, 2.0, 100e3, 0.09
+HOME, AWAY, WEND = 8, 8 + 1280, 8 + 1280 + 1024
+INIT = [(0, 512), (512, 768)]
+PARTS = {3: [[0, 1, 2, 3]], 4: [[0, 1, 2, 3]]}
+NEWS = [[0, 1], [2, 3]]
+GATHER_A, GATHER_A0, GATHER_AF = [1, 2, 3], [0, 1, 2, 3], [1, 2]
+SPLIT = [0]
+SUM_S = [3]
+SUM_V = [2]
+ROWS_V = [1, 2, 3]
+FLOOR = ["PPPP", "PPPP", "PPPP", "PPPP", "PPPP", "PPPP"]
+CYC, PCYC, PFIX, RLAT, RATE, SYNC = 0.0009, 0.00066, 0.0, 2.0, 200e3, 0.09
 
 SCRATCH = {
     "r0i": ("sbuf", [128, 768], "int32"), "oppi": ("sbuf", [128, 48], "int32"), "mub": ("sbuf", [128, 8], "bfloat16"),
     "ocb": ("sbuf", [128, 1280], "bfloat16"), "stb": ("sbuf", [128, 1280], "bfloat16"), "stc": ("sbuf", [128, 1280], "bfloat16"),
     "r16": ("sbuf", [128, 768], "float16"), "l0": ("sbuf", [128, 768], "float16"),
-    "W": ("sbuf", [128, 2056], "float32"), "H4": ("sbuf", [128, 256], "float32"), "ME": ("sbuf", [128, 256], "float32"),
+    "W": ("sbuf", [128, WEND], "float32"), "ME": ("sbuf", [128, 256], "float32"),
     "tb": ("sbuf", [128, 128], "bfloat16"), "io2": ("sbuf", [128, 144], "bfloat16"), "kcol": ("sbuf", [128, 4], "int32"),
     "zs0": ("sbuf", [128, 48], "int32"), "zs": ("sbuf", [128, 48], "int32"), "k15": ("sbuf", [128, 4], "int32"),
-    "kf": ("sbuf", [128, 8], "float32"), "PL": ("sbuf", [128, 4], "uint16"),
+    "kf": ("sbuf", [128, 8], "float32"),
     "TM": ("sbuf", [128, 2048], "bfloat16"), "BM": ("sbuf", [128, 144], "bfloat16"), "I1": ("sbuf", [128, 144], "bfloat16"),
-    "I2": ("sbuf", [128, 128], "bfloat16"), "I32": ("sbuf", [128, 128], "float32"), "WD": ("sbuf", [128, 11 * 128], "bfloat16"),
+    "I2": ("sbuf", [128, 128], "bfloat16"), "dn": ("sbuf", [128, 256], "float16"), "X": ("sbuf", [128, 1280], "float32"),
+    "I32": ("sbuf", [128, 128], "float32"), "NM": ("sbuf", [128, 128], "float32"),
+    "WD": ("sbuf", [128, 15 * 128], "bfloat16"), "WX": ("sbuf", [128, 9 * 128], "bfloat16"), "DG": ("sbuf", [128, 256], "bfloat16"),
     "wc": ("sbuf", [128, 32], "float32"), "PAT3": ("sbuf", [128, 256], "float32"), "PAT4": ("sbuf", [128, 320], "float32"),
-    "CH": ("sbuf", [128, 9 * 256], "bfloat16"), "CL": ("sbuf", [128, 9 * 256], "float16"),
+    "CF": ("sbuf", [128, 9 * 256], "float32"), "CH": ("sbuf", [128, 9 * 256], "bfloat16"), "CL": ("sbuf", [128, 9 * 256], "float16"),
     "o16": ("sbuf", [128, 48], "float16"), "aw": ("sbuf", [128, 48], "bfloat16"),
-    "LW": ("sbuf", [128, 768], "float32"), "REP": ("sbuf", [128, 768], "float16"),
-    "u1": ("sbuf", [128, 64], "uint16"), "OFF": ("sbuf", [128, 80], "uint16"), "CO": ("sbuf", [128, 64], "uint16"),
-    "WT": ("sbuf", [128, 48], "bfloat16"), "WI": ("sbuf", [128, 64], "bfloat16"), "UI": ("sbuf", [128, 64], "float32"),
-    "VI": ("sbuf", [128, 64], "float32"), "ZI": ("sbuf", [128, 64], "float32"), "SC": ("sbuf", [128, 128], "float32"),
-    "RH": ("sbuf", [128, 1024], "float32"), "MP": ("sbuf", [128, 640], "bfloat16"),
-    "OP": ("sbuf", [128, 64], "int32"), "OQ": ("sbuf", [128, 64], "int32"),
-    "sa": ("sbuf", [128, 48 * 24], "int32"), "sf": ("sbuf", [128, 48 * 18], "float32"), "Z": ("sbuf", [128, 96], "int32"),
+    "a16": ("sbuf", [128, 48], "float16"), "IN": ("sbuf", [128, 128], "bfloat16"), "LW": ("sbuf", [128, 776], "float32"), "REP": ("sbuf", [128, 768], "float16"),
+    "u1": ("sbuf", [128, 64], "uint16"), "OFF": ("sbuf", [128, 80], "uint16"), "OFN": ("sbuf", [128, 32], "uint16"),
+    "CO": ("sbuf", [128, 64], "uint16"),
+    "WT": ("sbuf", [128, 96], "bfloat16"), "WI": ("sbuf", [128, 48], "bfloat16"), "UI": ("sbuf", [128, 48], "float32"),
+    "VI": ("sbuf", [128, 48], "float32"), "ZI": ("sbuf", [128, 48], "float32"), "SC": ("sbuf", [128, 96], "float32"),
+    "ZZ": ("sbuf", [128, 64], "float32"), "ZB": ("sbuf", [128, 48], "float32"), "DZ": ("sbuf", [128, 64], "float32"),
+    "MZ": ("sbuf", [128, 64], "float32"), "EE": ("sbuf", [128, 32], "float32"),
+    "MP": ("sbuf", [128, 128], "bfloat16"), "OP": ("sbuf", [128, 48], "int32"),
+    "sa": ("sbuf", [128, 48 * 24], "int32"), "sf": ("sbuf", [128, 48 * 12], "float32"), "Z": ("sbuf", [128, 96], "int32"),
     "TK": ("sbuf", [128, 1280], "float32"), "DS": ("sbuf", [128, 1280], "float32"), "LT": ("sbuf", [128, 1536], "bfloat16"),
-    "TT": ("sbuf", [128, 1280], "bfloat16"), "V": ("sbuf", [128, 1280], "float32"), "X": ("sbuf", [128, 1280], "float32"),
-    "NT": ("sbuf", [128, 256], "float32"), "S3": ("sbuf", [128, 256], "float16"),
+    "TT": ("sbuf", [128, 1280], "bfloat16"), "TN": ("sbuf", [128, 256], "bfloat16"), "V": ("sbuf", [128, 1280], "float32"),
+    "NT": ("sbuf", [128, 256], "float32"), "RN": ("sbuf", [128, 256], "float32"), "RH": ("sbuf", [128, 1280], "float32"),
     "YR": ("sbuf", [128, 1280], "float32"), "YO": ("sbuf", [128, 32], "float32"), "Y": ("sbuf", [128, 256], "float32"),
-    "ph0": ("psum", [128, 512], "float32"), "ph1": ("psum", [128, 512], "float32"),
-    "pa0": ("psum", [128, 512], "float32"), "pa1": ("psum", [128, 512], "float32"),
-    "d0": ("psum", [128, 512], "float32"), "d1": ("psum", [128, 512], "float32"),
-    "d2": ("psum", [128, 512], "float32"), "d3": ("psum", [128, 512], "float32"),
 }
+for _k in ("h0", "h1", "h2", "h3", "d0", "d1", "d2", "dx"):
+    SCRATCH[_k] = ("psum", [128, 512], "float32")
 for _k in range(6):
     SCRATCH["dl%d" % _k] = ("sbuf", [128, 256 * (4 + _k // 3)], "float16")
     SCRATCH["ld%d" % _k] = ("sbuf", [128, 256 * (4 + _k // 3)], "float16")
-SEMAPHORES = ["sv", "sa", "sp", "sg", "ls"] + ["dm%d" % i for i in range(12)] + ["ar%d" % i for i in range(4 + 6 * NC)]
-
-
-def _mask(engines):
-    m = 0
-    for e in engines:
-        m |= 1 << e
-    return m
-
-
-def _helper(core, T, topo):
-    return [c for c in topo.cores_of(core) if topo.die(c) != topo.die(core) and T.rank_of(c) is None][0]
-
-
-def _messages():
-    ms = [("r16", "l0", 0, 384, VIA0[0]), ("r16", "l0", 384, 768, VIA0[1])]
-    for k in range(6):
-        f = 3 + k // 3
-        for i, cs in enumerate(SENDS):
-            ms.append(("dl%d" % k, "ld%d" % k, CP * (f + 1) * cs[0], CP * (f + 1) * (cs[-1] + 1), VIA[i]))
-    return ms
-
-
-def _helper_program(g, core, owner, T, topo):
-    n = len(T.cores)
-    prev = T.cores[(T.rank_of(owner) - 1) % n]
-    off = topo.engines(owner, prev)
-    near = [e for e in topo.engines(owner, core) if e not in off]
-    eng = topo.engines(core, prev)
-    rid, pid = topo.addr(prev, core)
-    sent = 0
-    for i, (src, dst, a, b, via) in enumerate(_messages()):
-        if via:
-            g.wait_ge(T.sem["ar%d" % i], len(near))
-            g.remote_dma(T[dst][:, a:b], T[dst][:, a:b], T.sem["ar%d" % i], T.sem.ls, pid, rid, _mask(eng))
-            sent += len(eng)
-    if sent:
-        g.wait_ge(T.sem.ls, sent)
-
+SEMAPHORES = ["sv", "sa", "sp", "sg", "ls", "l3"] + ["dm%d" % i for i in range(12)] + ["ar%d" % i for i in range(5 + 6 * NC)]
 
 KEPT = {}
-PASSES, SHAKES, SEED, SHAKE, FIRST = 6, 900, 1, 0.7, 3.5
+TWICE = [(3, 0), (3, 1)]
+WFIX = 0.45
+KEEP = 1
+DIRECT = 1
+CUT = 2
+PASSES, SHAKES, SWAPS, SEED, SHAKE, SLACK, FIRST = 6, 700, 3000, 1, 0.7, 0.0, 3.5
+PACES = [(0.87, 0.95), (1.25, 1.0), (0.95, 1.25)]
 
 
 def _order(ops, marks):
@@ -100,7 +73,7 @@ def _order(ops, marks):
             succ[j].append(i)
 
     def lag(a, b):
-        if ops[a]["q"] == "g" and ops[b]["q"] == "g":
+        if ops[a]["q"] == ops[b]["q"] and a not in ops[b]["hard"]:
             return 0.0
         return ops[a]["lat"] + (0.0 if ops[a]["q"] == "p" and ops[b]["q"] == "p" else SYNC)
 
@@ -139,7 +112,6 @@ def _order(ops, marks):
             best = (span, sorted(range(n), key=lambda i: (end[i] - ops[i]["cost"], i)), list(way))
         way = place(sorted(range(n), key=lambda i: (-end[i], -i)), True)
 
-
     def run(w):
         w = list(w)
         for i in range(n - 1, -1, -1):
@@ -170,30 +142,127 @@ def _order(ops, marks):
             w3, e3, t3 = run([new[i] if good[part[i]] else way[i] for i in range(n)])
             if t3[-1] < t[-1]:
                 way, end, t = w3, e3, t3
-    KEPT["span"] = t[-1]
-    return sorted(range(n), key=lambda i: (end[i] - ops[i]["cost"], i))
+    order = sorted(range(n), key=lambda i: (end[i] - ops[i]["cost"], i))
+
+    qs = [o["q"] for o in ops]
+    pl = [[(j, lag(j, i)) for j in pred[i]] for i in range(n)]
+    lat = [o["lat"] for o in ops]
+    costs = [[o["cost"] * p if o["q"] == "p" else 0.05 + (o["cost"] - 0.05) * v if o["q"] in "va" and o["cost"] < 1.2 and not o["lat"]
+              else o["cost"] for o in ops] for p, v in PACES]
+
+    def replay(seq, cost):
+        free, end, why, top, who = {}, [0.0] * n, [-1] * n, 0.0, 0
+        for i in seq:
+            t, w = 0.0, -1
+            for j, l in pl[i]:
+                e = end[j] + l
+                if e > t:
+                    t, w = e, j
+            q = qs[i]
+            if q != "r":
+                j = free.get(q, -1)
+                if j >= 0 and end[j] > t:
+                    t, w = end[j], j
+                free[q] = i
+            t += cost[i]
+            end[i], why[i] = t, w
+            if t + lat[i] > top:
+                top, who = t + lat[i], i
+        return top, why, who, end
+
+    def ahead(seq, p0, p1, cost, old):
+        end, free = list(old), {}
+        for p in range(p0 - 1, -1, -1):
+            free.setdefault(qs[seq[p]], end[seq[p]])
+            if len(free) == 6 or p < p0 - 300:
+                break
+        top = 0.0
+        for p in range(p0, p1 + 1):
+            i = seq[p]
+            q = qs[i]
+            t = free.get(q, 0.0) if q != "r" else 0.0
+            for j, l in pl[i]:
+                e = end[j] + l
+                if e > t:
+                    t = e
+            t += cost[i]
+            end[i] = free[q] = t
+            if t + lat[i] > top:
+                top = t + lat[i]
+        return top if p1 == n - 1 else t
+
+    def swaps(res):
+        found = []
+        for top, why, i, end in res:
+            while why[i] >= 0:
+                if qs[why[i]] == qs[i] and why[i] not in ops[i]["deps"]:
+                    found.append((why[i], i))
+                i = why[i]
+        return found
+
+    res = [replay(order, c) for c in costs]
+    now, moves = sum(r[0] for r in res), swaps(res)
+    best = (now, order, res)
+    for turn in range(SWAPS):
+        seed = (seed * 1103515245 + 12345) % 2147483648
+        a, b = moves[(seed >> 8) % len(moves)]
+        seed = (seed * 1103515245 + 12345) % 2147483648
+        pa, pb = order.index(a), order.index(b)
+        early = seed >> 20 & 1
+        for step in range((seed >> 12) % 4):
+            if early:
+                pa = max([p for p in range(max(0, pa - 40), pa) if qs[order[p]] == qs[a]] or [pa])
+            else:
+                pb = min([p for p in range(pb + 1, min(n, pb + 40)) if qs[order[p]] == qs[a]] or [pb])
+        mid = order[pa:pb + 1]
+        if early:
+            go = {b}
+            for i in reversed(mid):
+                if any(j in go for j in succ[i]):
+                    go.add(i)
+            mid = [i for i in mid if i in go] + [i for i in mid if i not in go]
+        else:
+            go = {a}
+            for i in mid:
+                if any(j in go for j in pred[i]):
+                    go.add(i)
+            mid = [i for i in mid if i not in go] + [i for i in mid if i in go]
+        new = order[:pa] + mid + order[pb + 1:]
+        slack = SLACK * (1.0 - turn / SWAPS) ** 2 + 1e-9
+        later = sorted(p for p in [order.index(m) for m in marks] if p > pb)
+        p1 = later[0] if later else n - 1
+        worse = 0.0
+        for c, x in zip(costs, res):
+            worse += ahead(new, pa, p1, c, x[3]) - (x[3][order[p1]] if later else x[0])
+            if worse > slack + 0.2:
+                break
+        if worse > slack:
+            continue
+        r = [replay(new, c) for c in costs]
+        if sum(x[0] for x in r) <= now + slack:
+            order, res, now = new, r, sum(x[0] for x in r)
+            moves = swaps(res)
+            if now < best[0]:
+                best = (now, order, res)
+    KEPT["span"] = best[2][0][0]
+    return best[1]
 
 
 def rank_program(g, core, T, topo):
     rank = T.rank_of(core)
     if rank is None:
-        for c in T.cores:
-            if _helper(c, T, topo) == core:
-                _helper_program(g, core, c, T, topo)
         return
     n = len(T.cores)
     prev, nxt = T.cores[(rank - 1) % n], T.cores[(rank + 1) % n]
-    helper = _helper(core, T, topo)
-    far = topo.engines(core, prev)
-    near = [e for e in topo.engines(core, helper) if e not in far]
-    msgs = _messages()
+    nfar, ncome = len(topo.engines(core, prev)), len(topo.engines(nxt, core))
+    rid, pid = topo.addr(prev, core)
 
     ops, lastw, readers, banks = [], {}, {}, {}
-    ndma, nsent, sent, marks = [0], [0], {}, []
+    ndma, nsent, sent, marks = [0], [0], [], []
 
     def add(q, fn, r=(), w=(), x=(), tok=None, cost=0.1, lat=0.0, after=()):
         i = len(ops)
-        deps = set(after)
+        deps = set()
         for k in r:
             if k in lastw:
                 deps.add(lastw[k])
@@ -202,7 +271,9 @@ def rank_program(g, core, T, topo):
                 deps.add(lastw[k])
             deps.update(readers.get(k, ()))
         for k in x:
-            deps.update(banks.setdefault(k, {}).values())
+            fills = q != "p" and (not w or w[0][:2] in ("XM", "CP", "PS", "PT"))
+            deps.update(j for e, j in banks.setdefault(k, {}).items() if e != q or fills)
+            after = list(after) + [j for e, j in banks[k].items() if e == q]
         for k in r:
             readers.setdefault(k, []).append(i)
         for k in w:
@@ -210,7 +281,7 @@ def rank_program(g, core, T, topo):
             readers[k] = []
         for k in x:
             banks[k][q] = i
-        ops.append({"q": q, "fn": fn, "deps": deps, "tok": tok, "cost": cost, "lat": lat})
+        ops.append({"q": q, "fn": fn, "hard": deps, "deps": deps | set(after), "tok": tok, "cost": cost, "lat": lat})
         return i
 
     def cy(out, k=1.0):
@@ -228,8 +299,8 @@ def rank_program(g, core, T, topo):
     def cp(out, in_, r=(), w=(), x=(), k=1.0):
         add("v", lambda: g.vector.tensor_copy(out, in_), r, w, x, cost=cy(out, k))
 
-    def ms(out, val, w):
-        add("v", lambda: g.vector.memset(out, val), (), w, cost=cy(out))
+    def ms(out, val, w, k=1.0):
+        add("v", lambda: g.vector.memset(out, val), (), w, cost=cy(out, k))
 
     def act(out, in_, func=F.Identity, bias=0.0, scale=1.0, r=(), w=(), x=(), more=0.0):
         add("a", lambda: g.scalar.activation(out, in_, func, bias=bias, scale=scale), r, w, x, cost=cy(out) + 0.03 + more)
@@ -237,11 +308,11 @@ def rank_program(g, core, T, topo):
     def mm(out, lhs, rhs, start, stop, r=(), x=(), k=1.0):
         add("p", lambda: g.tensor.matmul(out, lhs, rhs, start, stop), r, (), x, cost=PFIX + max(64, out.shape[1]) * k * PCYC)
 
-    def dma(q, out, in_, r=(), w=()):
+    def dma(q, out, in_, r=(), w=(), lat=2.2):
         s = "dm%d" % ndma[0]
         ndma[0] += 1
         eng = g.sync if q == "s" else g.scalar
-        add(q, lambda: eng.dma_start(out, in_), r, w, (), (s, 16, True), cost=0.1, lat=1.9 + out.shape[1] / 400)
+        add(q, lambda: eng.dma_start(out, in_), r, w, (), (s, 16, True), cost=0.1, lat=lat)
 
     def iota(out, pat, cm, key, small):
         if small:
@@ -249,34 +320,35 @@ def rank_program(g, core, T, topo):
         else:
             add("g", lambda: g.iota(out, pat, 0, cm), (), [key], cost=0.13 + 2 * out.shape[1] * CYC)
 
-    def send(i, keys):
-        src, dst, a, b, via = msgs[i]
-        to, eng = (helper, near) if via else (prev, far)
-        rid, pid = topo.addr(to, core)
-        nsent[0] += len(eng)
-        sent[i] = add("g", lambda: g.remote_dma(T[dst][:, a:b], T[src][:, a:b], T.sem["ar%d" % i], T.sem.ls, pid, rid, _mask(eng)),
-                      keys, (), (), ("ls", 0, False), cost=FIRST if i == 0 else 0.3 if via else max(0.3, (b - a) * 256 / RATE),
-                      lat=2 * RLAT + (b - a) * 512 / RATE if via else RLAT, after=[sent[i - 1]] if i else [])
+    def send(dst, src, keys, width, again=False):
+        i = len(sent)
+        local = "l3" if again else "ls"
+        if not again:
+            nsent[0] += nfar
+        sent.append(add("g", lambda: g.remote_dma(dst, src, T.sem["ar%d" % i], T.sem[local], pid, rid, topo.mask(core, prev)),
+                        keys, (), (), (local, nfar if again else 0, False), cost=FIRST if i == 0 else WFIX + width * 128 / RATE,
+                        lat=RLAT, after=sent[-1:]))
+        return i
 
     def arrive(i, keys):
-        sender = _helper(nxt, T, topo) if msgs[i][4] else nxt
-        add("r", None, (), keys, (), ("ar%d" % i, len(topo.engines(sender, core)), False), cost=0.0, after=[sent[i]])
+        add("r", None, (), keys, (), ("ar%d" % i, ncome, False), cost=0.0, after=[sent[i]])
 
-    W, win = T.W, T.W[:, 0:2056]
+    W = T.W
     HK = ["WH%d" % c for c in range(NC)]
     AK = ["WA%d" % c for c in range(NC)]
     MEK = ["ME%d" % c for c in range(NC)]
-    WIN = HK + AK + ["WB"]
+    WNK = ["WN%d_%d" % (f, c) for f in (3, 4) for c in range(NC)]
+    WIN = {3: (W[:, 0:AWAY + 768], HK + AK + WNK + ["WB"]), 4: (W[:, 0:WEND], HK + AK + WNK + ["WB", "WL"])}
+    HB = ["h0", "h1", "h2", "h3"]
+    DB = ["d0", "d1", "d2", "dx"]
     I1 = T.I1[:, 0:128]
+    MP, MN = T.MP[:, 0:64], T.MP[:, 64:128]
 
-    def hb(c):
-        return "ph%d" % (c // 2)
+    def wcols(base, c, lo, hi):
+        return W[:, base + 256 * lo + c:base + 256 * hi:4]
 
-    def ab(c):
-        return "pa%d" % (c // 2)
-
-    def reg(bank, c, s, m=1):
-        return T[bank][:, (c % 2) * 256 + 64 * s:(c % 2) * 256 + 64 * (s + m)]
+    def hreg(c, s, m=1):
+        return T[HB[c]][:, 64 * s:64 * (s + m)]
 
     def si(j, m=48):
         return T.sa[:, 48 * j:48 * j + m]
@@ -285,352 +357,441 @@ def rank_program(g, core, T, topo):
         return T.sf[:, 48 * j + o:48 * j + o + m]
 
     def wd(s, t):
-        j = 10 if s == t else [0, 4, 7, 9][s - t - 1] + t
-        return T.WD[:, 128 * j:128 * j + 128], "WD%d" % j
+        j = s * (s + 1) // 2 + t
+        return T.WD[:, 128 * j:128 * j + 128], ("WD%d" if t == s else "WR%d") % s
+
+    def wx(f, t):
+        j = 4 * (f - 3) + t
+        return T.WX[:, 128 * j:128 * j + 128], "WX%d" % f
+
+    def dg(f):
+        return T.DG[:, 128 * (f - 3):128 * (f - 2)], "DG%d" % f
+
+    def weights(s):
+        j = s * (s + 1) // 2
+        act(T.WD[:, 128 * (j + s):128 * (j + s + 1)], I1, scale=0.0625, r=["I1"], w=["WD%d" % s])
+        if s:
+            o, i, r = T.WD[:, 128 * j:128 * (j + s)], T.WD[:, 128 * (j - s):128 * j], ["WR%d" % (s - 1), "WD%d" % (s - 1), "wa"]
+            if s in ROWS_V:
+                ts(o, i, T.wc[:, s - 1:s], A.mult, r=r, w=["WR%d" % s], k=0.5)
+            else:
+                act(o, i, scale=T.wc[:, s - 1:s], r=r, w=["WR%d" % s])
+        if s >= 3 and not KEEP:
+            act(dg(s)[0], I1, scale=T.wc[:, 3 + s:4 + s], r=["I1", "wa"], w=[dg(s)[1]])
+            o, i, r = T.WX[:, 512 * (s - 3):512 * (s - 3) + 128 * (s + 1)], T.WD[:, 128 * j:128 * (j + s + 1)], ["WR%d" % s, "WD%d" % s, "wa"]
+            if s in ROWS_V:
+                ts(o, i, T.wc[:, 3 + s:4 + s], A.mult, r=r, w=["WX%d" % s], k=0.5)
+            else:
+                act(o, i, scale=T.wc[:, 3 + s:4 + s], r=r, w=["WX%d" % s])
 
     def lookup_list(src, rk, col, ck, m, c0, away, ak):
-        ts(si(0, m), src, 15, A.bitwise_and, r=[rk], w=["sa0"])
-        ts(si(1, m), src, 4, A.logical_shift_right, r=[rk], w=["sa1"])
-        ts(si(2, m), si(0, m), 48.0, A.mult, r=["sa0"], w=["sa2"])
-        ts(sfl(0, m), src, 1024.0, A.is_lt, 0.0625, A.mult, [rk], ["sf0"])
-        tt(si(3, m), si(2, m), si(1, m), A.add, ["sa2", "sa1"], ["sa3"])
-        ts(T.u1[:, c0:c0 + m], si(3, m), 767.0, A.min, r=["sa3"], w=["u1"])
-        tt(sfl(2, m), away, col, A.mult, [ak, ck], ["sf2"])
+        ts(T.u1[:, c0:c0 + m], src, 768.0, A.min, r=[rk], w=["u1"])
+        tt(T.a16[:, 0:m], away, col, A.mult, [ak, ck], ["a16"])
 
     def lookup_gather(m, c0, bank):
-        for j in range(m // 16):
-            cp(T.REP[:, 256 * j:256 * j + 256], T.LW[:, 0:768].indirect(T.u1[:, c0 + 16 * j:c0 + 16 * j + 16]),
-               ["LW0", "LW1", "u1"], ["REP%d" % j], k=1.5)
+        cp(T.REP[:, 0:16 * m], T.LW[:, :].indirect(T.u1[:, c0:c0 + m]), ["LW0", "LW1", "LWZ", "u1"], ["REP"], k=1.5)
+        mm(T[bank][:, 0:m], I1, T.a16[:, 0:m], True, False, ["I1", "a16"], [bank])
         for r in range(16):
-            mm(T[bank][:, 0:m], T.BM[:, 15 - r:143 - r], T.REP[:, r:16 * m:16], r == 0, r == 15,
-               ["BM"] + ["REP%d" % j for j in range(m // 16)], [bank])
+            mm(T[bank][:, 0:m], T.BM[:, 15 - r:143 - r], T.REP[:, r:16 * m:16], False, r == 15, ["BM", "REP"], [bank])
 
     def lookup_finish(m, c0, bank):
-        tt(sfl(3, m), T[bank][:, 0:m], sfl(0, m), A.mult, ["sf0"], ["sf3"], [bank])
-        tt(si(4, m), sfl(3, m), sfl(2, m), A.add, ["sf3", "sf2"], ["sa4"])
-        ts(T.Z[:, c0:c0 + m], si(4, m), 0x73F, A.bitwise_and, r=["sa4"], w=["Z%d" % c0])
+        cp(si(4, m), T[bank][:, 0:m], w=["sa4"], x=[bank])
+        ts(T.Z[:, c0:c0 + m], si(4, m), 0x4FF, A.bitwise_and, r=["sa4"], w=["Z%d" % c0])
         tt(sfl(4, m), T.Z[:, c0:c0 + m], T.zs[:, 0:m], A.is_equal, ["Z%d" % c0, "zs"], ["sf4"])
-        ts(sfl(5, m), sfl(4, m), 2048.0, A.mult, r=["sf4"], w=["sf5"])
-        tt(sfl(6, m), sfl(5, m), si(4, m), A.max, ["sf5", "sa4"], ["sf6"])
+        ts(sfl(5, m), sfl(4, m), -4096.0, A.mult, float(HOME), A.add, ["sf4"], ["sf5"])
+        tt(sfl(6, m), sfl(5, m), si(4, m), A.add, ["sf5", "sa4"], ["sf6"])
         cp(T.CO[:, c0:c0 + m], sfl(6, m), ["sf6"], ["CO%d" % c0])
 
-    def const(j, s, bias, bank, tmp):
-        f = 3 if j < 4 else 4
-        o = 1024 * (f - 3)
-        cs = slice(o + f - s, o + 256 * (f + 1), f + 1)
+    def player_columns(m, c0):
+        ts(sfl(9, m), T.Z[:, c0:c0 + m], 1024.0, A.is_ge, 256.0, A.mult, ["Z%d" % c0], ["sf9"])
+        tt(T.ZZ[:, c0:c0 + m], sfl(9, m), T.Z[:, c0:c0 + m], A.add, ["sf9", "Z%d" % c0], ["ZZ%d" % c0])
+
+    BK = KOFF - 15.0 / 512
+
+    def cplace(f, s, c0=0, c1=NC):
+        o, m = 1024 * (f - 3), f + KEEP
+        if s == m:
+            return slice(o + 256 * f + 64 * c0, o + 256 * f + 64 * c1)
+        return slice(o + 64 * m * c0 + m - 1 - s, o + 64 * m * c1, m)
+
+    def ckey(f, s):
+        return "%d_%d" % (f, s)
+
+    def const_again(s):
+        if DIRECT:
+            act(T.CF[:, cplace(4, s)], T.CF[:, cplace(3, s)], r=["CH" + ckey(3, s)], w=["CH" + ckey(4, s)])
+            return
+        act(T.CH[:, cplace(4, s)], T.CH[:, cplace(3, s)], r=["CH" + ckey(3, s)], w=["CH" + ckey(4, s)])
+        cp(T.CL[:, cplace(4, s)], T.CL[:, cplace(3, s)], ["CL" + ckey(3, s)], ["CL" + ckey(4, s)], k=0.5)
+
+    def const(f, s, bank):
+        bias = BK if s == f else T.wc[:, 16 + s:17 + s]
+        cs, p, key = cplace(f, s), T[bank][:, 0:256], ckey(f, s)
         for t in range(s + 1):
             m, k = wd(s, t)
-            mm(T[bank][:, 0:256], m, T.ocb[:, 256 * t:256 * t + 256], t == 0, t == s, [k, "ocb"], [bank])
-        act(T.CH[:, cs], T[bank][:, 0:256], bias=bias, r=["wc"], w=["CH%d" % j], x=[bank])
-        act(T[tmp][:, 0:256], T[bank][:, 0:256], bias=bias, r=["wc"], x=[bank, tmp])
-        tt(T.CL[:, cs], T[tmp][:, 0:256], T.CH[:, cs], A.subtract, ["CH%d" % j], ["CL%d" % j], [tmp])
-
-    CV = {3: [0, 1, 2, 3], 4: [7, 8, 4, 5, 6]}
-    BK, B0 = KOFF - 15.0 / 512, -15.0 / 512
+            mm(p, m, T.ocb[:, 256 * t:256 * t + 256], t == 0, t == s, [k, "ocb"], [bank])
+        if DIRECT:
+            act(T.CF[:, cs], p, bias=bias, r=["wk"], w=["CH" + key], x=[bank])
+            return
+        if (f, s) in TWICE:
+            act(T.CH[:, cs], p, bias=bias, r=["wk"], w=["CH" + key], x=[bank])
+            p = T[bank][:, 256:512]
+            for t in range(s + 1):
+                m, k = wd(s, t)
+                mm(p, m, T.ocb[:, 256 * t:256 * t + 256], t == 0, False, [k, "ocb"], [bank])
+            mm(p, T.IN[:, :], T.CH[:, cs], False, True, ["IN", "CH" + key], [bank])
+            ts(T.CL[:, cs], p, bias, A.add, r=["wk"], w=["CL" + key], x=[bank])
+            return
+        act(p, p, bias=bias, r=["wk"], w=["CP" + key], x=[bank])
+        act(T.CH[:, cs], p, r=["CP" + key], w=["CH" + key], x=[bank])
+        tt(T.CL[:, cs], p, T.CH[:, cs], A.subtract, ["CH" + key], ["CL" + key], [bank])
 
     def dreg(c, f, s):
-        d = T["d%d" % c]
-        return d[:, f - s:64 * (f + 1):f + 1]
+        m = f + KEEP
+        return T[DB[c]][:, m - 1 - s:64 * m:m] if s < m else T[DB[c]][:, 64 * f:64 * f + 64]
 
-    def preload(c, f):
-        o, d = 1024 * (f - 3), T["d%d" % c]
-        for out, a0, m, js in ((d[:, 0:64 * f + 64], o + (64 * f + 64) * c, 64 * f + 64, CV[f]),):
-            mm(out, I1, T.CH[:, a0:a0 + m], m > 64, False, ["I1"] + ["CH%d" % j for j in js], ["d%d" % c])
-            mm(out, I1, T.CL[:, a0:a0 + m], False, False, ["I1"] + ["CL%d" % j for j in js], ["d%d" % c])
-
-    def gather(out, ok, c, f, part, scalar):
-        b = 320 * c
-        lo = f if part == "new" else 2 if part == "high" else 0
-        hi = 2 if part == "low" else min(4, f if part == "old" else f + 1)
-        if lo < hi:
-            r = WIN + ["OFF"] + (["OFF3_%d" % c] if hi == 4 else [])
-            q, w = win.indirect(T.OFF[:, 16 * c + 4 * lo:16 * c + 4 * hi]), [ok + "%d_%d" % (c, s) for s in range(lo, hi)]
-            if c in scalar and part != "new":
-                qb = T.V[:, b + 64 * lo:b + 64 * hi]
-                act(qb, q, r=r, w=["V%d" % c], more=32 * (hi - lo) * CYC)
-                tt(out[:, b + 64 * lo:b + 64 * hi], qb, reg(hb(c), c, lo, hi - lo), A.subtract, ["V%d" % c], w, [hb(c)])
-            elif part == "new":
-                tt(out[:, b + 64 * lo:b + 64 * hi], win.indirect(T.OFF[:, 64 + 4 * c:68 + 4 * c]), T.S3[:, 64 * c:64 * c + 64],
-                   A.subtract, WIN + ["OFF4", "N3"], w, k=1.5)
-            else:
-                tt(out[:, b + 64 * lo:b + 64 * hi], q, T.RH[:, 256 * c + 64 * lo:256 * c + 64 * hi], A.subtract, r + ["RH%d" % c], w, k=1.5)
-        if f == 4 and part not in ("old", "low"):
-            tt(out[:, b + 256:b + 320], win.indirect(T.OFF[:, 64 + 4 * c:68 + 4 * c]), T.H4[:, 64 * c:64 * c + 64],
-               A.subtract, WIN + ["OFF4", "H4"], [ok + "%d_4" % c], k=1.5)
-
-    def new_rating(parts, keys, bank, out, ok):
-        lhs = [(I1, "I1"), (T.I1[:, 16:144], "I1"), (T.I2[:, :], "I2")]
-        jobs = [(m, k, p) for p in parts for m, k in lhs]
-        for i, (m, k, (o0, o1, rhs)) in enumerate(jobs):
-            mm(T[bank][:, o0:o1], m, rhs, i == 0, i == len(jobs) - 1, [k] + keys, [bank])
-        act(T.NT[:, :], T[bank][:, 0:256], bias=-0.25, scale=0.5, w=["NT"], x=[bank])
-        if out is not None:
-            ts(out, T.NT[:, :], MAG1, A.add, -MAG1, A.add, ["NT"], [ok])
+    def preload(c, k):
+        f = 3 + k // 3
+        m = 64 * (f + KEEP)
+        a0 = 1024 * (f - 3) + m * c
+        if DIRECT:
+            mm(T[DB[c]][:, 0:m], I1, T.ocb[:, 0:m], True, False, ["I1", "ocb"], [DB[c]])
+            act(T[DB[c]][:, 0:m], T.CF[:, a0:a0 + m], r=["CH" + ckey(f, s) for s in range(f + KEEP)], x=[DB[c]])
+            if FLOOR[k][c] == "H":
+                mm(dreg(c, f, 0), I1, MP, False, False, ["I1", "MP"], [DB[c]])
             return
-        act(T.ME[:, :], T.NT[:, :], bias=MAG1, r=["NT"], w=MEK)
-        for c in range(NC):
-            act(W[:, 1024 + 256 * c + 192:1024 + 256 * c + 256], T.ME[:, 64 * c:64 * c + 64], bias=-MAG1, r=MEK, w=[AK[c]])
+        mm(T[DB[c]][:, 0:m], I1, T.CH[:, a0:a0 + m], True, False, ["I1"] + ["CH" + ckey(f, s) for s in range(f + KEEP)], [DB[c]])
+        mm(T[DB[c]][:, 0:m], I1, T.CL[:, a0:a0 + m], False, False, ["I1"] + ["CL" + ckey(f, s) for s in range(f + KEEP)], [DB[c]])
+        if FLOOR[k][c] != "P" and not KEEP:
+            cs = cplace(f, f, c, c + 1)
+            mm(dreg(c, f, f), I1, T.CH[:, cs], False, False, ["I1", "CH" + ckey(f, f)], [DB[c]])
+            mm(dreg(c, f, f), I1, T.CL[:, cs], False, False, ["I1", "CL" + ckey(f, f)], [DB[c]])
+        if FLOOR[k][c] == "H":
+            mm(dreg(c, f, 0), I1, MP, False, False, ["I1", "MP"], [DB[c]])
 
-    def away_copy(c, m, scalar):
-        o = W[:, 1024 + 256 * c:1024 + 256 * c + 64 * m]
+    def gather(out, ok, c, lo, hi, wf, scalar):
+        b = 320 * c
+        win, wk = WIN[wf]
+        r = wk + ["OFF"] + ["OFF%d_%d" % (s, c) for s in range(max(lo, 3), hi)]
+        q, w = win.indirect(T.OFF[:, 20 * c + 4 * lo:20 * c + 4 * hi]), [ok + "%d_%d" % (c, s) for s in range(lo, hi)]
+        o = out[:, b + 64 * lo:b + 64 * hi]
         if scalar:
-            act(o, reg(ab(c), c, 0, m), w=[AK[c]], x=[ab(c)])
+            qb = T.V[:, b + 64 * lo:b + 64 * hi]
+            act(qb, q, r=r, w=["V%d_%d" % (c, lo)], more=32 * (hi - lo) * CYC)
+            tt(o, qb, hreg(c, lo, hi - lo), A.subtract, ["V%d_%d" % (c, lo)], w, [HB[c]])
         else:
-            cp(o, reg(ab(c), c, 0, m), w=[AK[c]], x=[ab(c)])
+            tt(o, q, T.RH[:, b + 64 * lo:b + 64 * hi], A.subtract, r + ["RH%d" % c], w, k=1.5)
 
-    dma("s", T.r0i[:, 0:384], T.r0[:, 0:384], w=["r0a"])
-    dma("a", T.r0i[:, 384:768], T.r0[:, 384:768], w=["r0b"])
-    dma("s", T.oppi[:, :], T.opp[:, :], w=["opp"])
-    dma("a", T.mub[:, :], T.mu[:, :], w=["mu"])
-    dma("s", T.ocb[:, :], T.oc[:, :], w=["ocb"])
-    dma("s", T.stb[:, :], T.stake[:, :], w=["stb"])
+    def limit(v, keys):
+        ts(v, v, 256.0, A.min, -256.0, A.max, keys, keys, k=0.5)
+
+    def half_sum(bank, f):
+        act(T.NT[:, :], T[bank][:, 0:256], bias=-0.25, scale=0.5, w=["NT"], x=[bank])
+        ts(T.RN[:, :], T.NT[:, :], MAG1, A.add, -MAG1, A.add, ["NT"], ["RN"])
+
+    def newest(f):
+        for c in range(NC):
+            act(T.ME[:, 64 * c:64 * c + 64], wcols(HOME, c, f - 1, f), r=[HK[c]], w=[MEK[c]])
+
+    NEXT = [(I1, "I1"), (T.I1[:, 16:144], "I1"), (T.I2[:, :], "I2")]
+
+    dma("s", T.r0i[:, 0:256], T.r0[:, 0:256], w=["r0_0"], lat=2.2)
+    dma("a", T.oppi[:, :], T.opp[:, :], w=["opp"], lat=2.3)
+    dma("s", T.r0i[:, 256:768], T.r0[:, 256:768], w=["r0_1", "r0_2"], lat=2.8)
+    dma("a", T.mub[:, :], T.mu[:, :], w=["mu"], lat=2.4)
+    dma("s", T.ocb[:, :], T.oc[:, :], w=["ocb"], lat=3.5)
+    dma("s", T.stb[:, :], T.stake[:, :], w=["stb"], lat=4.2)
     iota(T.tb[:, :], [[-16, 8], [0, 16]], 1, "tb", True)
     iota(T.io2[:, :], [[1, 144]], -1, "io2", True)
     iota(T.kcol[:, :], [[0, 4]], 1, "kcol", False)
-    iota(T.zs0[:, :], [[0, 3], [256, 4], [16, 4]], 0, "zs0", False)
-    act(W[:, 2048:2056], T.tb[:, 0:8], scale=0.0, bias=BIGV, r=["tb"], w=["WB"])
-    ms(T.OP[:, 48:64], 0, ["OPz"])
-    ms(T.PAT3[:, 0:256:4], ETA, ["PAT3_0"])
-    ms(T.PAT4[:, 0:320:5], ETA, ["PAT4_0"])
-    for c in range(NC):
-        act(W[:, 1024 + 256 * c + 192:1024 + 256 * c + 256], T.tb[:, 0:64], scale=0.0, r=["tb"], w=[AK[c]])
+    iota(T.zs0[:, :], [[0, 3], [1, 4], [64, 4]], 0, "zs0", False)
+    ms(W[:, HOME + 768:AWAY], 0.0, WNK)
+    for f in (3, 4):
+        ms(T["PAT%d" % f][:, 0:64 * (f + KEEP):f + KEEP], ETA, ["PAT%d_0" % f])
+    act(W[:, 0:HOME], T.tb[:, 0:HOME], scale=0.0, bias=BIGV, r=["tb"], w=["WB"])
+    act(MP, T.tb[:, 0:64], scale=0.0, bias=MAG, r=["tb"], w=["MP"])
+    act(MN, T.tb[:, 0:64], scale=0.0, bias=-MAG, r=["tb"], w=["MN"])
+    act(T.WI[:, 0:48:3], T.tb[:, 0:16], scale=0.0, bias=1.0, r=["tb"], w=["WI0"])
     for r in range(16):
         ts(T.TM[:, 128 * r:128 * r + 128], T.tb[:, :], float(r), A.is_equal, r=["tb"], w=["TM%d" % r], k=0.5)
-    act(T.MP[:, 0:320], T.TM[:, 0:320], scale=0.0, bias=MAG, r=["TM0", "TM1", "TM2"], w=["MP"])
-    act(T.MP[:, 320:640], T.TM[:, 0:320], scale=0.0, bias=-MAG, r=["TM0", "TM1", "TM2"], w=["MN"])
     ts(T.I1[:, :], T.io2[:, :], 0.0, A.is_equal, r=["io2"], w=["I1"], k=0.5)
+    if not DIRECT:
+        act(T.IN[:, :], I1, scale=-1.0, r=["I1"], w=["IN"])
+    act(T.LW[:, 768:776], T.tb[:, 0:8], scale=0.0, r=["tb"], w=["LWZ"])
+    for i, s in enumerate((0, 2)):
+        cp(T.r16[:, 256 * i:256 * i + 256], T.r0i[:, 256 * s:256 * s + 256], ["r0_%d" % s], ["r16_%d" % i])
+    for c in range(NC):
+        cp(T.r16[:, 512 + c:768:4], T.r0i[:, 256 + 64 * c:320 + 64 * c], ["r0_1"], ["r16_2%d" % c])
+    R16 = [["r16_0"], ["r16_1"], ["r16_2%d" % c for c in range(NC)]]
+    first_msgs = [send(T.l0[:, a:b], T.r16[:, a:b], [k for s in range(a // 256, b // 256) for k in R16[s]], 2 * (b - a)) for a, b in INIT]
+    src = T.oppi[:, :]
+    ts(si(12), src, 63, A.bitwise_and, r=["opp"], w=["sa12"])
+    ts(si(13), src, 6, A.logical_shift_right, 3, A.bitwise_and, ["opp"], ["sa13"])
+    ts(si(15), src, 0x700, A.bitwise_and, r=["opp"], w=["sa15"])
+    ts(si(14), si(12), 4.0, A.mult, r=["sa12"], w=["sa14"])
+    tt(si(16), si(14), si(13), A.add, ["sa14", "sa13"], ["sa16"])
+    tt(T.o16[:, :], si(15), si(16), A.add, ["sa15", "sa16"], ["o16"])
+    ts(T.aw[:, :], src, 1024.0, A.is_ge, r=["opp"], w=["aw"])
     for h in range(2):
-        for s in range(3):
-            cp(T.r16[:, 384 * h + 128 * s:384 * h + 128 * s + 128], T.r0i[:, 256 * s + 128 * h:256 * s + 128 * h + 128],
-               ["r0a", "r0b"], ["r16_%d%d" % (h, s)])
-        send(h, ["r16_%d%d" % (h, s) for s in range(3)])
-    ts(T.aw[:, :], T.oppi[:, :], 1024.0, A.is_ge, r=["opp"], w=["aw"])
-    src, oo = T.oppi[:, :], T.OP[:, 0:48]
-    ts(si(12), src, 6, A.logical_shift_right, 3, A.bitwise_and, ["opp"], ["sa12"])
-    ts(si(13), src, 8, A.logical_shift_right, r=["opp"], w=["sa13"])
-    ts(si(14), src, 1024.0, A.is_ge, 704.0, A.mult, ["opp"], ["sa14"])
-    tt(si(15), si(12), si(13), A.subtract, ["sa12", "sa13"], ["sa15"])
-    tt(si(16), src, si(14), A.add, ["opp", "sa14"], ["sa16"])
-    ts(si(17), si(15), 192.0, A.mult, r=["sa15"], w=["sa17"])
-    tt(T.o16[:, :], si(17), si(16), A.add, ["sa16", "sa17"], ["o16"])
-    tt(oo, si(17), si(16), A.add, ["sa16", "sa17"], ["OP"])
-    for r in range(16):
-        b = "d%d" % (r // 8)
-        mm(T[b][:, 48 * (r % 8):48 * (r % 8) + 48], T.TM[:, 128 * r:128 * r + 128], T.o16[:, :], r % 8 == 0, r % 8 == 7,
-           ["TM%d" % r, "o16"], [b])
-        if r % 8 == 7:
-            act(T.LW[:, 384 * (r // 8):384 * (r // 8) + 384], T[b][:, 0:384], w=["LW%d" % (r // 8)], x=[b])
-    lookup_list(src, "opp", oo, "OP", 48, 0, T.aw[:, :], "aw")
+        for r in range(16):
+            mm(T[DB[h]][:, r:384:16], T.TM[:, 128 * r:128 * r + 128], T.o16[:, 24 * h:24 * h + 24], r == 0, r == 15, ["TM%d" % r, "o16"], [DB[h]])
+        act(T.LW[:, 384 * h:384 * h + 384], T[DB[h]][:, 0:384], w=["LW%d" % h], x=[DB[h]])
+    lookup_list(src, "opp", T.o16[:, :], "o16", 48, 0, T.aw[:, :], "aw")
+    for c in range(NC):
+        for s in range(5):
+            o = 16 * (s % 3) + 4 * c
+            mm(T.d2[:, 20 * c + 4 * s:20 * c + 4 * s + 4], I1, T.o16[:, o:o + 4], c + s == 0, c + s == 7, ["I1", "o16"], ["d2"])
+    ts(T.OFF[:, :], T.d2[:, 0:80], float(HOME), A.add, w=["OFF"] + ["OFF%d_%d" % (s, c) for s in (3, 4) for c in range(NC)], x=["d2"])
     ts(T.k15[:, 0:1], T.kcol[:, 0:1], 15, A.bitwise_and, r=["kcol"], w=["k15"])
-    ts(T.k15[:, 1:2], T.kcol[:, 0:1], 3, A.bitwise_and, r=["kcol"], w=["k3"])
     ts(T.I2[:, :], T.io2[:, 16:144], 128.0, A.is_equal, r=["io2"], w=["I2"], k=0.5)
     ts(T.kf[:, 0:1], T.k15[:, 0:1], -1.0, A.mult, 15.0, A.add, ["k15"], ["kf0"])
-    cp(T.kf[:, 1:2], T.k15[:, 0:1], ["k15"], ["kf1"])
-    ts(T.BM[:, :], T.io2[:, :], T.kf[:, 0:1], A.is_equal, r=["io2", "kf0"], w=["BM"], k=0.5)
+    ts(T.kf[:, 1:2], T.k15[:, 0:1], 4.0, A.mult, r=["k15"], w=["kf1"])
+    ts(T.BM[:, :], T.io2[:, :], T.kf[:, 0:1], A.is_equal, 0.0625, A.mult, ["io2", "kf0"], ["BM"], k=0.5)
     ts(T.zs[:, :], T.zs0[:, :], T.kf[:, 1:2], A.add, r=["zs0", "kf1"], w=["zs"])
-    ts(T.kf[:, 2:3], T.k15[:, 1:2], -0.75, A.mult, T.kf[:, 1:2], A.add, ["k3", "kf1"], ["kf2"])
-    ts(T.kf[:, 4:8], T.zs0[:, 0:4], 0.0625, A.mult, T.kf[:, 2:3], A.add, ["zs0", "kf2"], ["kf4"])
-    ts(T.PL[:, :], T.kf[:, 4:8], 4.0, A.mult, r=["kf4"], w=["PL"])
-    cp(T.OQ[:, :], T.OP[:, 0:64].indirect(T.PL[:, :]), ["OP", "OPz", "PL"], ["OQ"], k=1.5)
-    cp(T.OFF[:, 0:64], T.OQ[:, :], ["OQ"], ["OFF"] + ["OFF3_%d" % c for c in range(NC)])
-    act(T.wc[:, 0:4], T.mub[:, 0:4], scale=1.0 / 32, r=["mu"], w=["w1"])
-    act(T.wc[:, 12:16], T.mub[:, 0:4], scale=0.5, r=["mu"], w=["wa"])
-    tt(T.wc[:, 4:7], T.wc[:, 0:3], T.wc[:, 13:16], A.mult, ["w1", "wa"], ["w2"])
-    tt(T.wc[:, 7:9], T.wc[:, 4:6], T.wc[:, 14:16], A.mult, ["w2", "wa"], ["w3"])
-    lookup_gather(48, 0, "d2")
-    for c in range(NC):
-        for s in range(3):
-            o = 384 * (c // 2) + 128 * s + 64 * (c % 2)
-            mm(reg(hb(c), c, s), I1, T.r16[:, o:o + 64], c % 2 == 0 and s == 0, False, ["I1", "r16_%d%d" % (c // 2, s)], [hb(c)])
-    new_rating([(128 * h, 128 * h + 128, T.r16[:, 384 * h + 256:384 * h + 384]) for h in range(2)], ["r16_02", "r16_12"],
-               "d3", T.S3[:, 0:256], "N3")
-
-    def diag(j):
-        k = "w1" if j < 4 else "w2" if j < 7 else "w3" if j < 9 else "w4"
-        act(T.WD[:, 128 * j:128 * j + 128], I1, scale=T.wc[:, j:j + 1], r=["I1", k], w=["WD%d" % j])
-
-    act(T.WD[:, 1280:1408], I1, scale=0.0625, r=["I1"], w=["WD10"])
-    for j in (0, 1, 2, 4, 5, 7):
-        diag(j)
-    act(T.wc[:, 16:20], T.mub[:, 4:8], scale=-KOFF / 2, bias=BK, r=["mu"], w=["wc"])
+    act(T.wc[:, 0:8], T.mub[:, 0:8], scale=0.5, r=["mu"], w=["wa"])
+    act(T.wc[:, 16:17], T.mub[:, 4:5], scale=-KOFF / 2, bias=KOFF, r=["mu"], w=["wk0"])
+    act(T.wc[:, 17:20], T.mub[:, 5:8], scale=-KOFF / 2, bias=BK, r=["mu", "wk0"], w=["wk"])
     act(T.wc[:, 20:24], T.mub[:, 4:8], scale=0.5, bias=ETA, r=["mu"], w=["wce"])
+    if not KEEP:
+        act(T.wc[:, 24:26], T.mub[:, 6:8], scale=-MAG / 2, r=["mu"], w=["wm"])
+    for s in range(4):
+        weights(s)
     for c in range(NC):
-        mm(reg(hb(c), c, 3), I1, T.S3[:, 64 * c:64 * c + 64], False, c % 2 == 1, ["I1", "N3"], [hb(c)])
+        for i in range(2):
+            mm(hreg(c, 2 * i), I1, T.r16[:, 256 * i + 64 * c:256 * i + 64 * c + 64], i == 0, False, ["I1", "r16_%d" % i], [HB[c]])
+        mm(hreg(c, 1), I1, T.r16[:, 512 + c:768:4], False, True, ["I1", "r16_2%d" % c], [HB[c]])
+        act(wcols(HOME, c, 0, 3), hreg(c, 0, 3), w=[HK[c]], x=[HB[c]])
+        if c not in GATHER_A0:
+            act(T.RH[:, 320 * c:320 * c + 192], hreg(c, 0, 3), w=["RH%d" % c], x=[HB[c]])
+    for i, (m, k) in enumerate(NEXT):
+        mm(T.dx[:, 0:256], m, T.r16[:, 256:512], i == 0, i == 2, [k] + R16[1], ["dx"])
+    half_sum("dx", 3)
+    const(3, 0, "d0")
+    const(3, 1, "d1")
+    lookup_gather(48, 0, "d2")
+    const(3, 2, "d0")
+    const(3, 3, "d1")
     lookup_finish(48, 0, "d2")
-    for h in range(2):
-        act(W[:, 512 * h:512 * h + 512], T["ph%d" % h][:, :], w=HK[2 * h:2 * h + 2], x=["ph%d" % h])
-    for h in range(2):
-        mm(T.pa1[:, 128 * h:128 * h + 128], I1, T.r16[:, 384 * h + 256:384 * h + 384], h == 0, h == 1, ["I1", "r16_%d2" % h], ["pa1"])
-    act(T.ME[:, :], T.pa1[:, 0:256], w=MEK, x=["pa1"])
-    const(0, 0, T.wc[:, 16:17], "d0", "d1")
-    const(1, 1, T.wc[:, 17:18], "d0", "d1")
-    ts(T.Z[:, 64:80], T.OP[:, 0:16], 0x73F, A.bitwise_and, r=["OP"], w=["Z64"])
-    const(2, 2, T.wc[:, 18:19], "d0", "d3")
-    const(3, 3, BK, "d1", "d3")
-    tt(sfl(7, 16), T.Z[:, 64:80], T.Z[:, 0:16], A.subtract, ["Z64", "Z0"], ["sf7"])
+    tt(sfl(7, 16), si(16, 16), T.Z[:, 0:16], A.subtract, ["sa16", "Z0"], ["sf7"])
     tt(sfl(8, 16), sfl(7, 16), sfl(4, 16), A.mult, ["sf7", "sf4"], ["sf8"])
-    tt(T.ZI[:, 0:64:4], sfl(8, 16), T.Z[:, 0:16], A.add, ["sf8", "Z0"], ["ZI0"])
-    for j in (1, 2):
-        cp(T.ZI[:, j:64:4], T.Z[:, 16 * j:16 * j + 16], ["Z0"], ["ZI%d" % j])
-    act(T.ZI[:, 3:64:4], T.tb[:, 0:16], scale=0.0, r=["tb"], w=["ZI3"])
-    act(T.WI[:, 0:64:4], T.tb[:, 0:16], scale=0.0, bias=1.0, r=["tb"], w=["WI0"])
-    act(T.WI[:, 3:64:4], T.tb[:, 0:16], scale=0.0, r=["tb"], w=["WI3"])
+    tt(T.Z[:, 0:16], sfl(8, 16), T.Z[:, 0:16], A.add, ["sf8", "Z0"], ["Z0"])
+    player_columns(48, 0)
+    for j in range(3):
+        act(T.ZI[:, j:48:3], T.ZZ[:, 16 * j:16 * j + 16], bias=HOME + 512.0, r=["ZZ0"], w=["ZI%d" % j])
 
     def pattern(f):
-        for j in range(1, f + 1):
-            s = f - j
-            act(T["PAT%d" % f][:, j:64 * f + 64:f + 1], T.io2[:, 0:64], bias=T.wc[:, 20 + s:21 + s], scale=0.0, r=["io2", "wce"], w=["PAT%d_%d" % (f, j)])
+        m = f + KEEP
+        for j in range(1, m):
+            s = m - 1 - j
+            act(T["PAT%d" % f][:, j:64 * m:m], T.io2[:, 0:64], bias=T.wc[:, 20 + s:21 + s], scale=0.0, r=["io2", "wce"], w=["PAT%d_%d" % (f, j)])
 
     pattern(3)
-    for h in range(2):
-        arrive(h, ["l0_%d" % h])
-        for c in (2 * h, 2 * h + 1):
-            for s in range(3):
-                o = 384 * h + 128 * s + 64 * (c % 2)
-                mm(reg(ab(c), c, s), I1, T.l0[:, o:o + 64], c % 2 == 0 and s == 0, c % 2 == 1 and s == 2, ["I1", "l0_%d" % h], [ab(c)])
-        for c in (2 * h, 2 * h + 1):
-            away_copy(c, 3, h == 0)
+    for i, (a, b) in zip(first_msgs, INIT):
+        arrive(i, ["l0_%d" % s for s in range(a // 256, b // 256)])
+        for s in range(a // 256, b // 256):
+            o = W[:, AWAY + 256 * (2 * s % 3):AWAY + 256 * (2 * s % 3) + 256]
+            if s == 2:
+                cp(o, T.l0[:, 512:768], ["l0_2"], ["WI%d_" % s])
+                continue
+            for c in range(NC):
+                mm(T.dx[:, c:256:4], I1, T.l0[:, 256 * s + 64 * c:256 * s + 64 * c + 64], c == 0, c == NC - 1, ["I1", "l0_%d" % s], ["dx"])
+            act(o, T.dx[:, 0:256], w=["WI%d_" % s], x=["dx"])
+    for wf in WIN:
+        WIN[wf][1].extend(["WI0_", "WI1_", "WI2_"])
 
     def part1(f):
-        pair = {(1, 0): 0, (2, 0): 1, (2, 1): 2, (3, 0): 3, (3, 1): 4, (3, 2): 5}
+        win, wk = WIN[3]
+        npair = f * (f - 1) // 2
+        many = len(PARTS[f]) > 1
+        zo = 48 * (f - 3)
+        for h, cs in enumerate(PARTS[f]):
+            p0, nn = 64 * cs[0], 64 * len(cs)
+            m, j0, base, tag = nn // 16, p0 // 16, f * p0, "_%d" % h
+            place = [(DB[h], nn * k) if many else (DB[k // 2], nn * (k % 2)) for k in range(f - 1)]
+            for k in range(f):
+                tk = T.TK[:, base + nn * k:base + nn * (k + 1)]
+                tt(tk, win.indirect(T.CO[:, 16 * k + j0:16 * k + j0 + m]), T.ME[:, p0:p0 + nn] if f == 4 else T.r16[:, 256 + p0:256 + p0 + nn],
+                   A.subtract, wk + ["CO48" if k == 3 else "CO0"] + ([MEK[c] for c in cs] if f == 4 else R16[1]), ["TK%d" % k + tag], k=1.5)
+                if k < f - 1:
+                    b, o = place[k]
+                    act(T[b][:, o:o + nn], tk, F.Abs, r=["TK%d" % k + tag], x=[b])
+                if k > 0:
+                    act(T.DS[:, base + nn * k:base + nn * (k + 1)], tk, F.Abs, r=["TK%d" % k + tag], w=["DS%d" % k + tag])
+            lb = npair * p0
+            for i, (k, j) in enumerate([(1, 0), (2, 1), (2, 0), (3, 0), (3, 1), (3, 2)][:npair]):
+                b, o = place[j]
+                tt(T.LT[:, lb + nn * i:lb + nn * (i + 1)], T.DS[:, base + nn * k:base + nn * (k + 1)], T[b][:, o:o + nn],
+                   A.is_lt, ["DS%d" % k + tag], ["LT%d" % i + tag], [b])
+                if i % 3 == 2:
+                    b, o = DB[2 + i // 3], lb + nn * (i - 2)
+                    for r in range(16):
+                        mm(T[b][:, 0:3 * m], T.BM[:, 15 - r:143 - r], T.LT[:, o + r:o + 3 * nn:16], r == 0, r == 15,
+                           ["BM"] + ["LT%d" % q + tag for q in range(i - 2, i + 1)], [b])
+            wo = 6 * j0
 
-        def gk(k):
-            ck = "CO48" if k == 3 else "CO0"
-            tk = T.TK[:, 256 * k:256 * k + 256]
-            tt(tk, win.indirect(T.CO[:, 16 * k:16 * k + 16]), T.ME[:, :], A.subtract, WIN + [ck] + MEK, ["TK%d" % k], k=1.5)
-            if k > 0:
-                act(T.DS[:, 256 * k:256 * k + 256], tk, F.Abs, r=["TK%d" % k], w=["DS%d" % k])
-            if k < f - 1:
-                act(T["d%d" % k][:, 0:256], tk, F.Abs, r=["TK%d" % k], x=["d%d" % k])
+            def wt(i, k=1):
+                return T.WT[:, wo + m * i:wo + m * (i + k)]
 
-        def lt(k, j):
-            i = pair[(k, j)]
-            tt(T.LT[:, 256 * i:256 * i + 256], T.DS[:, 256 * k:256 * k + 256], T["d%d" % j][:, 0:256], A.is_lt, ["DS%d" % k], ["LT%d" % i], ["d%d" % j])
+            def tri(buf, k):
+                return buf[:, 3 * j0 + k:3 * (j0 + m):3]
 
-        def count(b, bank):
-            for r in range(16):
-                mm(T[bank][:, 0:48], T.BM[:, 15 - r:143 - r], T.LT[:, 768 * b + r:768 * b + 768:16], r == 0, r == 15,
-                   ["BM"] + ["LT%d" % (3 * b + i) for i in range(3)], [bank])
-
-        for k in range(f):
-            gk(k)
-        lt(1, 0); lt(2, 0); lt(2, 1)
-        count(0, "d3")
-        if f == 4:
-            lt(3, 0); lt(3, 1); lt(3, 2)
-            count(1, "d0")
-        b1, w20, w21 = T.WT[:, 0:16], T.WT[:, 16:32], T.WT[:, 32:48]
-        e = [sfl(11 + j // 3, 16, 16 * (j % 3)) for j in range(6)]
-        ts(T.WT[:, :], T.d3[:, 0:48], 9.0, A.is_ge, w=["wt"], x=["d3"])
-        act(T.WI[:, 1:64:4], b1, r=["wt"], w=["WI1"])
-        tt(e[0], w21, w20, A.subtract, ["wt"], ["e0"])
-        tt(e[2], e[0], b1, A.mult, ["e0", "wt"], ["e2"])
-        tt(T.WI[:, 2:64:4], e[2], w20, A.add, ["e2", "wt"], ["WI2"])
-        if f == 4:
-            act(sfl(14, 16, 32), T.WI[:, 2:64:4], r=["WI2"], w=["s2"])
-            act(e[3], T.WI[:, 2:64:4], scale=-1.0, bias=1.0, r=["WI2"], w=["e3"])
-            tt(sfl(14, 16, 16), e[3], b1, A.mult, ["e3", "wt"], ["s1"])
-            tt(sfl(14, 16), e[3], sfl(14, 16, 16), A.subtract, ["e3", "s1"], ["s0"])
-            tt(sfl(15), T.d0[:, 0:48], sfl(14), A.mult, ["s0", "s1", "s2"], ["m"], ["d0"])
-            tt(e[4], sfl(15, 16), sfl(15, 16, 16), A.add, ["m"], ["e4"])
-            tt(e[5], e[4], sfl(15, 16, 32), A.add, ["m", "e4"], ["e5"])
-            ts(T.WI[:, 3:64:4], e[5], 9.0, A.is_ge, r=["e5"], w=["WI3"])
-        wk = ["WI%d" % j for j in range(4)]
-        act(T.UI[:, :], T.WI[:, :], scale=-1.0, bias=1.0, r=wk, w=["UI"])
-        tt(T.VI[:, :], T.WI[:, :], T.ZI[:, :], A.mult, wk + ["ZI%d" % j for j in range(4)], ["VI"], k=1.0)
-        o = 64 * (f - 3)
-        zk = "SC%d" % f
-        add("v", lambda: g.vector.tensor_tensor_scan(T.SC[:, o:o + 64], T.UI[:, :], T.VI[:, :], 0.0, A.mult, A.add), ["UI", "VI"], [zk], cost=0.11)
-        z = T.SC[:, o + 3:o + 64:4]
-        ts(T.OFF[:, 64:80], z, 64.0 * (f - 1), A.add, r=[zk], w=["OFF4"])
-        if f == 3:
-            for c in range(NC):
-                ts(T.OFF[:, 16 * c + 12:16 * c + 16], T.SC[:, 16 * c + 3:16 * c + 16:4], 64.0 * (f - 1), A.add, r=[zk], w=["OFF3_%d" % c])
+            w10, w21, w20 = wt(0), wt(1), wt(2)
+            e0, e1 = T.EE[:, j0:j0 + m], T.EE[:, 16 + j0:16 + j0 + m]
+            ts(wt(0, 3), T.d2[:, 0:3 * m], 9.0 / 16, A.is_ge, w=["wt" + tag], x=["d2"])
+            act(tri(T.WI, 1), w10, r=["wt" + tag], w=["WI1" + tag])
+            tt(e0, w21, w20, A.subtract, ["wt" + tag], ["e0" + tag])
+            tt(e1, e0, w10, A.mult, ["e0" + tag, "wt" + tag], ["e1" + tag])
+            tt(tri(T.WI, 2), e1, w20, A.add, ["e1" + tag, "wt" + tag], ["WI2" + tag])
+            zk = ["ZI%d" % j for j in range(3)]
+            if f == 4:
+                ts(wt(3, 3), T.dx[:, 0:3 * m], 9.0 / 16, A.is_ge, w=["wu" + tag], x=["dx"])
+                tt(T.MZ[:, 3 * j0:3 * (j0 + m)], wt(3, 3), T.DZ[:, 3 * j0:3 * (j0 + m)], A.mult, ["wu" + tag, "DZ" + tag], ["MZ" + tag])
+                for k in range(3):
+                    tt(tri(T.ZI, k), T.MZ[:, 3 * j0 + m * k:3 * j0 + m * (k + 1)], T.ZB[:, 16 * k + j0:16 * k + j0 + m], A.add,
+                       ["MZ" + tag, "ZB", "SC3"], ["ZJ%d" % k + tag])
+                zk = ["ZJ%d" % k + tag for k in range(3)]
+            a0, a1 = 3 * j0, 3 * (j0 + m)
+            wi = ["WI0", "WI1" + tag, "WI2" + tag]
+            act(T.UI[:, a0:a1], T.WI[:, a0:a1], scale=-1.0, bias=1.0, r=wi, w=["UI" + tag])
+            tt(T.VI[:, a0:a1], T.WI[:, a0:a1], T.ZI[:, a0:a1], A.mult, wi + zk, ["VI" + tag], k=1.0)
+            add("v", lambda a0=a0, a1=a1: g.vector.tensor_tensor_scan(T.SC[:, zo + a0:zo + a1], T.UI[:, a0:a1], T.VI[:, a0:a1], 0.0, A.mult, A.add),
+                ["UI" + tag, "VI" + tag], ["SC%d_%d" % (f, c) for c in cs] + ["SC%d" % f], cost=0.11)
+            o = 16 * (f - 3) + j0
+            cp(T.OFN[:, o:o + m], T.SC[:, zo + a0 + 2:zo + a1:3], ["SC%d_%d" % (f, c) for c in cs], ["OFN%d" % c for c in cs])
         for c in range(NC):
-            preload(c, f)
-            gather(T.TT, "TT", c, f, "old", GATHER_A0)
-        return z, zk
+            preload(c, 3 * (f - 3))
+            gather(T.TT, "TT", c, 0, f, 3, c in GATHER_A0)
+            limit(T.TT[:, 320 * c:320 * c + 64 * f], ["TT%d_%d" % (c, s) for s in range(f)])
+        for cs in NEWS:
+            p0, p1, o = 64 * cs[0], 64 * cs[-1] + 64, 16 * (f - 3)
+            tt(T.TN[:, p0:p1], WIN[f][0].indirect(T.OFN[:, o + p0 // 16:o + p1 // 16]), T.RN[:, p0:p1], A.subtract,
+               WIN[f][1] + ["OFN%d" % c for c in cs] + ["RN"], ["TN%d" % c for c in cs], k=1.5)
+            limit(T.TN[:, p0:p1], ["TN%d" % c for c in cs])
+        for c in range(NC):
+            act(wcols(HOME, c, f, f + 1), T.RN[:, 64 * c:64 * c + 64], r=["RN"], w=["WN%d_%d" % (f, c)])
+        return T.SC[:, zo + 2:zo + 48:3], ["SC%d_%d" % (f, c) for c in range(NC)]
 
     def node_numbers(f, z, zk):
-        cp(si(19, 16), z, [zk], ["sa19"])
-        ts(si(21, 16), si(19, 16), 63, A.bitwise_and, r=["sa19"], w=["sa21"])
-        ts(si(22, 16), si(19, 16), 2, A.logical_shift_right, 192, A.bitwise_and, ["sa19"], ["sa22"])
-        ts(si(23, 16), si(19, 16), 1024.0, A.is_ge, 1280.0, A.mult, ["sa19"], ["sa23"])
-        tt(si(6, 16), si(21, 16), si(22, 16), A.add, ["sa21", "sa22"], ["sa6"])
-        tt(si(7, 16), si(6, 16), si(23, 16), A.add, ["sa6", "sa23"], ["sa7"])
+        zo = 48 * (f - 3)
+        for c in range(NC):
+            cp(T.OFF[:, 20 * c + 4 * f:20 * c + 4 * f + 4], T.SC[:, zo + 12 * c + 2:zo + 12 * c + 12:3], zk, ["OFF%d_%d" % (f, c)])
+        ts(si(19, 16), z, -(HOME + 256.0 * (f - 1)), A.add, r=zk, w=["sa19"])
+        ts(si(21, 16), si(19, 16), 2, A.logical_shift_right, 63, A.bitwise_and, ["sa19"], ["sa21"])
+        ts(si(22, 16), si(19, 16), 3, A.bitwise_and, r=["sa19"], w=["sa22"])
+        ts(si(23, 16), si(19, 16), 1280.0, A.is_ge, 1280.0, A.mult, ["sa19"], ["sa23"])
+        ts(si(8, 16), si(22, 16), 64.0, A.mult, 256.0 * (f - 1), A.add, ["sa22"], ["sa8"])
+        tt(si(6, 16), si(21, 16), si(23, 16), A.add, ["sa21", "sa23"], ["sa6"])
         if f == 3:
-            ts(si(20, 16), si(7, 16), 256.0 * (f - 1), A.add, r=["sa7"], w=["sa20"])
-        ts(T.YO[:, 16 * (f - 3):16 * (f - 2)], si(7, 16), 256.0 * (f - 1), A.add, r=["sa7"], w=["YO%d" % f])
+            tt(si(20, 16), si(6, 16), si(8, 16), A.add, ["sa6", "sa8"], ["sa20"])
+        tt(T.YO[:, 16 * (f - 3):16 * (f - 2)], si(6, 16), si(8, 16), A.add, ["sa6", "sa8"], ["YO%d" % f])
 
     def sweep(k, idle):
         f = 3 + k // 3
         first, last = k % 3 == 0, k % 3 == 2
-        nn = 64 * (f + 1)
+        ns = f + KEEP
+        nn = 64 * ns
         dl, ld = T["dl%d" % k], T["ld%d" % k]
-        m0 = 2 + len(SENDS) * k
+        dgm, dgk = dg(f)
+        msgs = []
+
+        def lim(c, t):
+            if first and t == f:
+                return T.TN[:, 64 * c:64 * c + 64], "TN%d" % c
+            return T.TT[:, 320 * c + 64 * t:320 * c + 64 * t + 64], "TT%d_%d" % (c, t)
+
         for c in range(NC):
-            b, d, dk, xk = 320 * c, T["d%d" % c], "d%d" % c, "X%d" % c
-            cut = not first and c in SPLIT
-            if cut:
-                gather(T.TT, "TT", c, f, "low", GATHER_A)
-            gather(T.TT, "TT", c, f, "new" if first else "high" if cut else "all", GATHER_A)
-            tk = ["TT%d_%d" % (c, s) for s in range(f + 1)]
-            for lo, hi in ([(0, 2), (2, f + 1)] if cut else [(0, f), (f, f + 1)] if first and c in SPLIT0 else [(0, f + 1)]):
-                v = T.TT[:, b + 64 * lo:b + 64 * hi]
-                ts(v, v, 256.0, A.min, -256.0, A.max, tk[lo:hi], tk[lo:hi], k=0.5)
-            for t in range(f + 1):
-                for s in range(t, f + 1):
+            dk = DB[c]
+            if not first:
+                for lo, hi in ([(0, CUT), (CUT, f + 1)] if c in SPLIT else [(0, f + 1)]):
+                    gather(T.TT, "TT", c, lo, hi, f, c in GATHER_A)
+                    limit(T.TT[:, 320 * c + 64 * lo:320 * c + 64 * hi], ["TT%d_%d" % (c, s) for s in range(lo, hi)])
+            how, d = FLOOR[k][c], T[dk]
+            top = ns if how == "P" else f + 1
+            for t in range(top):
+                v, vk = lim(c, t)
+                for s in range(t, top):
                     m, mk = wd(s, t)
-                    mm(dreg(c, f, s), m, T.TT[:, b + 64 * t:b + 64 * t + 64], False, s == f and t == s and FLOOR[c] in "AV", [mk, tk[t]], [dk])
-            src, r, x = T.X[:, b:b + nn], [xk], []
-            if FLOOR[c] == "P":
-                mm(d[:, 0:nn], I1, T.MP[:, 0:nn], False, False, ["I1", "MP"], [dk])
-                mm(d[:, 0:nn], I1, T.MP[:, 320:320 + nn], False, True, ["I1", "MN"], [dk])
-                src, r, x = d[:, 0:nn], [], [dk]
-            elif FLOOR[c] == "H":
-                mm(d[:, 0:nn], I1, T.MP[:, 0:nn], False, True, ["I1", "MP"], [dk])
-                act(src, d[:, 0:nn], bias=-MAG, w=[xk], x=[dk])
-            elif FLOOR[c] == "A":
-                act(T.V[:, b:b + nn], d[:, 0:nn], bias=MAG, w=["V%d" % c], x=[dk])
-                act(src, T.V[:, b:b + nn], bias=-MAG, r=["V%d" % c], w=[xk])
-            else:
-                ts(src, d[:, 0:nn], MAG, A.add, -MAG, A.add, w=[xk], x=[dk])
-            add("v", lambda c=c, src=src: g.vector.tensor_tensor_scan(dl[:, nn * c:nn * (c + 1)], T["PAT%d" % f][:, :], src, 1536.0, A.mult, A.add),
-                r + ["PAT%d_%d" % (f, j) for j in range(f + 1)], ["dl%d_%d" % (k, c)], x, cost=0.05 + nn * CYC)
-            for i, cs in enumerate(SENDS):
-                if cs[-1] == c:
-                    send(m0 + i, ["dl%d_%d" % (k, q) for q in cs])
-        for c in range(NC):
-            for s in range(4):
-                mm(reg(hb(c), c, s), I1, dl[:, nn * c + f - s:nn * (c + 1):f + 1], c % 2 == 0 and s == 0, c % 2 == 1 and s == 3,
-                   ["I1", "dl%d_%d" % (k, c)], [hb(c)])
-            if c % 2 == 1:
-                h = c // 2
-                after = GATHER_AF if k == 5 else GATHER_A0 if k == 2 else GATHER_A
-                for cs in ([[c - 1, c]] if (c - 1 in after) == (c in after) else [[c - 1], [c]]):
-                    a0, a1 = 256 * cs[0], 256 * cs[-1] + 256
-                    ph, wh, hk = T["ph%d" % h][:, a0 - 512 * h:a1 - 512 * h], W[:, a0:a1], [HK[q] for q in cs]
-                    if cs[0] in after:
-                        tt(ph, ph, wh, A.add, hk, [], ["ph%d" % h])
-                        act(wh, ph, w=hk, x=["ph%d" % h])
+                    mm(dreg(c, f, s), m, v, False, how in "AV" and t == f, [mk, vk], [dk])
+                if t and how in "PH":
+                    mm(dreg(c, f, t), I1, MP, False, t == f and how == "H", ["I1", "MP"], [dk])
+                if t and how == "P":
+                    mm(dreg(c, f, t), I1, MN, False, t == f, ["I1", "MN"], [dk])
+            src, r, x = d[:, 0:nn], [], [dk]
+            if KEEP:
+                if how != "P":
+                    src, r, x = T.X[:, 320 * c:320 * c + nn], ["X%d" % c], []
+                    if how == "A":
+                        act(d[:, 0:nn], d[:, 0:nn], bias=MAG, w=["XM%d" % c], x=[dk])
+                    if how == "V":
+                        ts(src, d[:, 0:nn], MAG, A.add, -MAG, A.add, w=r, x=[dk])
                     else:
-                        tt(T.RH[:, a0:a1], ph, wh, A.add, hk, ["RH%d" % q for q in cs], ["ph%d" % h])
-                        act(wh, T.RH[:, a0:a1], r=["RH%d" % q for q in cs], w=hk)
-        if f == 4:
-            tt(T.H4[:, :], T.H4[:, :], dl[:, 0:1280:5], A.add, ["H4"] + ["dl%d_%d" % (k, c) for c in range(NC)], ["H4"])
+                        act(src, d[:, 0:nn], bias=-MAG, r=["XM%d" % c], w=r, x=[dk])
+            elif how == "P":
+                cell, cs = dreg(c, f, f - 1), cplace(f, f, c, c + 1)
+                mm(cell, dgm, T.CH[:, cs], False, False, [dgk, "CH" + ckey(f, f)], [dk])
+                mm(cell, dgm, T.CL[:, cs], False, False, [dgk, "CL" + ckey(f, f)], [dk])
+                for t in range(f + 1):
+                    v, vk = lim(c, t)
+                    m, mk = wx(f, t)
+                    mm(cell, m, v, False, False, [mk, vk], [dk])
+                mm(cell, dgm, MP, False, False, [dgk, "MP"], [dk])
+                mm(cell, dgm, MN, False, True, [dgk, "MN"], [dk])
+            else:
+                src, r, x = T.X[:, 256 * c:256 * c + nn], ["X%d" % c], []
+                if how == "A":
+                    act(d[:, 0:nn + 64], d[:, 0:nn + 64], bias=MAG, w=["XM%d" % c], x=[dk])
+                act(src, d[:, 0:nn], bias=-MAG, r=["XM%d" % c], w=r, x=[dk])
+                act(d[:, 320:384], dreg(c, f, f), scale=T.wc[:, 3 + f:4 + f], bias=T.wc[:, 21 + f:22 + f], r=["wa", "wm", "XM%d" % c], x=[dk])
+                xs = T.X[:, 256 * c:256 * c + nn:f]
+                tt(xs, d[:, 320:384], xs, A.add, r, r, [dk])
+            add("v", lambda c=c, src=src: g.vector.tensor_tensor_scan(dl[:, nn * c:nn * (c + 1)], T["PAT%d" % f][:, 0:nn], src, 1536.0, A.mult, A.add),
+                r + ["PAT%d_%d" % (f, j) for j in range(ns)], ["dl%d_%d" % (k, c)], x, cost=0.05 + nn * CYC)
+            msgs.append(send(ld[:, nn * c:nn * (c + 1)], dl[:, nn * c:nn * (c + 1)], ["dl%d_%d" % (k, c)], 2 * nn))
+        after = GATHER_AF if k == 5 else GATHER_A0 if k == 2 else GATHER_A
+        for c in range(NC):
+            dk, o, dn = DB[c], dreg(c, f, f), T.dn[:, 64 * c:64 * c + 64]
+            if KEEP:
+                pass
+            elif FLOOR[k][c] == "P":
+                cs = cplace(f, f, c, c + 1)
+                mm(o, I1, T.CH[:, cs], True, False, ["I1", "CH" + ckey(f, f)], [dk])
+                mm(o, I1, T.CL[:, cs], False, False, ["I1", "CL" + ckey(f, f)], [dk])
+                for t in range(f + 1):
+                    v, vk = lim(c, t)
+                    m, mk = wd(f, t)
+                    mm(o, m, v, False, t == f, [mk, vk], [dk])
+                ts(dn, o, 1.0 / 32, A.add, w=["dn%d" % c], x=[dk])
+            else:
+                ts(dn, o, -MAG, A.add, 1.0 / 32, A.add, w=["dn%d" % c], x=[dk])
+            for s in range(ns):
+                mm(hreg(c, s), I1, dl[:, nn * c + ns - 1 - s:nn * (c + 1):ns], s == 0, s == f, ["I1", "dl%d_%d" % (k, c)], [HB[c]])
+            if not KEEP:
+                mm(hreg(c, f), I1, dn, False, True, ["I1", "dn%d" % c], [HB[c]])
+            wh, hk, h = wcols(HOME, c, 0, f + 1), [HK[c], "WN%d_%d" % (f, c)], hreg(c, 0, f + 1)
+            if c in after:
+                tt(h, h, wh, A.add, hk, [], [HB[c]])
+                act(wh, h, w=hk[:1], x=[HB[c]])
+            else:
+                rh = T.RH[:, 320 * c:320 * c + 64 * f + 64]
+                tt(rh, h, wh, A.add, hk, ["RH%d" % c], [HB[c]])
+                act(wh, rh, r=["RH%d" % c], w=hk[:1])
+        if k == 2:
+            late = send(W[:, AWAY + 768:WEND], W[:, HOME + 768:HOME + 1024], HK, 1024, True)
         idle()
         if not last:
-            for c in range(NC):
-                preload(c, f)
-        for i, cs in enumerate(SENDS):
-            arrive(m0 + i, ["ld%d_%d" % (k, c) for c in cs])
-            for c in cs:
-                for s in range(4):
-                    mm(reg(ab(c), c, s), I1, ld[:, nn * c + f - s:nn * (c + 1):f + 1], s == 0, s == 3,
-                       ["I1", "ld%d_%d" % (k, c)], [ab(c)])
-                wa = W[:, 1024 + 256 * c:1024 + 256 * c + 256]
-                tt(wa, wa, reg(ab(c), c, 0, 4), A.add, [AK[c]], [AK[c]], [ab(c)])
+            for c in range(NC - 1):
+                preload(c, k + 1)
+        for c in range(NC):
+            arrive(msgs[c], ["ld%d_%d" % (k, c)])
+            for s in range(f):
+                mm(T.dx[:, 64 * s:64 * s + 64], I1, ld[:, nn * c + ns - 1 - s:nn * (c + 1):ns], s == 0, s == f - 1, ["I1", "ld%d_%d" % (k, c)], ["dx"])
+            wa = wcols(AWAY, c, 0, f)
+            tt(wa, wa, T.dx[:, 0:64 * f], A.add, [AK[c], "WI0_", "WI1_", "WI2_"] + (["WL"] if f == 4 else []), [AK[c]], ["dx"])
         marks.append(len(ops) - 1)
+        if k == 2:
+            arrive(late, ["WL"])
+        if not last:
+            preload(NC - 1, k + 1)
 
     def stakes(cs):
         for c in cs:
@@ -641,33 +802,36 @@ def rank_program(g, core, T, topo):
     z3, z3k = part1(3)
 
     def idle0():
-        new_rating([(128 * h, 128 * h + 128, T.l0[:, 384 * h + 256:384 * h + 384]) for h in range(2)], ["l0_0", "l0_1"], "d3", None, None)
         node_numbers(3, z3, z3k)
-        ts(si(5, 16), z3, 128.0, A.add, r=[z3k], w=["sa5"])
-        act(T.aw[:, 0:16], z3, F.Sigmoid, bias=-1856.0, scale=2.0, r=[z3k, HK[3]], w=["aw"], more=1.3)
+        ts(si(5, 16), z3, -float(HOME), A.add, r=z3k, w=["sa5"])
+        act(T.aw[:, 0:16], z3, F.Sigmoid, bias=-2.0 * AWAY, scale=2.0, r=z3k + [HK[3]], w=["aw"], more=1.3)
         lookup_list(si(20, 16), "sa20", si(5, 16), "sa5", 16, 48, T.aw[:, 0:16], "aw")
-        tt(T.wc[:, 9:10], T.wc[:, 7:8], T.wc[:, 15:16], A.mult, ["w3", "wa"], ["w4"])
-        for j in (3, 6, 8, 9):
-            diag(j)
-        const(4, 2, T.wc[:, 18:19], "d0", "d1")
-        const(7, 0, T.wc[:, 16:17], "d2", "d3")
-        const(8, 1, T.wc[:, 17:18], "d2", "d3")
-
-    S3K = ["N3"] + ["dl%d_%d" % (k, c) for k in range(3) for c in range(NC)]
-    S3P = [T.S3[:, :]] + [T["dl%d" % k][:, 0:1024:4] for k in range(3)]
+        weights(4)
+        const(4, 3, "d1")
+        for s in range(3):
+            const_again(s)
 
     def idle1():
         lookup_gather(16, 48, "d2")
         lookup_finish(16, 48, "d2")
-        cp(T.ZI[:, 3:64:4], T.Z[:, 48:64], ["Z48"], ["ZI3"])
-        const(5, 3, T.wc[:, 19:20], "d0", "d1")
-        const(6, 4, BK, "d0", "d1")
+        player_columns(16, 48)
+        act(T.ZB[:, :], T.ZZ[:, 0:48], bias=HOME + 768.0, r=["ZZ0"], w=["ZB"])
+        for h, cs in enumerate(PARTS[4]):
+            j0, m = 4 * cs[0], 4 * len(cs)
+            for k in range(3):
+                tt(T.DZ[:, 3 * j0 + m * k:3 * j0 + m * (k + 1)], T.ZZ[:, 48 + j0:48 + j0 + m], T.ZZ[:, 16 * k + j0:16 * k + j0 + m], A.subtract,
+                   ["ZZ0", "ZZ48"], ["DZ_%d" % h])
+        const(4, 4, "d1")
+        act(T.I32[:, :], I1, r=["I1"], w=["I32"])
+        for i, (m, k) in enumerate(NEXT):
+            mm(T.d1[:, 0:128], I1, m, i == 0, i == 2, ["I1", k], ["d1"])
+        act(T.NM[:, :], T.d1[:, 0:128], w=["NM"], x=["d1"])
 
     def idle2():
-        for h in range(4):
-            mm(T.d2[:, 0:256], I1, S3P[h], h == 0, h == 3, ["I1"] + S3K, ["d2"])
-        act(T.ME[:, :], T.d2[:, 0:256], w=MEK, x=["d2"])
-        new_rating([(0, 256, S3P[h]) for h in range(4)], S3K, "d3", T.H4[:, :], "H4")
+        newest(4)
+        for c in range(NC):
+            mm(T.d2[:, 64 * c:64 * c + 64], T.NM[:, :], wcols(HOME, c, 3, 4), c == 0, c == NC - 1, ["NM", HK[c]], ["d2"], k=4.0)
+        half_sum("d2", 4)
         pattern(4)
 
     sweep(0, idle0)
@@ -681,35 +845,49 @@ def rank_program(g, core, T, topo):
         stakes([0, 1])
 
     def idle4():
-        act(T.I32[:, :], I1, r=["I1"], w=["I32"])
         stakes([2, 3])
 
     def idle5():
-        ts(T.YR[:, 1024:1280], T.H4[:, :], -9216.0, A.add, r=["H4"], w=["YR4"])
         for c in range(NC):
-            for s in range(4):
+            for s in range(5):
                 o = T.YR[:, 256 * s + 64 * c:256 * s + 64 * c + 64]
+                i, r = wcols(HOME, c, s, s + 1), [HK[c]]
                 if c < 2:
-                    ts(o, W[:, 256 * c + 64 * s:256 * c + 64 * s + 64], -9216.0, A.add, r=[HK[c]], w=["YR%d%d" % (c, s)])
+                    ts(o, i, -9216.0, A.add, r=r, w=["YR%d%d" % (c, s)])
                 else:
-                    act(o, W[:, 256 * c + 64 * s:256 * c + 64 * s + 64], bias=-9216.0, r=[HK[c]], w=["YR%d%d" % (c, s)])
-        dma("s", T.yr[:, :], T.YR[:, :], r=["YR4"] + ["YR%d%d" % (c, s) for c in range(NC) for s in range(4)])
+                    act(o, i, bias=-9216.0, r=r, w=["YR%d%d" % (c, s)])
+        dma("s", T.yr[:, :], T.YR[:, :], r=["YR%d%d" % (c, s) for c in range(NC) for s in range(5)], lat=3.6)
 
     sweep(3, idle3)
     sweep(4, idle4)
     sweep(5, idle5)
 
     for c in range(NC):
-        b, d, dk = 320 * c, T["d%d" % c], "d%d" % c
-        gather(T.TK, "TF", c, 4, "all", GATHER_AF)
-        act(d[:, 0:320], T.TK[:, b:b + 320], F.Sigmoid, scale=-1.0 / 256, r=["TF%d_%d" % (c, s) for s in range(5)], x=[dk])
+        b, dk = 320 * c, DB[(c + 1) % NC]
+        d = T[dk]
         sk = ["stc%d_%d" % (c, s) for s in range(5)]
-        if c in SUM_V:
+        if c in SUM_S:
+            e, ek = T[HB[0]], HB[0]
+            for lo, hi, p, pk in ((0, 3, d, dk), (3, 5, e, ek)):
+                cols, key = slice(b + 64 * lo, b + 64 * hi), "PR%d_%d" % (c, lo)
+                gather(T.TK, "TF", c, lo, hi, 4, c in GATHER_AF)
+                act(p[:, 0:64 * (hi - lo)], T.TK[:, cols], F.Sigmoid, scale=-1.0 / 256, r=["TF%d_%d" % (c, s) for s in range(lo, hi)], x=[pk])
+                tt(T.DS[:, cols], p[:, 0:64 * (hi - lo)], T.stc[:, cols], A.mult, sk, [key], [pk])
+            for s in range(3):
+                mm(d[:, 320:384], T.I32[:, :], T.DS[:, b + 64 * s:b + 64 * s + 64], s == 0, s == 2, ["I32", "PR%d_0" % c], [dk], k=4.0)
+            tt(d[:, 384:448], d[:, 320:384], T.DS[:, b + 192:b + 256], A.add, ["PR%d_3" % c], ["PT%d" % c], [dk])
+            tt(T.Y[:, 64 * c:64 * c + 64], d[:, 384:448], T.DS[:, b + 256:b + 320], A.add, ["PR%d_3" % c, "PT%d" % c], ["Y%d" % c], [dk])
+        else:
+            gather(T.TK, "TF", c, 0, 5, 4, c in GATHER_AF)
+            act(d[:, 0:320], T.TK[:, b:b + 320], F.Sigmoid, scale=-1.0 / 256, r=["TF%d_%d" % (c, s) for s in range(5)], x=[dk])
+        if c in SUM_S:
+            pass
+        elif c in SUM_V:
             tt(T.DS[:, b:b + 192], d[:, 0:192], T.stc[:, b:b + 192], A.mult, sk, ["PR%d" % c], [dk])
-            tt(d[:, 192:320], d[:, 192:320], T.stc[:, b + 192:b + 320], A.mult, sk, [], [dk])
-            tt(d[:, 0:128], d[:, 192:320], T.DS[:, b:b + 128], A.add, ["PR%d" % c], [], [dk])
-            tt(T.DS[:, b:b + 64], d[:, 0:64], T.DS[:, b + 128:b + 192], A.add, ["PR%d" % c], ["PR%d" % c], [dk])
-            tt(T.Y[:, 64 * c:64 * c + 64], d[:, 64:128], T.DS[:, b:b + 64], A.add, ["PR%d" % c], ["Y%d" % c], [dk])
+            tt(d[:, 192:320], d[:, 192:320], T.stc[:, b + 192:b + 320], A.mult, sk, ["PS%d" % c], [dk])
+            tt(d[:, 320:448], d[:, 192:320], T.DS[:, b:b + 128], A.add, ["PR%d" % c, "PS%d" % c], ["PT%d" % c], [dk])
+            tt(T.DS[:, b + 192:b + 256], d[:, 320:384], T.DS[:, b + 128:b + 192], A.add, ["PR%d" % c, "PT%d" % c], ["PU%d" % c], [dk])
+            tt(T.Y[:, 64 * c:64 * c + 64], d[:, 384:448], T.DS[:, b + 192:b + 256], A.add, ["PU%d" % c], ["Y%d" % c], [dk])
         else:
             tt(T.DS[:, b:b + 320], d[:, 0:320], T.stc[:, b:b + 320], A.mult, sk, ["PR%d" % c], [dk])
             for s in range(5):
@@ -727,14 +905,14 @@ def rank_program(g, core, T, topo):
     semof = {"v": "sv", "a": "sa", "p": "sp", "g": "sg"}
     needed = set()
     for o in ops:
-        newest, keep = {}, []
-        for j in o["deps"]:
+        newest_of, keep = {}, []
+        for j in o["hard"]:
             qj = ops[j]["q"]
             if ops[j]["tok"] is not None:
                 keep.append(j)
-            elif not (qj == "p" and o["q"] == "p") and place[j] > place.get(newest.get(qj), -1):
-                newest[qj] = j
-        o["wait"] = keep + list(newest.values())
+            elif not (qj == "p" and o["q"] == "p") and place[j] > place.get(newest_of.get(qj), -1):
+                newest_of[qj] = j
+        o["wait"] = keep + list(newest_of.values())
         needed.update(o["wait"])
     cnt, known, clock, top = {}, {q: {} for q in queue}, {}, {}
     for i in order:
@@ -759,6 +937,7 @@ def rank_program(g, core, T, topo):
         if o["tok"] is not None:
             if o["tok"][2]:
                 ins.then_inc(T.sem[o["tok"][0]], 16)
+            if o["tok"][1]:
                 o["own"] = o["tok"][:2]
         elif q != "p" or i in needed:
             s = semof[q]

from concourse.mybir import AluOpType as A, ActivationFunctionType as F

NC, CP = 4, 64
MAG = float(3 * 2 ** 18)
MAG1 = float(3 * 2 ** 22)
KOFF = 1535.5
ETA = 2.0 ** -22
BIGV = 131072.0
HOME, AWAY, WEND = 8, 8 + 1280, 8 + 1280 + 1024
INIT = [(0, 512), (512, 768)]
PARTS = {3: [[0, 1, 2, 3]], 4: [[0, 1, 2, 3]]}
NEWS = [[0, 1], [2, 3]]
GATHER_A, GATHER_A0, GATHER_AF = [1, 2, 3], [0, 1, 2, 3], [1, 2]
SPLIT = [0]
SUM_S = [3]
SUM_V = [2]
ROWS_V = [1, 2, 3]
FLOOR = ["PPPP", "PPPP", "PPPP", "PPPP", "PPPP", "PPPP"]
CYC, PCYC, PFIX, RLAT, RATE, SYNC = 0.0009, 0.00066, 0.0, 2.0, 200e3, 0.09

SCRATCH = {
    "r0i": ("sbuf", [128, 768], "int32"), "oppi": ("sbuf", [128, 48], "int32"), "mub": ("sbuf", [128, 8], "bfloat16"),
    "ocb": ("sbuf", [128, 1280], "bfloat16"), "stb": ("sbuf", [128, 1280], "bfloat16"), "stc": ("sbuf", [128, 1280], "bfloat16"),
    "r16": ("sbuf", [128, 768], "float16"), "l0": ("sbuf", [128, 768], "float16"),
    "W": ("sbuf", [128, WEND], "float32"), "ME": ("sbuf", [128, 256], "float32"),
    "tb": ("sbuf", [128, 128], "bfloat16"), "io2": ("sbuf", [128, 144], "bfloat16"), "kcol": ("sbuf", [128, 4], "int32"),
    "zs0": ("sbuf", [128, 48], "int32"), "zs": ("sbuf", [128, 48], "int32"), "k15": ("sbuf", [128, 4], "int32"),
    "kf": ("sbuf", [128, 8], "float32"),
    "TM": ("sbuf", [128, 2048], "bfloat16"), "BM": ("sbuf", [128, 144], "bfloat16"), "I1": ("sbuf", [128, 144], "bfloat16"),
    "I2": ("sbuf", [128, 128], "bfloat16"), "dn": ("sbuf", [128, 256], "float16"), "X": ("sbuf", [128, 1280], "float32"),
    "I32": ("sbuf", [128, 128], "float32"), "NM": ("sbuf", [128, 128], "float32"),
    "WD": ("sbuf", [128, 15 * 128], "bfloat16"), "WX": ("sbuf", [128, 9 * 128], "bfloat16"), "DG": ("sbuf", [128, 256], "bfloat16"),
    "wc": ("sbuf", [128, 32], "float32"), "PAT3": ("sbuf", [128, 256], "float32"), "PAT4": ("sbuf", [128, 320], "float32"),
    "CF": ("sbuf", [128, 9 * 256], "float32"), "CH": ("sbuf", [128, 9 * 256], "bfloat16"), "CL": ("sbuf", [128, 9 * 256], "float16"),
    "o16": ("sbuf", [128, 48], "float16"), "aw": ("sbuf", [128, 48], "bfloat16"),
    "a16": ("sbuf", [128, 48], "float16"), "IN": ("sbuf", [128, 128], "bfloat16"), "LW": ("sbuf", [128, 776], "float32"), "REP": ("sbuf", [128, 768], "float16"),
    "u1": ("sbuf", [128, 64], "uint16"), "OFF": ("sbuf", [128, 80], "uint16"), "OFN": ("sbuf", [128, 32], "uint16"),
    "CO": ("sbuf", [128, 64], "uint16"),
    "WT": ("sbuf", [128, 96], "bfloat16"), "WI": ("sbuf", [128, 48], "bfloat16"), "UI": ("sbuf", [128, 48], "float32"),
    "VI": ("sbuf", [128, 48], "float32"), "ZI": ("sbuf", [128, 48], "float32"), "SC": ("sbuf", [128, 96], "float32"),
    "ZZ": ("sbuf", [128, 64], "float32"), "ZB": ("sbuf", [128, 48], "float32"), "DZ": ("sbuf", [128, 64], "float32"),
    "MZ": ("sbuf", [128, 64], "float32"), "EE": ("sbuf", [128, 32], "float32"),
    "MP": ("sbuf", [128, 128], "bfloat16"), "OP": ("sbuf", [128, 48], "int32"),
    "sa": ("sbuf", [128, 48 * 24], "int32"), "sf": ("sbuf", [128, 48 * 12], "float32"), "Z": ("sbuf", [128, 96], "int32"),
    "TK": ("sbuf", [128, 1280], "float32"), "DS": ("sbuf", [128, 1280], "float32"), "LT": ("sbuf", [128, 1536], "bfloat16"),
    "TT": ("sbuf", [128, 1280], "bfloat16"), "TN": ("sbuf", [128, 256], "bfloat16"), "V": ("sbuf", [128, 1280], "float32"),
    "NT": ("sbuf", [128, 256], "float32"), "RN": ("sbuf", [128, 256], "float32"), "RH": ("sbuf", [128, 1280], "float32"),
    "YR": ("sbuf", [128, 1280], "float32"), "YO": ("sbuf", [128, 32], "float32"), "Y": ("sbuf", [128, 256], "float32"),
}
for _k in ("h0", "h1", "h2", "h3", "d0", "d1", "d2", "dx"):
    SCRATCH[_k] = ("psum", [128, 512], "float32")
for _k in range(6):
    SCRATCH["dl%d" % _k] = ("sbuf", [128, 256 * (4 + _k // 3)], "float16")
    SCRATCH["ld%d" % _k] = ("sbuf", [128, 256 * (4 + _k // 3)], "float16")
SEMAPHORES = ["sv", "sa", "sp", "sg", "ls", "l3"] + ["dm%d" % i for i in range(12)] + ["ar%d" % i for i in range(5 + 6 * NC)]

KEPT = {}
TWICE = [(3, 0), (3, 1)]
WFIX = 0.45
KEEP = 1
DIRECT = 1
CUT = 2
PASSES, SHAKES, SWAPS, SEED, SHAKE, SLACK, FIRST = 6, 700, 3000, 1, 0.7, 0.0, 3.5
PACES = [(0.87, 0.95), (1.25, 1.0), (0.95, 1.25)]


def _order(ops, marks):
    n = len(ops)
    pred = [sorted(o["deps"]) for o in ops]
    succ = [[] for o in ops]
    for i in range(n):
        for j in pred[i]:
            succ[j].append(i)

    def lag(a, b):
        if ops[a]["q"] == ops[b]["q"] and a not in ops[b]["hard"]:
            return 0.0
        return ops[a]["lat"] + (0.0 if ops[a]["q"] == "p" and ops[b]["q"] == "p" else SYNC)

    def place(seq, back):
        busy, end = {}, [0.0] * n
        for i in seq:
            o = ops[i]
            if back:
                t = max([end[j] + lag(i, j) for j in succ[i]] + [o["lat"]])
            else:
                t = max([end[j] + lag(j, i) for j in pred[i]] + [0.0])
            if o["q"] != "r":
                iv = busy.setdefault(o["q"], [])
                lo, hi = 0, len(iv)
                while lo < hi:
                    m = (lo + hi) // 2
                    if iv[m][1] <= t:
                        lo = m + 1
                    else:
                        hi = m
                while lo < len(iv) and iv[lo][0] < t + o["cost"] - 1e-9:
                    t = max(t, iv[lo][1])
                    lo += 1
                iv.insert(lo, (t, t + o["cost"]))
            end[i] = t + o["cost"]
        return end

    way = [0.0] * n
    for i in range(n - 1, -1, -1):
        way[i] = ops[i]["cost"] + max([way[j] + lag(i, j) for j in succ[i]] + [ops[i]["lat"]])
    best, seed = None, SEED
    for turn in range(PASSES):
        end = place(sorted(range(n), key=lambda i: (-way[i], i)), False)
        span = max(end[i] + ops[i]["lat"] for i in range(n))
        if best is None or span < best[0]:
            best = (span, sorted(range(n), key=lambda i: (end[i] - ops[i]["cost"], i)), list(way))
        way = place(sorted(range(n), key=lambda i: (-end[i], -i)), True)

    def run(w):
        w = list(w)
        for i in range(n - 1, -1, -1):
            for j in succ[i]:
                if w[j] + 1e-6 > w[i]:
                    w[i] = w[j] + 1e-6
        end = place(sorted(range(n), key=lambda i: (-w[i], i)), False)
        t = [0.0] + [end[i] for i in marks] + [max(end[i] + ops[i]["lat"] for i in range(n))]
        return w, end, t

    way, end, t = run(best[2])
    for turn in range(SHAKES):
        part = [sum(1 for m in t[1:-1] if m < end[i]) for i in range(n)]
        new = list(way)
        for i in range(n):
            seed = (seed * 1103515245 + 12345) % 2147483648
            if seed % 1024 < 200:
                new[i] += SHAKE * (seed / 1073741824 - 1.0)
        new, e2, t2 = run(new)
        back = place(sorted(range(n), key=lambda i: (-e2[i], -i)), True)
        shift = max(way) - max(back)
        new, e2, t2 = run([b + shift for b in back])
        if t2[-1] < t[-1]:
            way, end, t = new, e2, t2
            continue
        good = [t2[p + 1] - t2[p] < t[p + 1] - t[p] - 1e-9 for p in range(len(t) - 1)]
        if any(good):
            w3, e3, t3 = run([new[i] if good[part[i]] else way[i] for i in range(n)])
            if t3[-1] < t[-1]:
                way, end, t = w3, e3, t3
    order = sorted(range(n), key=lambda i: (end[i] - ops[i]["cost"], i))

    qs = [o["q"] for o in ops]
    pl = [[(j, lag(j, i)) for j in pred[i]] for i in range(n)]
    lat = [o["lat"] for o in ops]
    costs = [[o["cost"] * p if o["q"] == "p" else 0.05 + (o["cost"] - 0.05) * v if o["q"] in "va" and o["cost"] < 1.2 and not o["lat"]
              else o["cost"] for o in ops] for p, v in PACES]

    def replay(seq, cost):
        free, end, why, top, who = {}, [0.0] * n, [-1] * n, 0.0, 0
        for i in seq:
            t, w = 0.0, -1
            for j, l in pl[i]:
                e = end[j] + l
                if e > t:
                    t, w = e, j
            q = qs[i]
            if q != "r":
                j = free.get(q, -1)
                if j >= 0 and end[j] > t:
                    t, w = end[j], j
                free[q] = i
            t += cost[i]
            end[i], why[i] = t, w
            if t + lat[i] > top:
                top, who = t + lat[i], i
        return top, why, who, end

    def ahead(seq, p0, p1, cost, old):
        end, free = list(old), {}
        for p in range(p0 - 1, -1, -1):
            free.setdefault(qs[seq[p]], end[seq[p]])
            if len(free) == 6 or p < p0 - 300:
                break
        top = 0.0
        for p in range(p0, p1 + 1):
            i = seq[p]
            q = qs[i]
            t = free.get(q, 0.0) if q != "r" else 0.0
            for j, l in pl[i]:
                e = end[j] + l
                if e > t:
                    t = e
            t += cost[i]
            end[i] = free[q] = t
            if t + lat[i] > top:
                top = t + lat[i]
        return top if p1 == n - 1 else t

    def swaps(res):
        found = []
        for top, why, i, end in res:
            while why[i] >= 0:
                if qs[why[i]] == qs[i] and why[i] not in ops[i]["deps"]:
                    found.append((why[i], i))
                i = why[i]
        return found

    res = [replay(order, c) for c in costs]
    now, moves = sum(r[0] for r in res), swaps(res)
    best = (now, order, res)
    for turn in range(SWAPS):
        seed = (seed * 1103515245 + 12345) % 2147483648
        a, b = moves[(seed >> 8) % len(moves)]
        seed = (seed * 1103515245 + 12345) % 2147483648
        pa, pb = order.index(a), order.index(b)
        early = seed >> 20 & 1
        for step in range((seed >> 12) % 4):
            if early:
                pa = max([p for p in range(max(0, pa - 40), pa) if qs[order[p]] == qs[a]] or [pa])
            else:
                pb = min([p for p in range(pb + 1, min(n, pb + 40)) if qs[order[p]] == qs[a]] or [pb])
        mid = order[pa:pb + 1]
        if early:
            go = {b}
            for i in reversed(mid):
                if any(j in go for j in succ[i]):
                    go.add(i)
            mid = [i for i in mid if i in go] + [i for i in mid if i not in go]
        else:
            go = {a}
            for i in mid:
                if any(j in go for j in pred[i]):
                    go.add(i)
            mid = [i for i in mid if i not in go] + [i for i in mid if i in go]
        new = order[:pa] + mid + order[pb + 1:]
        slack = SLACK * (1.0 - turn / SWAPS) ** 2 + 1e-9
        later = sorted(p for p in [order.index(m) for m in marks] if p > pb)
        p1 = later[0] if later else n - 1
        worse = 0.0
        for c, x in zip(costs, res):
            worse += ahead(new, pa, p1, c, x[3]) - (x[3][order[p1]] if later else x[0])
            if worse > slack + 0.2:
                break
        if worse > slack:
            continue
        r = [replay(new, c) for c in costs]
        if sum(x[0] for x in r) <= now + slack:
            order, res, now = new, r, sum(x[0] for x in r)
            moves = swaps(res)
            if now < best[0]:
                best = (now, order, res)
    KEPT["span"] = best[2][0][0]
    return best[1]


def rank_program(g, core, T, topo):
    rank = T.rank_of(core)
    if rank is None:
        return
    n = len(T.cores)
    prev, nxt = T.cores[(rank - 1) % n], T.cores[(rank + 1) % n]
    nfar, ncome = len(topo.engines(core, prev)), len(topo.engines(nxt, core))
    rid, pid = topo.addr(prev, core)

    ops, lastw, readers, banks = [], {}, {}, {}
    ndma, nsent, sent, marks = [0], [0], [], []

    def add(q, fn, r=(), w=(), x=(), tok=None, cost=0.1, lat=0.0, after=()):
        i = len(ops)
        deps = set()
        for k in r:
            if k in lastw:
                deps.add(lastw[k])
        for k in w:
            if k in lastw:
                deps.add(lastw[k])
            deps.update(readers.get(k, ()))
        for k in x:
            fills = q != "p" and (not w or w[0][:2] in ("XM", "CP", "PS", "PT"))
            deps.update(j for e, j in banks.setdefault(k, {}).items() if e != q or fills)
            after = list(after) + [j for e, j in banks[k].items() if e == q]
        for k in r:
            readers.setdefault(k, []).append(i)
        for k in w:
            lastw[k] = i
            readers[k] = []
        for k in x:
            banks[k][q] = i
        ops.append({"q": q, "fn": fn, "hard": deps, "deps": deps | set(after), "tok": tok, "cost": cost, "lat": lat})
        return i

    def cy(out, k=1.0):
        return 0.05 + max(64, out.shape[1] * k) * CYC

    def ts(out, in0, s1, op0, s2=None, op1=None, r=(), w=(), x=(), k=1.0):
        if op1 is None:
            add("v", lambda: g.vector.tensor_scalar(out, in0, s1, None, op0), r, w, x, cost=cy(out, k))
        else:
            add("v", lambda: g.vector.tensor_scalar(out, in0, s1, s2, op0, op1), r, w, x, cost=cy(out, k))

    def tt(out, in0, in1, op, r=(), w=(), x=(), k=None):
        add("v", lambda: g.vector.tensor_tensor(out, in0, in1, op), r, w, x, cost=cy(out, k or (1.0 if x else 2.0)))

    def cp(out, in_, r=(), w=(), x=(), k=1.0):
        add("v", lambda: g.vector.tensor_copy(out, in_), r, w, x, cost=cy(out, k))

    def ms(out, val, w, k=1.0):
        add("v", lambda: g.vector.memset(out, val), (), w, cost=cy(out, k))

    def act(out, in_, func=F.Identity, bias=0.0, scale=1.0, r=(), w=(), x=(), more=0.0):
        add("a", lambda: g.scalar.activation(out, in_, func, bias=bias, scale=scale), r, w, x, cost=cy(out) + 0.03 + more)

    def mm(out, lhs, rhs, start, stop, r=(), x=(), k=1.0):
        add("p", lambda: g.tensor.matmul(out, lhs, rhs, start, stop), r, (), x, cost=PFIX + max(64, out.shape[1]) * k * PCYC)

    def dma(q, out, in_, r=(), w=(), lat=2.2):
        s = "dm%d" % ndma[0]
        ndma[0] += 1
        eng = g.sync if q == "s" else g.scalar
        add(q, lambda: eng.dma_start(out, in_), r, w, (), (s, 16, True), cost=0.1, lat=lat)

    def iota(out, pat, cm, key, small):
        if small:
            add("g", lambda: g.iota(out, pat, 0, cm, allow_small_or_imprecise_dtypes=True), (), [key], cost=0.13 + 2 * out.shape[1] * CYC)
        else:
            add("g", lambda: g.iota(out, pat, 0, cm), (), [key], cost=0.13 + 2 * out.shape[1] * CYC)

    def send(dst, src, keys, width, again=False):
        i = len(sent)
        local = "l3" if again else "ls"
        if not again:
            nsent[0] += nfar
        sent.append(add("g", lambda: g.remote_dma(dst, src, T.sem["ar%d" % i], T.sem[local], pid, rid, topo.mask(core, prev)),
                        keys, (), (), (local, nfar if again else 0, False), cost=FIRST if i == 0 else WFIX + width * 128 / RATE,
                        lat=RLAT, after=sent[-1:]))
        return i

    def arrive(i, keys):
        add("r", None, (), keys, (), ("ar%d" % i, ncome, False), cost=0.0, after=[sent[i]])

    W = T.W
    HK = ["WH%d" % c for c in range(NC)]
    AK = ["WA%d" % c for c in range(NC)]
    MEK = ["ME%d" % c for c in range(NC)]
    WNK = ["WN%d_%d" % (f, c) for f in (3, 4) for c in range(NC)]
    WIN = {3: (W[:, 0:AWAY + 768], HK + AK + WNK + ["WB"]), 4: (W[:, 0:WEND], HK + AK + WNK + ["WB", "WL"])}
    HB = ["h0", "h1", "h2", "h3"]
    DB = ["d0", "d1", "d2", "dx"]
    I1 = T.I1[:, 0:128]
    MP, MN = T.MP[:, 0:64], T.MP[:, 64:128]

    def wcols(base, c, lo, hi):
        return W[:, base + 256 * lo + c:base + 256 * hi:4]

    def hreg(c, s, m=1):
        return T[HB[c]][:, 64 * s:64 * (s + m)]

    def si(j, m=48):
        return T.sa[:, 48 * j:48 * j + m]

    def sfl(j, m=48, o=0):
        return T.sf[:, 48 * j + o:48 * j + o + m]

    def wd(s, t):
        j = s * (s + 1) // 2 + t
        return T.WD[:, 128 * j:128 * j + 128], ("WD%d" if t == s else "WR%d") % s

    def wx(f, t):
        j = 4 * (f - 3) + t
        return T.WX[:, 128 * j:128 * j + 128], "WX%d" % f

    def dg(f):
        return T.DG[:, 128 * (f - 3):128 * (f - 2)], "DG%d" % f

    def weights(s):
        j = s * (s + 1) // 2
        act(T.WD[:, 128 * (j + s):128 * (j + s + 1)], I1, scale=0.0625, r=["I1"], w=["WD%d" % s])
        if s:
            o, i, r = T.WD[:, 128 * j:128 * (j + s)], T.WD[:, 128 * (j - s):128 * j], ["WR%d" % (s - 1), "WD%d" % (s - 1), "wa"]
            if s in ROWS_V:
                ts(o, i, T.wc[:, s - 1:s], A.mult, r=r, w=["WR%d" % s], k=0.5)
            else:
                act(o, i, scale=T.wc[:, s - 1:s], r=r, w=["WR%d" % s])
        if s >= 3 and not KEEP:
            act(dg(s)[0], I1, scale=T.wc[:, 3 + s:4 + s], r=["I1", "wa"], w=[dg(s)[1]])
            o, i, r = T.WX[:, 512 * (s - 3):512 * (s - 3) + 128 * (s + 1)], T.WD[:, 128 * j:128 * (j + s + 1)], ["WR%d" % s, "WD%d" % s, "wa"]
            if s in ROWS_V:
                ts(o, i, T.wc[:, 3 + s:4 + s], A.mult, r=r, w=["WX%d" % s], k=0.5)
            else:
                act(o, i, scale=T.wc[:, 3 + s:4 + s], r=r, w=["WX%d" % s])

    def lookup_list(src, rk, col, ck, m, c0, away, ak):
        ts(T.u1[:, c0:c0 + m], src, 768.0, A.min, r=[rk], w=["u1"])
        tt(T.a16[:, 0:m], away, col, A.mult, [ak, ck], ["a16"])

    def lookup_gather(m, c0, bank):
        cp(T.REP[:, 0:16 * m], T.LW[:, :].indirect(T.u1[:, c0:c0 + m]), ["LW0", "LW1", "LWZ", "u1"], ["REP"], k=1.5)
        mm(T[bank][:, 0:m], I1, T.a16[:, 0:m], True, False, ["I1", "a16"], [bank])
        for r in range(16):
            mm(T[bank][:, 0:m], T.BM[:, 15 - r:143 - r], T.REP[:, r:16 * m:16], False, r == 15, ["BM", "REP"], [bank])

    def lookup_finish(m, c0, bank):
        cp(si(4, m), T[bank][:, 0:m], w=["sa4"], x=[bank])
        ts(T.Z[:, c0:c0 + m], si(4, m), 0x4FF, A.bitwise_and, r=["sa4"], w=["Z%d" % c0])
        tt(sfl(4, m), T.Z[:, c0:c0 + m], T.zs[:, 0:m], A.is_equal, ["Z%d" % c0, "zs"], ["sf4"])
        ts(sfl(5, m), sfl(4, m), -4096.0, A.mult, float(HOME), A.add, ["sf4"], ["sf5"])
        tt(sfl(6, m), sfl(5, m), si(4, m), A.add, ["sf5", "sa4"], ["sf6"])
        cp(T.CO[:, c0:c0 + m], sfl(6, m), ["sf6"], ["CO%d" % c0])

    def player_columns(m, c0):
        ts(sfl(9, m), T.Z[:, c0:c0 + m], 1024.0, A.is_ge, 256.0, A.mult, ["Z%d" % c0], ["sf9"])
        tt(T.ZZ[:, c0:c0 + m], sfl(9, m), T.Z[:, c0:c0 + m], A.add, ["sf9", "Z%d" % c0], ["ZZ%d" % c0])

    BK = KOFF - 15.0 / 512

    def cplace(f, s, c0=0, c1=NC):
        o, m = 1024 * (f - 3), f + KEEP
        if s == m:
            return slice(o + 256 * f + 64 * c0, o + 256 * f + 64 * c1)
        return slice(o + 64 * m * c0 + m - 1 - s, o + 64 * m * c1, m)

    def ckey(f, s):
        return "%d_%d" % (f, s)

    def const_again(s):
        if DIRECT:
            act(T.CF[:, cplace(4, s)], T.CF[:, cplace(3, s)], r=["CH" + ckey(3, s)], w=["CH" + ckey(4, s)])
            return
        act(T.CH[:, cplace(4, s)], T.CH[:, cplace(3, s)], r=["CH" + ckey(3, s)], w=["CH" + ckey(4, s)])
        cp(T.CL[:, cplace(4, s)], T.CL[:, cplace(3, s)], ["CL" + ckey(3, s)], ["CL" + ckey(4, s)], k=0.5)

    def const(f, s, bank):
        bias = BK if s == f else T.wc[:, 16 + s:17 + s]
        cs, p, key = cplace(f, s), T[bank][:, 0:256], ckey(f, s)
        for t in range(s + 1):
            m, k = wd(s, t)
            mm(p, m, T.ocb[:, 256 * t:256 * t + 256], t == 0, t == s, [k, "ocb"], [bank])
        if DIRECT:
            act(T.CF[:, cs], p, bias=bias, r=["wk"], w=["CH" + key], x=[bank])
            return
        if (f, s) in TWICE:
            act(T.CH[:, cs], p, bias=bias, r=["wk"], w=["CH" + key], x=[bank])
            p = T[bank][:, 256:512]
            for t in range(s + 1):
                m, k = wd(s, t)
                mm(p, m, T.ocb[:, 256 * t:256 * t + 256], t == 0, False, [k, "ocb"], [bank])
            mm(p, T.IN[:, :], T.CH[:, cs], False, True, ["IN", "CH" + key], [bank])
            ts(T.CL[:, cs], p, bias, A.add, r=["wk"], w=["CL" + key], x=[bank])
            return
        act(p, p, bias=bias, r=["wk"], w=["CP" + key], x=[bank])
        act(T.CH[:, cs], p, r=["CP" + key], w=["CH" + key], x=[bank])
        tt(T.CL[:, cs], p, T.CH[:, cs], A.subtract, ["CH" + key], ["CL" + key], [bank])

    def dreg(c, f, s):
        m = f + KEEP
        return T[DB[c]][:, m - 1 - s:64 * m:m] if s < m else T[DB[c]][:, 64 * f:64 * f + 64]

    def preload(c, k):
        f = 3 + k // 3
        m = 64 * (f + KEEP)
        a0 = 1024 * (f - 3) + m * c
        if DIRECT:
            mm(T[DB[c]][:, 0:m], I1, T.ocb[:, 0:m], True, False, ["I1", "ocb"], [DB[c]])
            act(T[DB[c]][:, 0:m], T.CF[:, a0:a0 + m], r=["CH" + ckey(f, s) for s in range(f + KEEP)], x=[DB[c]])
            if FLOOR[k][c] == "H":
                mm(dreg(c, f, 0), I1, MP, False, False, ["I1", "MP"], [DB[c]])
            return
        mm(T[DB[c]][:, 0:m], I1, T.CH[:, a0:a0 + m], True, False, ["I1"] + ["CH" + ckey(f, s) for s in range(f + KEEP)], [DB[c]])
        mm(T[DB[c]][:, 0:m], I1, T.CL[:, a0:a0 + m], False, False, ["I1"] + ["CL" + ckey(f, s) for s in range(f + KEEP)], [DB[c]])
        if FLOOR[k][c] != "P" and not KEEP:
            cs = cplace(f, f, c, c + 1)
            mm(dreg(c, f, f), I1, T.CH[:, cs], False, False, ["I1", "CH" + ckey(f, f)], [DB[c]])
            mm(dreg(c, f, f), I1, T.CL[:, cs], False, False, ["I1", "CL" + ckey(f, f)], [DB[c]])
        if FLOOR[k][c] == "H":
            mm(dreg(c, f, 0), I1, MP, False, False, ["I1", "MP"], [DB[c]])

    def gather(out, ok, c, lo, hi, wf, scalar):
        b = 320 * c
        win, wk = WIN[wf]
        r = wk + ["OFF"] + ["OFF%d_%d" % (s, c) for s in range(max(lo, 3), hi)]
        q, w = win.indirect(T.OFF[:, 20 * c + 4 * lo:20 * c + 4 * hi]), [ok + "%d_%d" % (c, s) for s in range(lo, hi)]
        o = out[:, b + 64 * lo:b + 64 * hi]
        if scalar:
            qb = T.V[:, b + 64 * lo:b + 64 * hi]
            act(qb, q, r=r, w=["V%d_%d" % (c, lo)], more=32 * (hi - lo) * CYC)
            tt(o, qb, hreg(c, lo, hi - lo), A.subtract, ["V%d_%d" % (c, lo)], w, [HB[c]])
        else:
            tt(o, q, T.RH[:, b + 64 * lo:b + 64 * hi], A.subtract, r + ["RH%d" % c], w, k=1.5)

    def limit(v, keys):
        ts(v, v, 256.0, A.min, -256.0, A.max, keys, keys, k=0.5)

    def half_sum(bank, f):
        act(T.NT[:, :], T[bank][:, 0:256], bias=-0.25, scale=0.5, w=["NT"], x=[bank])
        ts(T.RN[:, :], T.NT[:, :], MAG1, A.add, -MAG1, A.add, ["NT"], ["RN"])

    def newest(f):
        for c in range(NC):
            act(T.ME[:, 64 * c:64 * c + 64], wcols(HOME, c, f - 1, f), r=[HK[c]], w=[MEK[c]])

    NEXT = [(I1, "I1"), (T.I1[:, 16:144], "I1"), (T.I2[:, :], "I2")]

    dma("s", T.r0i[:, 0:256], T.r0[:, 0:256], w=["r0_0"], lat=2.2)
    dma("a", T.oppi[:, :], T.opp[:, :], w=["opp"], lat=2.3)
    dma("s", T.r0i[:, 256:768], T.r0[:, 256:768], w=["r0_1", "r0_2"], lat=2.8)
    dma("a", T.mub[:, :], T.mu[:, :], w=["mu"], lat=2.4)
    dma("s", T.ocb[:, :], T.oc[:, :], w=["ocb"], lat=3.5)
    dma("s", T.stb[:, :], T.stake[:, :], w=["stb"], lat=4.2)
    iota(T.tb[:, :], [[-16, 8], [0, 16]], 1, "tb", True)
    iota(T.io2[:, :], [[1, 144]], -1, "io2", True)
    iota(T.kcol[:, :], [[0, 4]], 1, "kcol", False)
    iota(T.zs0[:, :], [[0, 3], [1, 4], [64, 4]], 0, "zs0", False)
    ms(W[:, HOME + 768:AWAY], 0.0, WNK)
    for f in (3, 4):
        ms(T["PAT%d" % f][:, 0:64 * (f + KEEP):f + KEEP], ETA, ["PAT%d_0" % f])
    act(W[:, 0:HOME], T.tb[:, 0:HOME], scale=0.0, bias=BIGV, r=["tb"], w=["WB"])
    act(MP, T.tb[:, 0:64], scale=0.0, bias=MAG, r=["tb"], w=["MP"])
    act(MN, T.tb[:, 0:64], scale=0.0, bias=-MAG, r=["tb"], w=["MN"])
    act(T.WI[:, 0:48:3], T.tb[:, 0:16], scale=0.0, bias=1.0, r=["tb"], w=["WI0"])
    for r in range(16):
        ts(T.TM[:, 128 * r:128 * r + 128], T.tb[:, :], float(r), A.is_equal, r=["tb"], w=["TM%d" % r], k=0.5)
    ts(T.I1[:, :], T.io2[:, :], 0.0, A.is_equal, r=["io2"], w=["I1"], k=0.5)
    if not DIRECT:
        act(T.IN[:, :], I1, scale=-1.0, r=["I1"], w=["IN"])
    act(T.LW[:, 768:776], T.tb[:, 0:8], scale=0.0, r=["tb"], w=["LWZ"])
    for i, s in enumerate((0, 2)):
        cp(T.r16[:, 256 * i:256 * i + 256], T.r0i[:, 256 * s:256 * s + 256], ["r0_%d" % s], ["r16_%d" % i])
    for c in range(NC):
        cp(T.r16[:, 512 + c:768:4], T.r0i[:, 256 + 64 * c:320 + 64 * c], ["r0_1"], ["r16_2%d" % c])
    R16 = [["r16_0"], ["r16_1"], ["r16_2%d" % c for c in range(NC)]]
    first_msgs = [send(T.l0[:, a:b], T.r16[:, a:b], [k for s in range(a // 256, b // 256) for k in R16[s]], 2 * (b - a)) for a, b in INIT]
    src = T.oppi[:, :]
    ts(si(12), src, 63, A.bitwise_and, r=["opp"], w=["sa12"])
    ts(si(13), src, 6, A.logical_shift_right, 3, A.bitwise_and, ["opp"], ["sa13"])
    ts(si(15), src, 0x700, A.bitwise_and, r=["opp"], w=["sa15"])
    ts(si(14), si(12), 4.0, A.mult, r=["sa12"], w=["sa14"])
    tt(si(16), si(14), si(13), A.add, ["sa14", "sa13"], ["sa16"])
    tt(T.o16[:, :], si(15), si(16), A.add, ["sa15", "sa16"], ["o16"])
    ts(T.aw[:, :], src, 1024.0, A.is_ge, r=["opp"], w=["aw"])
    for h in range(2):
        for r in range(16):
            mm(T[DB[h]][:, r:384:16], T.TM[:, 128 * r:128 * r + 128], T.o16[:, 24 * h:24 * h + 24], r == 0, r == 15, ["TM%d" % r, "o16"], [DB[h]])
        act(T.LW[:, 384 * h:384 * h + 384], T[DB[h]][:, 0:384], w=["LW%d" % h], x=[DB[h]])
    lookup_list(src, "opp", T.o16[:, :], "o16", 48, 0, T.aw[:, :], "aw")
    for c in range(NC):
        for s in range(5):
            o = 16 * (s % 3) + 4 * c
            mm(T.d2[:, 20 * c + 4 * s:20 * c + 4 * s + 4], I1, T.o16[:, o:o + 4], c + s == 0, c + s == 7, ["I1", "o16"], ["d2"])
    ts(T.OFF[:, :], T.d2[:, 0:80], float(HOME), A.add, w=["OFF"] + ["OFF%d_%d" % (s, c) for s in (3, 4) for c in range(NC)], x=["d2"])
    ts(T.k15[:, 0:1], T.kcol[:, 0:1], 15, A.bitwise_and, r=["kcol"], w=["k15"])
    ts(T.I2[:, :], T.io2[:, 16:144], 128.0, A.is_equal, r=["io2"], w=["I2"], k=0.5)
    ts(T.kf[:, 0:1], T.k15[:, 0:1], -1.0, A.mult, 15.0, A.add, ["k15"], ["kf0"])
    ts(T.kf[:, 1:2], T.k15[:, 0:1], 4.0, A.mult, r=["k15"], w=["kf1"])
    ts(T.BM[:, :], T.io2[:, :], T.kf[:, 0:1], A.is_equal, 0.0625, A.mult, ["io2", "kf0"], ["BM"], k=0.5)
    ts(T.zs[:, :], T.zs0[:, :], T.kf[:, 1:2], A.add, r=["zs0", "kf1"], w=["zs"])
    act(T.wc[:, 0:8], T.mub[:, 0:8], scale=0.5, r=["mu"], w=["wa"])
    act(T.wc[:, 16:17], T.mub[:, 4:5], scale=-KOFF / 2, bias=KOFF, r=["mu"], w=["wk0"])
    act(T.wc[:, 17:20], T.mub[:, 5:8], scale=-KOFF / 2, bias=BK, r=["mu", "wk0"], w=["wk"])
    act(T.wc[:, 20:24], T.mub[:, 4:8], scale=0.5, bias=ETA, r=["mu"], w=["wce"])
    if not KEEP:
        act(T.wc[:, 24:26], T.mub[:, 6:8], scale=-MAG / 2, r=["mu"], w=["wm"])
    for s in range(4):
        weights(s)
    for c in range(NC):
        for i in range(2):
            mm(hreg(c, 2 * i), I1, T.r16[:, 256 * i + 64 * c:256 * i + 64 * c + 64], i == 0, False, ["I1", "r16_%d" % i], [HB[c]])
        mm(hreg(c, 1), I1, T.r16[:, 512 + c:768:4], False, True, ["I1", "r16_2%d" % c], [HB[c]])
        act(wcols(HOME, c, 0, 3), hreg(c, 0, 3), w=[HK[c]], x=[HB[c]])
        if c not in GATHER_A0:
            act(T.RH[:, 320 * c:320 * c + 192], hreg(c, 0, 3), w=["RH%d" % c], x=[HB[c]])
    for i, (m, k) in enumerate(NEXT):
        mm(T.dx[:, 0:256], m, T.r16[:, 256:512], i == 0, i == 2, [k] + R16[1], ["dx"])
    half_sum("dx", 3)
    const(3, 0, "d0")
    const(3, 1, "d1")
    lookup_gather(48, 0, "d2")
    const(3, 2, "d0")
    const(3, 3, "d1")
    lookup_finish(48, 0, "d2")
    tt(sfl(7, 16), si(16, 16), T.Z[:, 0:16], A.subtract, ["sa16", "Z0"], ["sf7"])
    tt(sfl(8, 16), sfl(7, 16), sfl(4, 16), A.mult, ["sf7", "sf4"], ["sf8"])
    tt(T.Z[:, 0:16], sfl(8, 16), T.Z[:, 0:16], A.add, ["sf8", "Z0"], ["Z0"])
    player_columns(48, 0)
    for j in range(3):
        act(T.ZI[:, j:48:3], T.ZZ[:, 16 * j:16 * j + 16], bias=HOME + 512.0, r=["ZZ0"], w=["ZI%d" % j])

    def pattern(f):
        m = f + KEEP
        for j in range(1, m):
            s = m - 1 - j
            act(T["PAT%d" % f][:, j:64 * m:m], T.io2[:, 0:64], bias=T.wc[:, 20 + s:21 + s], scale=0.0, r=["io2", "wce"], w=["PAT%d_%d" % (f, j)])

    pattern(3)
    for i, (a, b) in zip(first_msgs, INIT):
        arrive(i, ["l0_%d" % s for s in range(a // 256, b // 256)])
        for s in range(a // 256, b // 256):
            o = W[:, AWAY + 256 * (2 * s % 3):AWAY + 256 * (2 * s % 3) + 256]
            if s == 2:
                cp(o, T.l0[:, 512:768], ["l0_2"], ["WI%d_" % s])
                continue
            for c in range(NC):
                mm(T.dx[:, c:256:4], I1, T.l0[:, 256 * s + 64 * c:256 * s + 64 * c + 64], c == 0, c == NC - 1, ["I1", "l0_%d" % s], ["dx"])
            act(o, T.dx[:, 0:256], w=["WI%d_" % s], x=["dx"])
    for wf in WIN:
        WIN[wf][1].extend(["WI0_", "WI1_", "WI2_"])

    def part1(f):
        win, wk = WIN[3]
        npair = f * (f - 1) // 2
        many = len(PARTS[f]) > 1
        zo = 48 * (f - 3)
        for h, cs in enumerate(PARTS[f]):
            p0, nn = 64 * cs[0], 64 * len(cs)
            m, j0, base, tag = nn // 16, p0 // 16, f * p0, "_%d" % h
            place = [(DB[h], nn * k) if many else (DB[k // 2], nn * (k % 2)) for k in range(f - 1)]
            for k in range(f):
                tk = T.TK[:, base + nn * k:base + nn * (k + 1)]
                tt(tk, win.indirect(T.CO[:, 16 * k + j0:16 * k + j0 + m]), T.ME[:, p0:p0 + nn] if f == 4 else T.r16[:, 256 + p0:256 + p0 + nn],
                   A.subtract, wk + ["CO48" if k == 3 else "CO0"] + ([MEK[c] for c in cs] if f == 4 else R16[1]), ["TK%d" % k + tag], k=1.5)
                if k < f - 1:
                    b, o = place[k]
                    act(T[b][:, o:o + nn], tk, F.Abs, r=["TK%d" % k + tag], x=[b])
                if k > 0:
                    act(T.DS[:, base + nn * k:base + nn * (k + 1)], tk, F.Abs, r=["TK%d" % k + tag], w=["DS%d" % k + tag])
            lb = npair * p0
            for i, (k, j) in enumerate([(1, 0), (2, 1), (2, 0), (3, 0), (3, 1), (3, 2)][:npair]):
                b, o = place[j]
                tt(T.LT[:, lb + nn * i:lb + nn * (i + 1)], T.DS[:, base + nn * k:base + nn * (k + 1)], T[b][:, o:o + nn],
                   A.is_lt, ["DS%d" % k + tag], ["LT%d" % i + tag], [b])
                if i % 3 == 2:
                    b, o = DB[2 + i // 3], lb + nn * (i - 2)
                    for r in range(16):
                        mm(T[b][:, 0:3 * m], T.BM[:, 15 - r:143 - r], T.LT[:, o + r:o + 3 * nn:16], r == 0, r == 15,
                           ["BM"] + ["LT%d" % q + tag for q in range(i - 2, i + 1)], [b])
            wo = 6 * j0

            def wt(i, k=1):
                return T.WT[:, wo + m * i:wo + m * (i + k)]

            def tri(buf, k):
                return buf[:, 3 * j0 + k:3 * (j0 + m):3]

            w10, w21, w20 = wt(0), wt(1), wt(2)
            e0, e1 = T.EE[:, j0:j0 + m], T.EE[:, 16 + j0:16 + j0 + m]
            ts(wt(0, 3), T.d2[:, 0:3 * m], 9.0 / 16, A.is_ge, w=["wt" + tag], x=["d2"])
            act(tri(T.WI, 1), w10, r=["wt" + tag], w=["WI1" + tag])
            tt(e0, w21, w20, A.subtract, ["wt" + tag], ["e0" + tag])
            tt(e1, e0, w10, A.mult, ["e0" + tag, "wt" + tag], ["e1" + tag])
            tt(tri(T.WI, 2), e1, w20, A.add, ["e1" + tag, "wt" + tag], ["WI2" + tag])
            zk = ["ZI%d" % j for j in range(3)]
            if f == 4:
                ts(wt(3, 3), T.dx[:, 0:3 * m], 9.0 / 16, A.is_ge, w=["wu" + tag], x=["dx"])
                tt(T.MZ[:, 3 * j0:3 * (j0 + m)], wt(3, 3), T.DZ[:, 3 * j0:3 * (j0 + m)], A.mult, ["wu" + tag, "DZ" + tag], ["MZ" + tag])
                for k in range(3):
                    tt(tri(T.ZI, k), T.MZ[:, 3 * j0 + m * k:3 * j0 + m * (k + 1)], T.ZB[:, 16 * k + j0:16 * k + j0 + m], A.add,
                       ["MZ" + tag, "ZB", "SC3"], ["ZJ%d" % k + tag])
                zk = ["ZJ%d" % k + tag for k in range(3)]
            a0, a1 = 3 * j0, 3 * (j0 + m)
            wi = ["WI0", "WI1" + tag, "WI2" + tag]
            act(T.UI[:, a0:a1], T.WI[:, a0:a1], scale=-1.0, bias=1.0, r=wi, w=["UI" + tag])
            tt(T.VI[:, a0:a1], T.WI[:, a0:a1], T.ZI[:, a0:a1], A.mult, wi + zk, ["VI" + tag], k=1.0)
            add("v", lambda a0=a0, a1=a1: g.vector.tensor_tensor_scan(T.SC[:, zo + a0:zo + a1], T.UI[:, a0:a1], T.VI[:, a0:a1], 0.0, A.mult, A.add),
                ["UI" + tag, "VI" + tag], ["SC%d_%d" % (f, c) for c in cs] + ["SC%d" % f], cost=0.11)
            o = 16 * (f - 3) + j0
            cp(T.OFN[:, o:o + m], T.SC[:, zo + a0 + 2:zo + a1:3], ["SC%d_%d" % (f, c) for c in cs], ["OFN%d" % c for c in cs])
        for c in range(NC):
            preload(c, 3 * (f - 3))
            gather(T.TT, "TT", c, 0, f, 3, c in GATHER_A0)
            limit(T.TT[:, 320 * c:320 * c + 64 * f], ["TT%d_%d" % (c, s) for s in range(f)])
        for cs in NEWS:
            p0, p1, o = 64 * cs[0], 64 * cs[-1] + 64, 16 * (f - 3)
            tt(T.TN[:, p0:p1], WIN[f][0].indirect(T.OFN[:, o + p0 // 16:o + p1 // 16]), T.RN[:, p0:p1], A.subtract,
               WIN[f][1] + ["OFN%d" % c for c in cs] + ["RN"], ["TN%d" % c for c in cs], k=1.5)
            limit(T.TN[:, p0:p1], ["TN%d" % c for c in cs])
        for c in range(NC):
            act(wcols(HOME, c, f, f + 1), T.RN[:, 64 * c:64 * c + 64], r=["RN"], w=["WN%d_%d" % (f, c)])
        return T.SC[:, zo + 2:zo + 48:3], ["SC%d_%d" % (f, c) for c in range(NC)]

    def node_numbers(f, z, zk):
        zo = 48 * (f - 3)
        for c in range(NC):
            cp(T.OFF[:, 20 * c + 4 * f:20 * c + 4 * f + 4], T.SC[:, zo + 12 * c + 2:zo + 12 * c + 12:3], zk, ["OFF%d_%d" % (f, c)])
        ts(si(19, 16), z, -(HOME + 256.0 * (f - 1)), A.add, r=zk, w=["sa19"])
        ts(si(21, 16), si(19, 16), 2, A.logical_shift_right, 63, A.bitwise_and, ["sa19"], ["sa21"])
        ts(si(22, 16), si(19, 16), 3, A.bitwise_and, r=["sa19"], w=["sa22"])
        ts(si(23, 16), si(19, 16), 1280.0, A.is_ge, 1280.0, A.mult, ["sa19"], ["sa23"])
        ts(si(8, 16), si(22, 16), 64.0, A.mult, 256.0 * (f - 1), A.add, ["sa22"], ["sa8"])
        tt(si(6, 16), si(21, 16), si(23, 16), A.add, ["sa21", "sa23"], ["sa6"])
        if f == 3:
            tt(si(20, 16), si(6, 16), si(8, 16), A.add, ["sa6", "sa8"], ["sa20"])
        tt(T.YO[:, 16 * (f - 3):16 * (f - 2)], si(6, 16), si(8, 16), A.add, ["sa6", "sa8"], ["YO%d" % f])

    def sweep(k, idle):
        f = 3 + k // 3
        first, last = k % 3 == 0, k % 3 == 2
        ns = f + KEEP
        nn = 64 * ns
        dl, ld = T["dl%d" % k], T["ld%d" % k]
        dgm, dgk = dg(f)
        msgs = []

        def lim(c, t):
            if first and t == f:
                return T.TN[:, 64 * c:64 * c + 64], "TN%d" % c
            return T.TT[:, 320 * c + 64 * t:320 * c + 64 * t + 64], "TT%d_%d" % (c, t)

        for c in range(NC):
            dk = DB[c]
            if not first:
                for lo, hi in ([(0, CUT), (CUT, f + 1)] if c in SPLIT else [(0, f + 1)]):
                    gather(T.TT, "TT", c, lo, hi, f, c in GATHER_A)
                    limit(T.TT[:, 320 * c + 64 * lo:320 * c + 64 * hi], ["TT%d_%d" % (c, s) for s in range(lo, hi)])
            how, d = FLOOR[k][c], T[dk]
            top = ns if how == "P" else f + 1
            for t in range(top):
                v, vk = lim(c, t)
                for s in range(t, top):
                    m, mk = wd(s, t)
                    mm(dreg(c, f, s), m, v, False, how in "AV" and t == f, [mk, vk], [dk])
                if t and how in "PH":
                    mm(dreg(c, f, t), I1, MP, False, t == f and how == "H", ["I1", "MP"], [dk])
                if t and how == "P":
                    mm(dreg(c, f, t), I1, MN, False, t == f, ["I1", "MN"], [dk])
            src, r, x = d[:, 0:nn], [], [dk]
            if KEEP:
                if how != "P":
                    src, r, x = T.X[:, 320 * c:320 * c + nn], ["X%d" % c], []
                    if how == "A":
                        act(d[:, 0:nn], d[:, 0:nn], bias=MAG, w=["XM%d" % c], x=[dk])
                    if how == "V":
                        ts(src, d[:, 0:nn], MAG, A.add, -MAG, A.add, w=r, x=[dk])
                    else:
                        act(src, d[:, 0:nn], bias=-MAG, r=["XM%d" % c], w=r, x=[dk])
            elif how == "P":
                cell, cs = dreg(c, f, f - 1), cplace(f, f, c, c + 1)
                mm(cell, dgm, T.CH[:, cs], False, False, [dgk, "CH" + ckey(f, f)], [dk])
                mm(cell, dgm, T.CL[:, cs], False, False, [dgk, "CL" + ckey(f, f)], [dk])
                for t in range(f + 1):
                    v, vk = lim(c, t)
                    m, mk = wx(f, t)
                    mm(cell, m, v, False, False, [mk, vk], [dk])
                mm(cell, dgm, MP, False, False, [dgk, "MP"], [dk])
                mm(cell, dgm, MN, False, True, [dgk, "MN"], [dk])
            else:
                src, r, x = T.X[:, 256 * c:256 * c + nn], ["X%d" % c], []
                if how == "A":
                    act(d[:, 0:nn + 64], d[:, 0:nn + 64], bias=MAG, w=["XM%d" % c], x=[dk])
                act(src, d[:, 0:nn], bias=-MAG, r=["XM%d" % c], w=r, x=[dk])
                act(d[:, 320:384], dreg(c, f, f), scale=T.wc[:, 3 + f:4 + f], bias=T.wc[:, 21 + f:22 + f], r=["wa", "wm", "XM%d" % c], x=[dk])
                xs = T.X[:, 256 * c:256 * c + nn:f]
                tt(xs, d[:, 320:384], xs, A.add, r, r, [dk])
            add("v", lambda c=c, src=src: g.vector.tensor_tensor_scan(dl[:, nn * c:nn * (c + 1)], T["PAT%d" % f][:, 0:nn], src, 1536.0, A.mult, A.add),
                r + ["PAT%d_%d" % (f, j) for j in range(ns)], ["dl%d_%d" % (k, c)], x, cost=0.05 + nn * CYC)
            msgs.append(send(ld[:, nn * c:nn * (c + 1)], dl[:, nn * c:nn * (c + 1)], ["dl%d_%d" % (k, c)], 2 * nn))
        after = GATHER_AF if k == 5 else GATHER_A0 if k == 2 else GATHER_A
        for c in range(NC):
            dk, o, dn = DB[c], dreg(c, f, f), T.dn[:, 64 * c:64 * c + 64]
            if KEEP:
                pass
            elif FLOOR[k][c] == "P":
                cs = cplace(f, f, c, c + 1)
                mm(o, I1, T.CH[:, cs], True, False, ["I1", "CH" + ckey(f, f)], [dk])
                mm(o, I1, T.CL[:, cs], False, False, ["I1", "CL" + ckey(f, f)], [dk])
                for t in range(f + 1):
                    v, vk = lim(c, t)
                    m, mk = wd(f, t)
                    mm(o, m, v, False, t == f, [mk, vk], [dk])
                ts(dn, o, 1.0 / 32, A.add, w=["dn%d" % c], x=[dk])
            else:
                ts(dn, o, -MAG, A.add, 1.0 / 32, A.add, w=["dn%d" % c], x=[dk])
            for s in range(ns):
                mm(hreg(c, s), I1, dl[:, nn * c + ns - 1 - s:nn * (c + 1):ns], s == 0, s == f, ["I1", "dl%d_%d" % (k, c)], [HB[c]])
            if not KEEP:
                mm(hreg(c, f), I1, dn, False, True, ["I1", "dn%d" % c], [HB[c]])
            wh, hk, h = wcols(HOME, c, 0, f + 1), [HK[c], "WN%d_%d" % (f, c)], hreg(c, 0, f + 1)
            if c in after:
                tt(h, h, wh, A.add, hk, [], [HB[c]])
                act(wh, h, w=hk[:1], x=[HB[c]])
            else:
                rh = T.RH[:, 320 * c:320 * c + 64 * f + 64]
                tt(rh, h, wh, A.add, hk, ["RH%d" % c], [HB[c]])
                act(wh, rh, r=["RH%d" % c], w=hk[:1])
        if k == 2:
            late = send(W[:, AWAY + 768:WEND], W[:, HOME + 768:HOME + 1024], HK, 1024, True)
        idle()
        if not last:
            for c in range(NC - 1):
                preload(c, k + 1)
        for c in range(NC):
            arrive(msgs[c], ["ld%d_%d" % (k, c)])
            for s in range(f):
                mm(T.dx[:, 64 * s:64 * s + 64], I1, ld[:, nn * c + ns - 1 - s:nn * (c + 1):ns], s == 0, s == f - 1, ["I1", "ld%d_%d" % (k, c)], ["dx"])
            wa = wcols(AWAY, c, 0, f)
            tt(wa, wa, T.dx[:, 0:64 * f], A.add, [AK[c], "WI0_", "WI1_", "WI2_"] + (["WL"] if f == 4 else []), [AK[c]], ["dx"])
        marks.append(len(ops) - 1)
        if k == 2:
            arrive(late, ["WL"])
        if not last:
            preload(NC - 1, k + 1)

    def stakes(cs):
        for c in cs:
            for s in range(5):
                act(T.stc[:, 320 * c + 64 * s:320 * c + 64 * s + 64], T.stb[:, 256 * s + 64 * c:256 * s + 64 * c + 64],
                    r=["stb", HK[3]], w=["stc%d_%d" % (c, s)])

    z3, z3k = part1(3)

    def idle0():
        node_numbers(3, z3, z3k)
        ts(si(5, 16), z3, -float(HOME), A.add, r=z3k, w=["sa5"])
        act(T.aw[:, 0:16], z3, F.Sigmoid, bias=-2.0 * AWAY, scale=2.0, r=z3k + [HK[3]], w=["aw"], more=1.3)
        lookup_list(si(20, 16), "sa20", si(5, 16), "sa5", 16, 48, T.aw[:, 0:16], "aw")
        weights(4)
        const(4, 3, "d1")
        for s in range(3):
            const_again(s)

    def idle1():
        lookup_gather(16, 48, "d2")
        lookup_finish(16, 48, "d2")
        player_columns(16, 48)
        act(T.ZB[:, :], T.ZZ[:, 0:48], bias=HOME + 768.0, r=["ZZ0"], w=["ZB"])
        for h, cs in enumerate(PARTS[4]):
            j0, m = 4 * cs[0], 4 * len(cs)
            for k in range(3):
                tt(T.DZ[:, 3 * j0 + m * k:3 * j0 + m * (k + 1)], T.ZZ[:, 48 + j0:48 + j0 + m], T.ZZ[:, 16 * k + j0:16 * k + j0 + m], A.subtract,
                   ["ZZ0", "ZZ48"], ["DZ_%d" % h])
        const(4, 4, "d1")
        act(T.I32[:, :], I1, r=["I1"], w=["I32"])
        for i, (m, k) in enumerate(NEXT):
            mm(T.d1[:, 0:128], I1, m, i == 0, i == 2, ["I1", k], ["d1"])
        act(T.NM[:, :], T.d1[:, 0:128], w=["NM"], x=["d1"])

    def idle2():
        newest(4)
        for c in range(NC):
            mm(T.d2[:, 64 * c:64 * c + 64], T.NM[:, :], wcols(HOME, c, 3, 4), c == 0, c == NC - 1, ["NM", HK[c]], ["d2"], k=4.0)
        half_sum("d2", 4)
        pattern(4)

    sweep(0, idle0)
    sweep(1, idle1)
    sweep(2, idle2)
    z4, z4k = part1(4)

    def idle3():
        node_numbers(4, z4, z4k)
        dma("s", T.yo[:, :], T.YO[:, :], r=["YO3", "YO4"])
        stakes([0, 1])

    def idle4():
        stakes([2, 3])

    def idle5():
        for c in range(NC):
            for s in range(5):
                o = T.YR[:, 256 * s + 64 * c:256 * s + 64 * c + 64]
                i, r = wcols(HOME, c, s, s + 1), [HK[c]]
                if c < 2:
                    ts(o, i, -9216.0, A.add, r=r, w=["YR%d%d" % (c, s)])
                else:
                    act(o, i, bias=-9216.0, r=r, w=["YR%d%d" % (c, s)])
        dma("s", T.yr[:, :], T.YR[:, :], r=["YR%d%d" % (c, s) for c in range(NC) for s in range(5)], lat=3.6)

    sweep(3, idle3)
    sweep(4, idle4)
    sweep(5, idle5)

    for c in range(NC):
        b, dk = 320 * c, DB[(c + 1) % NC]
        d = T[dk]
        sk = ["stc%d_%d" % (c, s) for s in range(5)]
        if c in SUM_S:
            e, ek = T[HB[0]], HB[0]
            for lo, hi, p, pk in ((0, 3, d, dk), (3, 5, e, ek)):
                cols, key = slice(b + 64 * lo, b + 64 * hi), "PR%d_%d" % (c, lo)
                gather(T.TK, "TF", c, lo, hi, 4, c in GATHER_AF)
                act(p[:, 0:64 * (hi - lo)], T.TK[:, cols], F.Sigmoid, scale=-1.0 / 256, r=["TF%d_%d" % (c, s) for s in range(lo, hi)], x=[pk])
                tt(T.DS[:, cols], p[:, 0:64 * (hi - lo)], T.stc[:, cols], A.mult, sk, [key], [pk])
            for s in range(3):
                mm(d[:, 320:384], T.I32[:, :], T.DS[:, b + 64 * s:b + 64 * s + 64], s == 0, s == 2, ["I32", "PR%d_0" % c], [dk], k=4.0)
            tt(d[:, 384:448], d[:, 320:384], T.DS[:, b + 192:b + 256], A.add, ["PR%d_3" % c], ["PT%d" % c], [dk])
            tt(T.Y[:, 64 * c:64 * c + 64], d[:, 384:448], T.DS[:, b + 256:b + 320], A.add, ["PR%d_3" % c, "PT%d" % c], ["Y%d" % c], [dk])
        else:
            gather(T.TK, "TF", c, 0, 5, 4, c in GATHER_AF)
            act(d[:, 0:320], T.TK[:, b:b + 320], F.Sigmoid, scale=-1.0 / 256, r=["TF%d_%d" % (c, s) for s in range(5)], x=[dk])
        if c in SUM_S:
            pass
        elif c in SUM_V:
            tt(T.DS[:, b:b + 192], d[:, 0:192], T.stc[:, b:b + 192], A.mult, sk, ["PR%d" % c], [dk])
            tt(d[:, 192:320], d[:, 192:320], T.stc[:, b + 192:b + 320], A.mult, sk, ["PS%d" % c], [dk])
            tt(d[:, 320:448], d[:, 192:320], T.DS[:, b:b + 128], A.add, ["PR%d" % c, "PS%d" % c], ["PT%d" % c], [dk])
            tt(T.DS[:, b + 192:b + 256], d[:, 320:384], T.DS[:, b + 128:b + 192], A.add, ["PR%d" % c, "PT%d" % c], ["PU%d" % c], [dk])
            tt(T.Y[:, 64 * c:64 * c + 64], d[:, 384:448], T.DS[:, b + 192:b + 256], A.add, ["PU%d" % c], ["Y%d" % c], [dk])
        else:
            tt(T.DS[:, b:b + 320], d[:, 0:320], T.stc[:, b:b + 320], A.mult, sk, ["PR%d" % c], [dk])
            for s in range(5):
                mm(d[:, 320:384], T.I32[:, :], T.DS[:, b + 64 * s:b + 64 * s + 64], s == 0, s == 4, ["I32", "PR%d" % c], [dk], k=4.0)
            act(T.Y[:, 64 * c:64 * c + 64], d[:, 320:384], w=["Y%d" % c], x=[dk])
        if c % 2 == 1:
            dma("s", T.y[:, 64 * c - 64:64 * c + 64], T.Y[:, 64 * c - 64:64 * c + 64], r=["Y%d" % (c - 1), "Y%d" % c])

    if "order" not in KEPT:
        KEPT["order"] = _order(ops, marks)
    order = KEPT["order"]
    place = {i: p for p, i in enumerate(order)}

    queue = {"v": g.vector, "a": g.scalar, "p": g.tensor, "g": g, "s": g.sync}
    semof = {"v": "sv", "a": "sa", "p": "sp", "g": "sg"}
    needed = set()
    for o in ops:
        newest_of, keep = {}, []
        for j in o["hard"]:
            qj = ops[j]["q"]
            if ops[j]["tok"] is not None:
                keep.append(j)
            elif not (qj == "p" and o["q"] == "p") and place[j] > place.get(newest_of.get(qj), -1):
                newest_of[qj] = j
        o["wait"] = keep + list(newest_of.values())
        needed.update(o["wait"])
    cnt, known, clock, top = {}, {q: {} for q in queue}, {}, {}
    for i in order:
        o = ops[i]
        q = o["q"]
        if q == "r":
            clock[i] = {o["tok"][0]: o["tok"][1]}
            top[o["tok"][0]] = o["tok"][1]
            o["own"] = o["tok"][:2]
            continue
        kn = known[q]
        for j in sorted(o["wait"], key=lambda j: -place[j]):
            own = ops[j]["own"]
            if own is not None and kn.get(own[0], 0) < own[1]:
                queue[q].wait_ge(T.sem[own[0]], own[1])
            for s, v in clock[j].items():
                if kn.get(s, 0) < v:
                    kn[s] = v
        ck = dict(kn)
        o["own"] = None
        ins = o["fn"]()
        if o["tok"] is not None:
            if o["tok"][2]:
                ins.then_inc(T.sem[o["tok"][0]], 16)
            if o["tok"][1]:
                o["own"] = o["tok"][:2]
        elif q != "p" or i in needed:
            s = semof[q]
            cnt[s] = cnt.get(s, 0) + 1
            ins.then_inc(T.sem[s], 1)
            o["own"] = (s, cnt[s])
        if o["own"] is not None:
            ck[o["own"][0]] = o["own"][1]
            top[o["own"][0]] = o["own"][1]
        clock[i] = ck
    top["ls"] = nsent[0]
    for s, v in top.items():
        if known["g"].get(s, 0) < v:
            g.wait_ge(T.sem[s], v)
